import numpy as np
import ml_dtypes


def mxq(x, axis, fmt="e4m3"):
    dtype, down = {"e4m3": (ml_dtypes.float8_e4m3fn, 7), "e5m2": (ml_dtypes.float8_e5m2, 14)}[fmt]
    v = np.moveaxis(np.asarray(x, np.float32).astype(ml_dtypes.bfloat16).astype(np.float64), axis, -1)
    blocks = v.reshape(v.shape[:-1] + (-1, 32))
    amax = np.abs(blocks).max(-1, keepdims=True)
    byte = np.maximum(np.where(amax > 0, np.frexp(amax)[1] - 1 + 127, 0) - down, 1)
    scale = np.exp2(byte - 127.0)
    codes = (blocks / scale).astype(np.float32).astype(dtype).astype(np.float64)
    return np.moveaxis((codes * scale).reshape(v.shape), -1, axis)


WIDE = False


def mx_kscale(k):
    if not WIDE:
        return np.ones(k)
    levels = np.array([10, -10, 5, -5, 0])
    if k % 512:
        return np.exp2(np.random.permutation(np.resize(levels, k // 32))).repeat(32)
    a = np.empty((k // 512, 16))
    for p in range(k // 512):
        a[p, :8] = np.random.permutation(np.resize(levels, 8))
        for g in range(8):
            far = levels[np.abs(levels - a[p, g]) >= 10]
            a[p, g + 8] = far[np.random.randint(len(far))]
    return np.exp2(a.ravel()).repeat(32)


def f64(x):
    return np.asarray(x).astype(np.float64)


def striped(idx):
    return np.tile(idx.reshape(-1, 16).T, (8, 1)).astype(np.uint16)


def unstriped(offs):
    return offs[:16].T.reshape(-1).astype(np.int64)


E2M1 = np.array([0.0, 0.5, 1.0, 1.5, 2.0, 3.0, 4.0, 6.0, -0.0, -0.5, -1.0, -1.5, -2.0, -3.0, -4.0, -6.0])


def pack_weight(w, fmt):
    k, n = w.shape
    w = f64(np.asarray(w, np.float32).astype(ml_dtypes.bfloat16)).reshape(k // 32, 32, n)
    amax = np.abs(w).max(1)
    if fmt == "e4m3":
        byte = np.frexp(amax)[1] - 1 + 127 - 7
    else:
        mant, ex = np.frexp(amax / 6.0)
        byte = np.where(mant > 0.5, ex, ex - 1) + 127
    byte = np.clip(np.where(amax > 0, byte, 1), 1, 254)
    scaled = (w * np.exp2(127.0 - byte)[:, None, :]).reshape(k, n).astype(np.float32)
    by_word = np.ascontiguousarray(scaled.reshape(k // 512, 128, 4, n).transpose(0, 1, 3, 2))
    if fmt == "e4m3":
        words = by_word.astype(ml_dtypes.float8_e4m3fn).view(np.uint8)
    else:
        c = by_word.astype(ml_dtypes.float4_e2m1fn).view(np.uint8) & 0xF
        words = (c[..., 0::2] | (c[..., 1::2] << 4)).reshape(k // 512, 128, 2 * n)
    return np.ascontiguousarray(words), np.ascontiguousarray(byte.astype(np.uint8).reshape(k // 512, 16, n))


def unpack_weight(words, scales, fmt):
    g, _, n = scales.shape
    words = np.ascontiguousarray(words).reshape(g, 128, n, -1)
    if fmt == "e4m3":
        vals = words.view(ml_dtypes.float8_e4m3fn).astype(np.float64)
    else:
        nib = np.empty((g, 128, n, 4), np.uint8)
        nib[..., 0::2] = words & 0xF
        nib[..., 1::2] = words >> 4
        vals = E2M1[nib]
    vals = vals * np.repeat(np.exp2(scales.astype(np.float64) - 127.0), 8, axis=1)[..., None]
    return vals.transpose(0, 1, 3, 2).reshape(g * 512, n)


def gelu(v):
    return 0.5 * v * (1.0 + np.tanh(np.sqrt(2.0 / np.pi) * (v + 0.044715 * v**3)))


K, H, N, T, S, T2, P = 512, 1024, 512, 4096, 1024, 2048, 1024

def setup_inputs():
    n = np.random.standard_normal
    s = mx_kscale(K)[:, None]
    u = mx_kscale(H)[:, None]
    tab_words, tab_scales = pack_weight(n((K, T)) * s, "e4m3")
    w2_words, w2_scales = pack_weight(n((K, H)) / np.sqrt(K) / s, "e2m1")
    w3_words, w3_scales = pack_weight(n((H, N)) / np.sqrt(H) / u, "e4m3")
    lam = np.random.uniform(0.3, 0.8, N)
    return {
        "tab_words": tab_words, "tab_scales": tab_scales,
        "offs": striped(np.random.permutation(T)[:S]),
        "offs2": striped(np.random.permutation(T2)[:S]),
        "offs3": striped(np.random.permutation(T2)[:P]),
        "offs4": striped(np.random.permutation(T2)[:P]),
        "w1": (n((K, H)) / np.sqrt(K) / s * u.T).astype(np.float32),
        "w2_words": w2_words, "w2_scales": w2_scales,
        "wgs": np.exp(0.3 * n((128, S))).astype(np.float32),
        "hist": (n((H, T2)) * u).astype(np.float32),
        "w3_words": w3_words, "w3_scales": w3_scales,
        "lam": lam.astype(np.float32),
        "snap": (n((N, P)) * (1.0 - lam[:, None])).astype(np.float32),
        "wgo": np.exp(0.3 * n((128, P))).astype(np.float32),
    }

def reference(tab_words, tab_scales, offs, offs2, offs3, offs4, w1, w2_words, w2_scales,
              wgs, hist, w3_words, w3_scales, lam, snap, wgo):
    v = unpack_weight(tab_words, tab_scales, "e4m3")[:, unstriped(offs)]
    a = mxq(f64(w1), 0, "e4m3").T @ v
    b = unpack_weight(w2_words, w2_scales, "e2m1").T @ v
    h = a / (0.5 + np.abs(b))
    page = np.zeros((H, T2))
    page[:, unstriped(offs2)] = np.tile(f64(wgs), (H // 128, 1)) * h
    z = page + f64(hist)
    y = unpack_weight(w3_words, w3_scales, "e4m3").T @ mxq(z, 0, "e4m3")
    x = y[:, unstriped(offs3)]
    x = f64(lam)[:, None] * x + f64(snap)
    out = np.zeros((N, T2))
    out[:, unstriped(offs4)] = np.tile(f64(wgo), (N // 128, 1)) * x
    return out

@@ -1,0 +1,295 @@
+from contextlib import ExitStack
+
+import concourse.mybir as mybir
+from concourse.masks import make_identity
+
+K, H, N, T, S, T2, M = 512, 1024, 512, 4096, 1024, 2048, 1024
+FLOPS = 2 * (2 * K * H * S + H * N * T2)
+
+F32 = mybir.dt.float32
+BF16 = mybir.dt.bfloat16
+I32 = mybir.dt.int32
+U32 = mybir.dt.uint32
+U16 = mybir.dt.uint16
+U8 = mybir.dt.uint8
+FP8X4 = mybir.dt.float8_e4m3fn_x4
+FP4X4 = mybir.dt.float4_e2m1fn_x4
+ACT = mybir.ActivationFunctionType
+ALU = mybir.AluOpType
+
+P = 128
+BANK = 512
+PAGES = H // P
+PASSES = H // 512
+GROUPS = T2 // BANK
+W1_CHUNK = 256
+
+
+def tile_list_lag_rewind_features_kernel(
+    tc, tab_words, tab_scales, offs, offs2, offs3, offs4, w1, w2_words, w2_scales,
+    wgs, hist, w3_words, w3_scales, lam, snap, wgo, out,
+):
+    nc = tc.nc
+    with ExitStack() as ctx:
+        keep = ctx.enter_context(tc.tile_pool(name="keep", bufs=1))
+        shared = ctx.enter_context(tc.tile_pool(name="shared", bufs=1))
+        ring = ctx.enter_context(tc.tile_pool(name="ring", bufs=2))
+        ring3 = ctx.enter_context(tc.tile_pool(name="ring3", bufs=3))
+        ring4 = ctx.enter_context(tc.tile_pool(name="ring4", bufs=4))
+        psum = ctx.enter_context(tc.psum_pool(name="psum", bufs=1))
+
+        banks = [psum.tile([P, BANK], F32, name=f"bank{i}") for i in range(8)]
+        a_banks, b_banks, z_banks, w_banks = banks[0:2], banks[2:4], banks[4:6], banks[6:8]
+
+        def load_scale_rows(queue, plane, rows):
+            for q in range(4):
+                queue.dma_start(out=plane[32 * q : 32 * q + 4].bitcast(I32), in_=rows(q).bitcast(I32))
+
+        tab_sc = keep.tile([P, T], U8, name="tab_sc", align_bytes=64)
+        nc.vector.memset(tab_sc[:].bitcast(I32), 0)
+        w2_sc = keep.tile([P, H], U8, name="w2_sc", align_bytes=64)
+        nc.gpsimd.memset(w2_sc[:].bitcast(I32), 0)
+
+        def load_list(name, source):
+            t = keep.tile([P, S // 16], U16, name=name)
+            nc.sync.dma_start(t[:], source)
+            return t
+
+        w1_rows = w1.rearrange("(p j) c -> p j c", j=4)
+        w1_raw = []
+
+        def load_w1(k):
+            raw = ring4.tile([P, 4, W1_CHUNK], F32, name="w1_raw", tag="quarter")
+            nc.sync.dma_start(out=raw[:], in_=w1_rows[:, :, k * W1_CHUNK : (k + 1) * W1_CHUNK])
+            w1_raw.append(raw)
+
+        idx = load_list("idx", offs)
+        tab_w = shared.tile([P, T], I32, name="tab_w", offset=0)
+        tab_rows = tab_words[0].rearrange("p t i -> p (t i)").bitcast(I32)
+        nc.sync.dma_start(out=tab_w[:, : T // 2], in_=tab_rows[:, : T // 2])
+        load_scale_rows(nc.sync, tab_sc, lambda q: tab_scales[0, 4 * q : 4 * q + 4, :])
+        nc.sync.dma_start(out=tab_w[:, T // 2 :], in_=tab_rows[:, T // 2 :])
+        w2_w = keep.tile([P, 2 * H], U8, name="w2_w", align_bytes=64)
+        nc.sync.dma_start(out=w2_w[:].bitcast(I32), in_=w2_words[0].bitcast(I32))
+        load_scale_rows(nc.sync, w2_sc, lambda q: w2_scales[0, 4 * q : 4 * q + 4, :])
+        load_w1(0)
+        wgs_sb = keep.tile([P, S], F32, name="wgs_sb")
+        nc.sync.dma_start(out=wgs_sb[:], in_=wgs)
+        idx2 = load_list("idx2", offs2)
+
+        half = keep.tile([P, 1], F32, name="half")
+        nc.gpsimd.memset(half[:], 0.5)
+        warm = keep.tile([P, 1], F32, name="warm")
+        nc.scalar.activation(warm[:], half[:], ACT.Abs_reciprocal_sqrt)
+        ident = keep.tile([P, P], F32, name="ident")
+        make_identity(nc, ident[:])
+
+        pages = [keep.tile([P, T2], F32, name=f"page{i}") for i in range(2)]
+        for t in pages:
+            nc.gpsimd.memset(t[:], 0.0)
+        w3_sc = keep.tile([P, PASSES, N], U8, name="w3_sc", align_bytes=64)
+        nc.gpsimd.memset(w3_sc[:].rearrange("p a n -> p (a n)").bitcast(I32), 0)
+
+        hist_sb = []
+
+        def load_hist(c):
+            t = ring4.tile([P, T2], F32, name="hist_sb", tag="rows")
+            nc.sync.dma_start(out=t[:], in_=hist[c * P : (c + 1) * P, :])
+            hist_sb.append(t)
+
+        load_w1(1)
+        load_hist(0)
+        load_w1(2)
+        load_w1(3)
+        load_hist(1)
+
+        v_sc = keep.tile([P, S], U8, name="v_sc", align_bytes=64)
+        nc.vector.tensor_copy(v_sc[:], tab_sc[:].indirect(idx[:]))
+        v_w = keep.tile([P, S], U32, name="v_w", align_bytes=64)
+        for hf in range(2):
+            nc.vector.tensor_copy(
+                v_w[:, hf * BANK : (hf + 1) * BANK],
+                tab_w[:].bitcast(U32).indirect(idx[:, hf * 32 : (hf + 1) * 32]),
+            )
+
+        slots = [shared.tile([P, T2], F32, name=f"slots{i}", offset=i * 4 * T2) for i in range(2)]
+        for t in slots:
+            nc.gpsimd.memset(t[:], 0.0)
+
+        w1_w = keep.tile([P, H], U32, name="w1_w", align_bytes=64)
+        w1_sc = keep.tile([P, H], U8, name="w1_sc", align_bytes=64)
+
+        def quantize_w1(k):
+            cols = slice(k * W1_CHUNK, (k + 1) * W1_CHUNK)
+            grouped = ring.tile([P, W1_CHUNK, 4], BF16, name="w1_grouped", align_bytes=64)
+            nc.scalar.copy(out=grouped[:], in_=w1_raw[k][:].rearrange("p j c -> p c j"))
+            nc.vector.quantize_mx(
+                out=w1_w[:, cols].bitcast(FP8X4), scales=w1_sc[:, cols],
+                in_=grouped[:].rearrange("p c j -> p (c j)"),
+            )
+
+        damp = {}
+
+        def damping(c):
+            r = ring.tile([P, S], F32, name="damp")
+            damp[c] = r
+            hs = [slice(hf * BANK, (hf + 1) * BANK) for hf in range(2)]
+            for hf in range(2):
+                nc.tensor.matmul_mx(
+                    out=b_banks[hf][:],
+                    lhsT=w2_w[:, 2 * c * P : 2 * (c + 1) * P].bitcast(FP4X4),
+                    lhsT_scale=w2_sc[:, c * P : (c + 1) * P],
+                    rhs=v_w[:, hs[hf]].bitcast(FP8X4), rhs_scale=v_sc[:, hs[hf]],
+                    start=True, stop=True,
+                )
+            for hf in range(2):
+                nc.scalar.activation(r[:, hs[hf]], b_banks[hf][:], ACT.Abs)
+            for hf in range(2):
+                nc.scalar.activation(r[:, hs[hf]], r[:, hs[hf]], ACT.Abs_reciprocal_sqrt, bias=half[:])
+            for hf in range(2):
+                nc.scalar.activation(r[:, hs[hf]], r[:, hs[hf]], ACT.Square)
+
+        def fill_page(c):
+            h = ring.tile([P, S], F32, name="h", tag="listed")
+            for hf in range(2):
+                cols = slice(hf * BANK, (hf + 1) * BANK)
+                nc.tensor.matmul_mx(
+                    out=a_banks[hf][:],
+                    lhsT=w1_w[:, c * P : (c + 1) * P].bitcast(FP8X4),
+                    lhsT_scale=w1_sc[:, c * P : (c + 1) * P],
+                    rhs=v_w[:, cols].bitcast(FP8X4), rhs_scale=v_sc[:, cols],
+                    start=True, stop=True,
+                )
+                nc.vector.tensor_tensor(h[:, cols], a_banks[hf][:], damp[c][:, cols], ALU.mult)
+                if c == 0:
+                    nc.vector.tensor_tensor(
+                        pages[0][:].indirect(idx2[:, hf * 32 : (hf + 1) * 32]), h[:, cols], wgs_sb[:, cols], ALU.mult
+                    )
+            if c > 0:
+                nc.vector.tensor_tensor(pages[c % 2][:].indirect(idx2[:]), h[:], wgs_sb[:], ALU.mult)
+
+        zt = [[keep.tile([P, 4, 2, P, 2], BF16, name=f"zt{a}_{g}") for g in range(GROUPS)] for a in range(PASSES)]
+
+        def add_history(c):
+            a, cc = divmod(c, 4)
+            last = c == PAGES - 1
+            for g in range(GROUPS):
+                bank = (z_banks + b_banks)[g] if last else z_banks[g % 2]
+                for n, rows in enumerate((hist_sb[c], pages[c % 2])):
+                    for k in range(4):
+                        t0 = (4 * g + k) * P
+                        nc.tensor.matmul(
+                            bank[:, k * P : (k + 1) * P], lhsT=rows[:, t0 : t0 + P], rhs=ident[:],
+                            is_transpose=True, start=(n == 0 and k == 0), stop=(n == 1 and k == 3),
+                        )
+                dst = zt[a][g][:, :, :, 32 * cc : 32 * cc + 32, :]
+                src = bank[:].rearrange("p (k i u e) -> p k u i e", k=4, u=2, e=2)
+                if last and g % 2 == 1:
+                    nc.vector.tensor_copy(out=dst, in_=src)
+                else:
+                    nc.scalar.copy(out=dst, in_=src)
+
+        z_w = [keep.tile([P, T2], U32, name=f"z_w{a}", align_bytes=64) for a in range(PASSES)]
+        z_sc = [keep.tile([P, T2], U8, name=f"z_sc{a}", align_bytes=64) for a in range(PASSES)]
+
+        def quantize_z(a, g, turn_banks, share):
+            words = zt[a][g][:].rearrange("p k u r e -> p (k u r e)").bitcast(F32)
+            grouped = ring3.tile([P, BANK, 2], F32, name="z_grouped", align_bytes=64)
+            for j in range(2):
+                bank = turn_banks[j]
+                for u in range(2):
+                    for kk in range(2):
+                        w0 = ((2 * j + kk) * 2 + u) * P
+                        o0 = (u * 2 + kk) * P
+                        nc.tensor.transpose(bank[:, o0 : o0 + P], words[:, w0 : w0 + P], ident[:])
+                dst = grouped[:, j * 256 : (j + 1) * 256, :]
+                src = bank[:].rearrange("p (u n) -> p n u", u=2)
+                if share and j == 1:
+                    nc.vector.tensor_copy(out=dst, in_=src)
+                else:
+                    nc.scalar.copy(out=dst, in_=src)
+            cols = slice(g * BANK, (g + 1) * BANK)
+            nc.vector.quantize_mx(
+                out=z_w[a][:, cols].bitcast(FP8X4), scales=z_sc[a][:, cols],
+                in_=grouped[:].rearrange("p n u -> p (n u)").bitcast(BF16),
+            )
+
+        w3_w = keep.tile([P, PASSES, N], I32, name="w3_w", align_bytes=64)
+        wgo_sb = keep.tile([P, M], F32, name="wgo_sb")
+        lam_sb = keep.tile([P, N // P], F32, name="lam_sb")
+        snap_sb = []
+        late_lists = []
+
+        def load_second_stage():
+            nc.sync.dma_start(out=w3_w[:], in_=w3_words.rearrange("a p c i -> p a (c i)").bitcast(I32))
+            load_scale_rows(nc.sync, w3_sc, lambda q: w3_scales[:, 4 * q : 4 * q + 4, :].rearrange("a q n -> q a n"))
+            nc.sync.dma_start(out=wgo_sb[:], in_=wgo)
+            late_lists.extend([load_list("idx3", offs3), load_list("idx4", offs4)])
+            with nc.allow_non_contiguous_dma(reason="one value of lam for each partition"):
+                nc.sync.dma_start(out=lam_sb[:], in_=lam.rearrange("(i p) -> p i", p=P))
+            for i in range(N // P):
+                t = ring4.tile([P, M], F32, name="snap_sb", tag="quarter")
+                nc.sync.dma_start(out=t[:], in_=snap[i * P : (i + 1) * P, :])
+                snap_sb.append(t)
+
+        quantize_w1(0)
+        damping(0)
+        for c in range(PAGES):
+            if c + 2 < PAGES:
+                load_hist(c + 2)
+            if c == 2:
+                load_second_stage()
+            if c + 1 < PAGES:
+                damping(c + 1)
+            fill_page(c)
+            if c < 3:
+                quantize_w1(c + 1)
+            if c >= 1:
+                add_history(c - 1)
+            if c >= 4:
+                quantize_z(0, c - 4, w_banks, False)
+        add_history(PAGES - 1)
+
+        def product_pass(i, g, a, bank):
+            cols = slice(g * BANK, (g + 1) * BANK)
+            nc.tensor.matmul_mx(
+                out=bank[:],
+                lhsT=w3_w[:, a, i * P : (i + 1) * P].bitcast(FP8X4),
+                lhsT_scale=w3_sc[:, a, i * P : (i + 1) * P],
+                rhs=z_w[a][:, cols].bitcast(FP8X4), rhs_scale=z_sc[a][:, cols],
+                start=(a == 0), stop=(a == PASSES - 1),
+            )
+
+        y_banks = [a_banks + z_banks, b_banks + w_banks]
+        turn = [w_banks, z_banks, w_banks, b_banks]
+        y_sb = [ring4.tile([P, T2], F32, name="y_sb", tag="rows") for i in range(N // P)]
+
+        def leave_bank(i, g):
+            cols = slice(g * BANK, (g + 1) * BANK)
+            nc.scalar.activation(y_sb[i][:, cols], y_banks[i % 2][g][:], ACT.Copy, scale=lam_sb[:, i : i + 1])
+
+        for g in range(2):
+            product_pass(0, g, 0, y_banks[0][g])
+        for g in range(GROUPS):
+            quantize_z(1, g, turn[g], True)
+        for g in range(GROUPS):
+            if g >= 2:
+                product_pass(0, g, 0, y_banks[0][g])
+            product_pass(0, g, 1, y_banks[0][g])
+            leave_bank(0, g)
+
+        idx3, idx4 = late_lists
+
+        def pick(i):
+            x = ring.tile([P, M], F32, name="x", tag="listed")
+            nc.vector.tensor_tensor(x[:], y_sb[i][:].indirect(idx3[:]), snap_sb[i][:], ALU.add)
+            nc.vector.tensor_tensor(slots[i % 2][:].indirect(idx4[:]), x[:], wgo_sb[:], ALU.mult)
+            nc.sync.dma_start(out=out[i * P : (i + 1) * P, :], in_=slots[i % 2][:])
+
+        for i in range(N // P):
+            if i + 1 < N // P:
+                for g in range(GROUPS):
+                    for a in range(PASSES):
+                        product_pass(i + 1, g, a, y_banks[(i + 1) % 2][g])
+                    leave_bank(i + 1, g)
+            pick(i)

@@ -39,7 +39,7 @@ def tile_list_lag_rewind_features_kernel(
         psum = ctx.enter_context(tc.psum_pool(name="psum", bufs=1))
 
         banks = [psum.tile([P, BANK], F32, name=f"bank{i}") for i in range(8)]
-        a_banks, b_banks, z_banks, w_banks = banks[0:2], banks[2:4], banks[4:6], banks[6:8]
+        pairs, b_banks, w_banks = [banks[0:2], banks[2:4]], banks[4:6], banks[6:8]
 
         def load_scale_rows(queue, plane, rows):
             for q in range(4):
@@ -84,7 +84,7 @@ def tile_list_lag_rewind_features_kernel(
         ident = keep.tile([P, P], F32, name="ident")
         make_identity(nc, ident[:])
 
-        pages = [keep.tile([P, T2], F32, name=f"page{i}") for i in range(2)]
+        pages = [keep.tile([P, T2], F32, name=f"page{i}") for i in range(3)]
         for t in pages:
             nc.gpsimd.memset(t[:], 0.0)
         w3_sc = keep.tile([P, PASSES, N], U8, name="w3_sc", align_bytes=64)
@@ -131,7 +131,7 @@ def tile_list_lag_rewind_features_kernel(
         damp = {}
 
         def damping(c):
-            r = ring.tile([P, S], F32, name="damp")
+            r = ring3.tile([P, S], F32, name="damp")
             damp[c] = r
             hs = [slice(hf * BANK, (hf + 1) * BANK) for hf in range(2)]
             for hf in range(2):
@@ -149,39 +149,47 @@ def tile_list_lag_rewind_features_kernel(
             for hf in range(2):
                 nc.scalar.activation(r[:, hs[hf]], r[:, hs[hf]], ACT.Square)
 
-        def fill_page(c):
-            h = ring.tile([P, S], F32, name="h", tag="listed")
+        def motion(c):
             for hf in range(2):
                 cols = slice(hf * BANK, (hf + 1) * BANK)
                 nc.tensor.matmul_mx(
-                    out=a_banks[hf][:],
+                    out=pairs[c % 2][hf][:],
                     lhsT=w1_w[:, c * P : (c + 1) * P].bitcast(FP8X4),
                     lhsT_scale=w1_sc[:, c * P : (c + 1) * P],
                     rhs=v_w[:, cols].bitcast(FP8X4), rhs_scale=v_sc[:, cols],
                     start=True, stop=True,
                 )
-                nc.vector.tensor_tensor(h[:, cols], a_banks[hf][:], damp[c][:, cols], ALU.mult)
+
+        def fill_page(c):
+            h = ring.tile([P, S], F32, name="h", tag="listed")
+            page = pages[c % len(pages)]
+            for hf in range(2):
+                cols = slice(hf * BANK, (hf + 1) * BANK)
+                nc.vector.tensor_tensor(h[:, cols], pairs[c % 2][hf][:], damp[c][:, cols], ALU.mult)
                 if c == 0:
                     nc.vector.tensor_tensor(
-                        pages[0][:].indirect(idx2[:, hf * 32 : (hf + 1) * 32]), h[:, cols], wgs_sb[:, cols], ALU.mult
+                        page[:].indirect(idx2[:, hf * 32 : (hf + 1) * 32]), h[:, cols], wgs_sb[:, cols], ALU.mult
                     )
             if c > 0:
-                nc.vector.tensor_tensor(pages[c % 2][:].indirect(idx2[:]), h[:], wgs_sb[:], ALU.mult)
+                nc.vector.tensor_tensor(page[:].indirect(idx2[:]), h[:], wgs_sb[:], ALU.mult)
 
         zt = [[keep.tile([P, 4, 2, P, 2], BF16, name=f"zt{a}_{g}") for g in range(GROUPS)] for a in range(PASSES)]
 
-        def add_history(c):
+        def add_history(c, groups, parts=(0, 1)):
             a, cc = divmod(c, 4)
             last = c == PAGES - 1
-            for g in range(GROUPS):
-                bank = (z_banks + b_banks)[g] if last else z_banks[g % 2]
-                for n, rows in enumerate((hist_sb[c], pages[c % 2])):
+            for g in groups:
+                bank = (b_banks + pairs[(c + 1) % 2])[g]
+                for n in parts:
+                    rows = (hist_sb[c], pages[c % 3])[n]
                     for k in range(4):
                         t0 = (4 * g + k) * P
                         nc.tensor.matmul(
                             bank[:, k * P : (k + 1) * P], lhsT=rows[:, t0 : t0 + P], rhs=ident[:],
                             is_transpose=True, start=(n == 0 and k == 0), stop=(n == 1 and k == 3),
                         )
+                if 1 not in parts:
+                    continue
                 dst = zt[a][g][:, :, :, 32 * cc : 32 * cc + 32, :]
                 src = bank[:].rearrange("p (k i u e) -> p k u i e", k=4, u=2, e=2)
                 if last and g % 2 == 1:
@@ -234,21 +242,27 @@ def tile_list_lag_rewind_features_kernel(
 
         quantize_w1(0)
         damping(0)
+        motion(0)
+        motion(1)
+        damping(1)
         for c in range(PAGES):
             if c + 2 < PAGES:
                 load_hist(c + 2)
             if c == 2:
                 load_second_stage()
-            if c + 1 < PAGES:
-                damping(c + 1)
             fill_page(c)
             if c < 3:
                 quantize_w1(c + 1)
             if c >= 1:
-                add_history(c - 1)
-            if c >= 4:
-                quantize_z(0, c - 4, w_banks, False)
-        add_history(PAGES - 1)
+                if c + 1 < PAGES:
+                    motion(c + 1)
+                add_history(c - 1, range(GROUPS))
+            if c + 2 < PAGES:
+                damping(c + 2)
+            for g in {4: (0,), 5: (1,), 6: (2,), 7: (3,)}.get(c, ()):
+                quantize_z(0, g, w_banks, False)
+        add_history(PAGES - 1, range(GROUPS), (0,))
+        add_history(PAGES - 1, range(GROUPS), (1,))
 
         def product_pass(i, g, a, bank):
             cols = slice(g * BANK, (g + 1) * BANK)
@@ -260,21 +274,17 @@ def tile_list_lag_rewind_features_kernel(
                 start=(a == 0), stop=(a == PASSES - 1),
             )
 
-        y_banks = [a_banks + z_banks, b_banks + w_banks]
-        turn = [w_banks, z_banks, w_banks, b_banks]
+        y_banks = [w_banks + pairs[1], w_banks + pairs[1]]
         y_sb = [ring4.tile([P, T2], F32, name="y_sb", tag="rows") for i in range(N // P)]
 
         def leave_bank(i, g):
             cols = slice(g * BANK, (g + 1) * BANK)
             nc.scalar.activation(y_sb[i][:, cols], y_banks[i % 2][g][:], ACT.Copy, scale=lam_sb[:, i : i + 1])
 
-        for g in range(2):
+        for g in range(GROUPS):
             product_pass(0, g, 0, y_banks[0][g])
         for g in range(GROUPS):
-            quantize_z(1, g, turn[g], True)
-        for g in range(GROUPS):
-            if g >= 2:
-                product_pass(0, g, 0, y_banks[0][g])
+            quantize_z(1, g, (b_banks, pairs[0])[g % 2], True)
             product_pass(0, g, 1, y_banks[0][g])
             leave_bank(0, g)
 

@@ -18,11 +18,20 @@ ACT = mybir.ActivationFunctionType
 ALU = mybir.AluOpType
 
 P = 128
+PACK = 4
+PER_COLUMN = 16
 BANK = 512
 PAGES = H // P
-PASSES = H // 512
+PAGES_PER_PASS = PACK
+PASSES = PAGES // PAGES_PER_PASS
 GROUPS = T2 // BANK
+BLOCKS = BANK // P
+PAGE_TILES = 3
 W1_CHUNK = 256
+EARLY_CHUNKS = 2
+FIRST_PIECE = 256
+LATE_ROUNDED_AT = (4096, 7168)
+SLOTS_AT = (0, 8192)
 
 
 def tile_list_lag_rewind_features_kernel(
@@ -33,46 +42,53 @@ def tile_list_lag_rewind_features_kernel(
     with ExitStack() as ctx:
         keep = ctx.enter_context(tc.tile_pool(name="keep", bufs=1))
         shared = ctx.enter_context(tc.tile_pool(name="shared", bufs=1))
-        ring = ctx.enter_context(tc.tile_pool(name="ring", bufs=2))
+        ring2 = ctx.enter_context(tc.tile_pool(name="ring2", bufs=2))
         ring3 = ctx.enter_context(tc.tile_pool(name="ring3", bufs=3))
         ring4 = ctx.enter_context(tc.tile_pool(name="ring4", bufs=4))
         psum = ctx.enter_context(tc.psum_pool(name="psum", bufs=1))
 
         banks = [psum.tile([P, BANK], F32, name=f"bank{i}") for i in range(8)]
-        pairs, b_banks, w_banks = [banks[0:2], banks[2:4]], banks[4:6], banks[6:8]
+        motion_banks, spread_banks, turn_banks = [banks[0:2], banks[2:4]], banks[4:6], banks[6:8]
 
-        def load_scale_rows(queue, plane, rows):
+        def load_scale_rows(plane, rows):
             for q in range(4):
-                queue.dma_start(out=plane[32 * q : 32 * q + 4].bitcast(I32), in_=rows(q).bitcast(I32))
+                nc.sync.dma_start(out=plane[32 * q : 32 * q + 4].bitcast(I32), in_=rows(q).bitcast(I32))
+
+        def load_list(name, source):
+            offsets = keep.tile([P, S // PER_COLUMN], U16, name=name)
+            nc.sync.dma_start(offsets[:], source)
+            return offsets
+
+        def entries(offsets, lo, hi):
+            return offsets[:, lo // PER_COLUMN : hi // PER_COLUMN]
+
+        def half_of(hf):
+            return slice(hf * BANK, (hf + 1) * BANK)
 
         tab_sc = keep.tile([P, T], U8, name="tab_sc", align_bytes=64)
         nc.vector.memset(tab_sc[:].bitcast(I32), 0)
         w2_sc = keep.tile([P, H], U8, name="w2_sc", align_bytes=64)
         nc.gpsimd.memset(w2_sc[:].bitcast(I32), 0)
 
-        def load_list(name, source):
-            t = keep.tile([P, S // 16], U16, name=name)
-            nc.sync.dma_start(t[:], source)
-            return t
-
-        w1_rows = w1.rearrange("(p j) c -> p j c", j=4)
+        w1_rows = w1.rearrange("(p t) c -> p t c", t=PACK)
         w1_raw = []
 
         def load_w1(k):
-            raw = ring4.tile([P, 4, W1_CHUNK], F32, name="w1_raw", tag="quarter")
+            raw = ring4.tile([P, PACK, W1_CHUNK], F32, name="w1_raw", tag="quarter")
             nc.sync.dma_start(out=raw[:], in_=w1_rows[:, :, k * W1_CHUNK : (k + 1) * W1_CHUNK])
             w1_raw.append(raw)
 
         idx = load_list("idx", offs)
         tab_w = shared.tile([P, T], I32, name="tab_w", offset=0)
-        tab_rows = tab_words[0].rearrange("p t i -> p (t i)").bitcast(I32)
+        tab_rows = tab_words[0].rearrange("p c t -> p (c t)").bitcast(I32)
         nc.sync.dma_start(out=tab_w[:, : T // 2], in_=tab_rows[:, : T // 2])
-        load_scale_rows(nc.sync, tab_sc, lambda q: tab_scales[0, 4 * q : 4 * q + 4, :])
+        load_scale_rows(tab_sc, lambda q: tab_scales[0, 4 * q : 4 * q + 4, :])
         nc.sync.dma_start(out=tab_w[:, T // 2 :], in_=tab_rows[:, T // 2 :])
         w2_w = keep.tile([P, 2 * H], U8, name="w2_w", align_bytes=64)
         nc.sync.dma_start(out=w2_w[:].bitcast(I32), in_=w2_words[0].bitcast(I32))
-        load_scale_rows(nc.sync, w2_sc, lambda q: w2_scales[0, 4 * q : 4 * q + 4, :])
-        load_w1(0)
+        load_scale_rows(w2_sc, lambda q: w2_scales[0, 4 * q : 4 * q + 4, :])
+        for k in range(EARLY_CHUNKS):
+            load_w1(k)
         wgs_sb = keep.tile([P, S], F32, name="wgs_sb")
         nc.sync.dma_start(out=wgs_sb[:], in_=wgs)
         idx2 = load_list("idx2", offs2)
@@ -84,23 +100,22 @@ def tile_list_lag_rewind_features_kernel(
         ident = keep.tile([P, P], F32, name="ident")
         make_identity(nc, ident[:])
 
-        pages = [keep.tile([P, T2], F32, name=f"page{i}") for i in range(3)]
-        for t in pages:
-            nc.gpsimd.memset(t[:], 0.0)
+        pages = [keep.tile([P, T2], F32, name=f"page{i}") for i in range(PAGE_TILES)]
+        for page in pages:
+            nc.vector.memset(page[:], 0.0)
         w3_sc = keep.tile([P, PASSES, N], U8, name="w3_sc", align_bytes=64)
         nc.gpsimd.memset(w3_sc[:].rearrange("p a n -> p (a n)").bitcast(I32), 0)
 
         hist_sb = []
 
         def load_hist(c):
-            t = ring4.tile([P, T2], F32, name="hist_sb", tag="rows")
-            nc.sync.dma_start(out=t[:], in_=hist[c * P : (c + 1) * P, :])
-            hist_sb.append(t)
+            rows = ring4.tile([P, T2], F32, name="hist_sb", tag="rows")
+            nc.sync.dma_start(out=rows[:], in_=hist[c * P : (c + 1) * P, :])
+            hist_sb.append(rows)
 
-        load_w1(1)
+        for k in range(EARLY_CHUNKS, H // W1_CHUNK):
+            load_w1(k)
         load_hist(0)
-        load_w1(2)
-        load_w1(3)
         load_hist(1)
 
         v_sc = keep.tile([P, S], U8, name="v_sc", align_bytes=64)
@@ -108,114 +123,126 @@ def tile_list_lag_rewind_features_kernel(
         v_w = keep.tile([P, S], U32, name="v_w", align_bytes=64)
         for hf in range(2):
             nc.vector.tensor_copy(
-                v_w[:, hf * BANK : (hf + 1) * BANK],
-                tab_w[:].bitcast(U32).indirect(idx[:, hf * 32 : (hf + 1) * 32]),
+                v_w[:, half_of(hf)], tab_w[:].bitcast(U32).indirect(entries(idx, hf * BANK, (hf + 1) * BANK))
             )
-
-        slots = [shared.tile([P, T2], F32, name=f"slots{i}", offset=i * 4 * T2) for i in range(2)]
-        for t in slots:
-            nc.gpsimd.memset(t[:], 0.0)
 
         w1_w = keep.tile([P, H], U32, name="w1_w", align_bytes=64)
         w1_sc = keep.tile([P, H], U8, name="w1_sc", align_bytes=64)
 
         def quantize_w1(k):
             cols = slice(k * W1_CHUNK, (k + 1) * W1_CHUNK)
-            grouped = ring.tile([P, W1_CHUNK, 4], BF16, name="w1_grouped", align_bytes=64)
-            nc.scalar.copy(out=grouped[:], in_=w1_raw[k][:].rearrange("p j c -> p c j"))
+            if k < EARLY_CHUNKS:
+                rounded = ring2.tile([P, W1_CHUNK, PACK], BF16, name="w1_rounded", align_bytes=64)
+                nc.vector.tensor_copy(out=rounded[:], in_=w1_raw[k][:].rearrange("p t c -> p c t"))
+            else:
+                rounded = shared.tile(
+                    [P, W1_CHUNK, PACK], BF16, name=f"w1_rounded{k}", align_bytes=64,
+                    offset=LATE_ROUNDED_AT[k - EARLY_CHUNKS],
+                )
+                nc.scalar.copy(out=rounded[:], in_=w1_raw[k][:].rearrange("p t c -> p c t"))
             nc.vector.quantize_mx(
                 out=w1_w[:, cols].bitcast(FP8X4), scales=w1_sc[:, cols],
-                in_=grouped[:].rearrange("p c j -> p (c j)"),
+                in_=rounded[:].rearrange("p c t -> p (c t)"),
             )
+
+        def step_halves(step):
+            return [divmod(unit, 2) for unit in (2 * step - 1, 2 * step) if 0 <= unit < 2 * PAGES]
 
         damp = {}
 
-        def damping(c):
-            r = ring3.tile([P, S], F32, name="damp")
-            damp[c] = r
-            hs = [slice(hf * BANK, (hf + 1) * BANK) for hf in range(2)]
-            for hf in range(2):
+        def damping(step):
+            damp[step] = ring3.tile([P, 2, BANK], F32, name="damp")
+            halves = step_halves(step)
+            sums = spread_banks[::-1] if step == 1 else spread_banks
+            for n, (c, hf) in enumerate(halves):
                 nc.tensor.matmul_mx(
-                    out=b_banks[hf][:],
+                    out=sums[n][:],
                     lhsT=w2_w[:, 2 * c * P : 2 * (c + 1) * P].bitcast(FP4X4),
                     lhsT_scale=w2_sc[:, c * P : (c + 1) * P],
-                    rhs=v_w[:, hs[hf]].bitcast(FP8X4), rhs_scale=v_sc[:, hs[hf]],
+                    rhs=v_w[:, half_of(hf)].bitcast(FP8X4), rhs_scale=v_sc[:, half_of(hf)],
                     start=True, stop=True,
                 )
-            for hf in range(2):
-                nc.scalar.activation(r[:, hs[hf]], b_banks[hf][:], ACT.Abs)
-            for hf in range(2):
-                nc.scalar.activation(r[:, hs[hf]], r[:, hs[hf]], ACT.Abs_reciprocal_sqrt, bias=half[:])
-            for hf in range(2):
-                nc.scalar.activation(r[:, hs[hf]], r[:, hs[hf]], ACT.Square)
+            if len(halves) == 2:
+                runs = [(n, slice(0, BANK)) for n in range(2)]
+            else:
+                runs = [(0, slice(0, BANK // 2)), (0, slice(BANK // 2, BANK))]
+            for n, cols in runs:
+                nc.scalar.activation(damp[step][:, n, cols], sums[n][:, cols], ACT.Abs)
+            for n, cols in runs:
+                nc.scalar.activation(
+                    damp[step][:, n, cols], damp[step][:, n, cols], ACT.Abs_reciprocal_sqrt, bias=half[:]
+                )
+            for n, cols in runs:
+                nc.scalar.activation(damp[step][:, n, cols], damp[step][:, n, cols], ACT.Square)
 
-        def motion(c):
-            for hf in range(2):
-                cols = slice(hf * BANK, (hf + 1) * BANK)
+        def motion(step):
+            for n, (c, hf) in enumerate(step_halves(step)):
                 nc.tensor.matmul_mx(
-                    out=pairs[c % 2][hf][:],
+                    out=motion_banks[step % 2][n][:],
                     lhsT=w1_w[:, c * P : (c + 1) * P].bitcast(FP8X4),
                     lhsT_scale=w1_sc[:, c * P : (c + 1) * P],
-                    rhs=v_w[:, cols].bitcast(FP8X4), rhs_scale=v_sc[:, cols],
+                    rhs=v_w[:, half_of(hf)].bitcast(FP8X4), rhs_scale=v_sc[:, half_of(hf)],
                     start=True, stop=True,
                 )
 
-        def fill_page(c):
-            h = ring.tile([P, S], F32, name="h", tag="listed")
-            page = pages[c % len(pages)]
-            for hf in range(2):
-                cols = slice(hf * BANK, (hf + 1) * BANK)
-                nc.vector.tensor_tensor(h[:, cols], pairs[c % 2][hf][:], damp[c][:, cols], ALU.mult)
-                if c == 0:
-                    nc.vector.tensor_tensor(
-                        page[:].indirect(idx2[:, hf * 32 : (hf + 1) * 32]), h[:, cols], wgs_sb[:, cols], ALU.mult
-                    )
-            if c > 0:
-                nc.vector.tensor_tensor(page[:].indirect(idx2[:]), h[:], wgs_sb[:], ALU.mult)
+        h_sb = {}
 
-        zt = [[keep.tile([P, 4, 2, P, 2], BF16, name=f"zt{a}_{g}") for g in range(GROUPS)] for a in range(PASSES)]
+        def damp_motion(step, lo, hi):
+            for n, (c, hf) in enumerate(step_halves(step)):
+                if c not in h_sb:
+                    h_sb[c] = ring2.tile([P, S], F32, name="h", tag="listed")
+                nc.vector.tensor_tensor(
+                    h_sb[c][:, hf * BANK + lo : hf * BANK + hi],
+                    motion_banks[step % 2][n][:, lo:hi], damp[step][:, n, lo:hi], ALU.mult,
+                )
 
-        def add_history(c, groups, parts=(0, 1)):
-            a, cc = divmod(c, 4)
-            last = c == PAGES - 1
-            for g in groups:
-                bank = (b_banks + pairs[(c + 1) % 2])[g]
-                for n in parts:
-                    rows = (hist_sb[c], pages[c % 3])[n]
-                    for k in range(4):
-                        t0 = (4 * g + k) * P
-                        nc.tensor.matmul(
-                            bank[:, k * P : (k + 1) * P], lhsT=rows[:, t0 : t0 + P], rhs=ident[:],
-                            is_transpose=True, start=(n == 0 and k == 0), stop=(n == 1 and k == 3),
-                        )
-                if 1 not in parts:
-                    continue
-                dst = zt[a][g][:, :, :, 32 * cc : 32 * cc + 32, :]
-                src = bank[:].rearrange("p (k i u e) -> p k u i e", k=4, u=2, e=2)
-                if last and g % 2 == 1:
-                    nc.vector.tensor_copy(out=dst, in_=src)
-                else:
-                    nc.scalar.copy(out=dst, in_=src)
+        def scatter_page(c, lo, hi):
+            nc.vector.tensor_tensor(
+                pages[c % PAGE_TILES][:].indirect(entries(idx2, lo, hi)),
+                h_sb[c][:, lo:hi], wgs_sb[:, lo:hi], ALU.mult,
+            )
+
+        z_turned = [
+            [keep.tile([P, BLOCKS, 2, P, 2], BF16, name=f"z_turned{a}_{g}") for g in range(GROUPS)]
+            for a in range(PASSES)
+        ]
+
+        def history_banks(c):
+            return spread_banks + motion_banks[c % 2 if c < PAGES - 1 else 0]
+
+        def turn_into_sum(c, g, rows, opens):
+            bank = history_banks(c)[g]
+            for k in range(BLOCKS):
+                tick = g * BANK + k * P
+                nc.tensor.matmul(
+                    bank[:, k * P : (k + 1) * P], lhsT=rows[:, tick : tick + P], rhs=ident[:], is_transpose=True,
+                    start=(opens and k == 0), stop=(not opens and k == BLOCKS - 1),
+                )
+
+        def close_sum(c, g, copy):
+            turn_into_sum(c, g, pages[c % PAGE_TILES], False)
+            a, quarter = divmod(c, PAGES_PER_PASS)
+            copy(
+                out=z_turned[a][g][:, :, :, 32 * quarter : 32 * quarter + 32, :],
+                in_=history_banks(c)[g][:].rearrange("p (k i u e) -> p k u i e", k=BLOCKS, u=2, e=2),
+            )
 
         z_w = [keep.tile([P, T2], U32, name=f"z_w{a}", align_bytes=64) for a in range(PASSES)]
         z_sc = [keep.tile([P, T2], U8, name=f"z_sc{a}", align_bytes=64) for a in range(PASSES)]
 
-        def quantize_z(a, g, turn_banks, share):
-            words = zt[a][g][:].rearrange("p k u r e -> p (k u r e)").bitcast(F32)
+        def quantize_z(a, g, pair, copies):
+            words = z_turned[a][g][:].rearrange("p k u r e -> p (k u r e)").bitcast(F32)
             grouped = ring3.tile([P, BANK, 2], F32, name="z_grouped", align_bytes=64)
             for j in range(2):
-                bank = turn_banks[j]
                 for u in range(2):
                     for kk in range(2):
-                        w0 = ((2 * j + kk) * 2 + u) * P
-                        o0 = (u * 2 + kk) * P
-                        nc.tensor.transpose(bank[:, o0 : o0 + P], words[:, w0 : w0 + P], ident[:])
-                dst = grouped[:, j * 256 : (j + 1) * 256, :]
-                src = bank[:].rearrange("p (u n) -> p n u", u=2)
-                if share and j == 1:
-                    nc.vector.tensor_copy(out=dst, in_=src)
-                else:
-                    nc.scalar.copy(out=dst, in_=src)
+                        source = ((2 * j + kk) * 2 + u) * P
+                        target = (u * 2 + kk) * P
+                        nc.tensor.transpose(pair[j][:, target : target + P], words[:, source : source + P], ident[:])
+                copies[j](
+                    out=grouped[:, j * BANK // 2 : (j + 1) * BANK // 2, :],
+                    in_=pair[j][:].rearrange("p (u n) -> p n u", u=2),
+                )
             cols = slice(g * BANK, (g + 1) * BANK)
             nc.vector.quantize_mx(
                 out=z_w[a][:, cols].bitcast(FP8X4), scales=z_sc[a][:, cols],
@@ -228,78 +255,98 @@ def tile_list_lag_rewind_features_kernel(
         snap_sb = []
         late_lists = []
 
-        def load_second_stage():
-            nc.sync.dma_start(out=w3_w[:], in_=w3_words.rearrange("a p c i -> p a (c i)").bitcast(I32))
-            load_scale_rows(nc.sync, w3_sc, lambda q: w3_scales[:, 4 * q : 4 * q + 4, :].rearrange("a q n -> q a n"))
+        def preload_second_stage():
+            nc.sync.dma_start(out=w3_w[:], in_=w3_words.rearrange("a p c t -> p a (c t)").bitcast(I32))
+            load_scale_rows(w3_sc, lambda q: w3_scales[:, 4 * q : 4 * q + 4, :].rearrange("a q n -> q a n"))
             nc.sync.dma_start(out=wgo_sb[:], in_=wgo)
             late_lists.extend([load_list("idx3", offs3), load_list("idx4", offs4)])
-            with nc.allow_non_contiguous_dma(reason="one value of lam for each partition"):
+            with nc.allow_non_contiguous_dma(reason="one value of lam for each partition and row tile"):
                 nc.sync.dma_start(out=lam_sb[:], in_=lam.rearrange("(i p) -> p i", p=P))
             for i in range(N // P):
-                t = ring4.tile([P, M], F32, name="snap_sb", tag="quarter")
-                nc.sync.dma_start(out=t[:], in_=snap[i * P : (i + 1) * P, :])
-                snap_sb.append(t)
+                rows = ring4.tile([P, M], F32, name="snap_sb", tag="quarter")
+                nc.sync.dma_start(out=rows[:], in_=snap[i * P : (i + 1) * P, :])
+                snap_sb.append(rows)
 
+        slots = []
         quantize_w1(0)
         damping(0)
         motion(0)
-        motion(1)
         damping(1)
+        motion(1)
+        damp_motion(0, 0, FIRST_PIECE)
+        scatter_page(0, 0, FIRST_PIECE)
+        damp_motion(0, FIRST_PIECE, BANK)
+        quantize_w1(1)
+        damping(2)
         for c in range(PAGES):
             if c + 2 < PAGES:
                 load_hist(c + 2)
             if c == 2:
-                load_second_stage()
-            fill_page(c)
-            if c < 3:
-                quantize_w1(c + 1)
+                preload_second_stage()
+            damp_motion(c + 1, 0, BANK)
+            scatter_page(c, FIRST_PIECE if c == 0 else 0, S)
+            if c == 0:
+                for k in range(EARLY_CHUNKS, H // W1_CHUNK):
+                    quantize_w1(k)
+                for i, offset in enumerate(SLOTS_AT):
+                    slots.append(shared.tile([P, T2], F32, name=f"slots{i}", offset=offset))
+                    nc.gpsimd.memset(slots[i][:], 0.0)
+            if c + 2 <= PAGES:
+                motion(c + 2)
             if c >= 1:
-                if c + 1 < PAGES:
-                    motion(c + 1)
-                add_history(c - 1, range(GROUPS))
-            if c + 2 < PAGES:
-                damping(c + 2)
-            for g in {4: (0,), 5: (1,), 6: (2,), 7: (3,)}.get(c, ()):
-                quantize_z(0, g, w_banks, False)
-        add_history(PAGES - 1, range(GROUPS), (0,))
-        add_history(PAGES - 1, range(GROUPS), (1,))
+                for g in range(GROUPS):
+                    turn_into_sum(c - 1, g, hist_sb[c - 1], True)
+                    close_sum(c - 1, g, nc.scalar.copy)
+            if c + 3 <= PAGES:
+                damping(c + 3)
+            if c >= PAGES_PER_PASS:
+                quantize_z(0, c - PAGES_PER_PASS, turn_banks, (nc.scalar.copy, nc.scalar.copy))
 
-        def product_pass(i, g, a, bank):
+        for g in range(GROUPS):
+            turn_into_sum(PAGES - 1, g, hist_sb[PAGES - 1], True)
+        for g in range(GROUPS):
+            close_sum(PAGES - 1, g, (nc.scalar.copy, nc.vector.tensor_copy)[g % 2])
+
+        y_banks = motion_banks[1] + spread_banks
+        y_sb = [ring4.tile([P, T2], F32, name="y_sb", tag="rows") for i in range(N // P)]
+
+        def product_pass(i, g, a):
             cols = slice(g * BANK, (g + 1) * BANK)
             nc.tensor.matmul_mx(
-                out=bank[:],
+                out=y_banks[g][:],
                 lhsT=w3_w[:, a, i * P : (i + 1) * P].bitcast(FP8X4),
                 lhsT_scale=w3_sc[:, a, i * P : (i + 1) * P],
                 rhs=z_w[a][:, cols].bitcast(FP8X4), rhs_scale=z_sc[a][:, cols],
                 start=(a == 0), stop=(a == PASSES - 1),
             )
 
-        y_banks = [w_banks + pairs[1], w_banks + pairs[1]]
-        y_sb = [ring4.tile([P, T2], F32, name="y_sb", tag="rows") for i in range(N // P)]
-
         def leave_bank(i, g):
-            cols = slice(g * BANK, (g + 1) * BANK)
-            nc.scalar.activation(y_sb[i][:, cols], y_banks[i % 2][g][:], ACT.Copy, scale=lam_sb[:, i : i + 1])
+            nc.scalar.activation(
+                y_sb[i][:, g * BANK : (g + 1) * BANK], y_banks[g][:], ACT.Copy, scale=lam_sb[:, i : i + 1]
+            )
 
+        free_groups = len(motion_banks[1])
+        turn_pairs = (turn_banks, spread_banks, motion_banks[0])
+        for g in range(free_groups):
+            product_pass(0, g, 0)
         for g in range(GROUPS):
-            product_pass(0, g, 0, y_banks[0][g])
+            quantize_z(1, g, turn_pairs[g % len(turn_pairs)], (nc.vector.tensor_copy, nc.scalar.copy))
         for g in range(GROUPS):
-            quantize_z(1, g, (b_banks, pairs[0])[g % 2], True)
-            product_pass(0, g, 1, y_banks[0][g])
+            if g >= free_groups:
+                product_pass(0, g, 0)
+            product_pass(0, g, 1)
             leave_bank(0, g)
 
         idx3, idx4 = late_lists
-
-        def pick(i):
-            x = ring.tile([P, M], F32, name="x", tag="listed")
-            nc.vector.tensor_tensor(x[:], y_sb[i][:].indirect(idx3[:]), snap_sb[i][:], ALU.add)
-            nc.vector.tensor_tensor(slots[i % 2][:].indirect(idx4[:]), x[:], wgo_sb[:], ALU.mult)
-            nc.sync.dma_start(out=out[i * P : (i + 1) * P, :], in_=slots[i % 2][:])
-
         for i in range(N // P):
             if i + 1 < N // P:
                 for g in range(GROUPS):
                     for a in range(PASSES):
-                        product_pass(i + 1, g, a, y_banks[(i + 1) % 2][g])
+                        product_pass(i + 1, g, a)
                     leave_bank(i + 1, g)
-            pick(i)
+            x = ring2.tile([P, M], F32, name="x", tag="listed")
+            nc.vector.tensor_tensor(x[:], y_sb[i][:].indirect(idx3[:]), snap_sb[i][:], ALU.add)
+            nc.vector.tensor_tensor(slots[i % 2][:].indirect(idx4[:]), x[:], wgo_sb[:], ALU.mult)
+            for hf in range(2):
+                cols = slice(hf * T2 // 2, (hf + 1) * T2 // 2)
+                nc.sync.dma_start(out=out[i * P : (i + 1) * P, cols], in_=slots[i % 2][:, cols])

@@ -174,6 +174,12 @@ def tile_list_lag_rewind_features_kernel(
                 )
             for n, cols in runs:
                 nc.scalar.activation(damp[step][:, n, cols], damp[step][:, n, cols], ACT.Square)
+            for n, cols in runs:
+                first = halves[n][1] * BANK
+                nc.gpsimd.tensor_tensor(
+                    damp[step][:, n, cols], damp[step][:, n, cols],
+                    wgs_sb[:, first + cols.start : first + cols.stop], ALU.mult,
+                )
 
         def motion(step):
             for n, (c, hf) in enumerate(step_halves(step)):
@@ -197,10 +203,7 @@ def tile_list_lag_rewind_features_kernel(
                 )
 
         def scatter_page(c, lo, hi):
-            nc.vector.tensor_tensor(
-                pages[c % PAGE_TILES][:].indirect(entries(idx2, lo, hi)),
-                h_sb[c][:, lo:hi], wgs_sb[:, lo:hi], ALU.mult,
-            )
+            nc.vector.tensor_copy(pages[c % PAGE_TILES][:].indirect(entries(idx2, lo, hi)), h_sb[c][:, lo:hi])
 
         z_turned = [
             [keep.tile([P, BLOCKS, 2, P, 2], BF16, name=f"z_turned{a}_{g}") for g in range(GROUPS)]

@@ -21,17 +21,30 @@ P = 128
 PACK = 4
 PER_COLUMN = 16
 BANK = 512
+QUARTER = 256
 PAGES = H // P
+LAST = PAGES - 1
 PAGES_PER_PASS = PACK
 PASSES = PAGES // PAGES_PER_PASS
 GROUPS = T2 // BANK
 BLOCKS = BANK // P
 PAGE_TILES = 3
-W1_CHUNK = 256
-EARLY_CHUNKS = 2
-FIRST_PIECE = 256
-LATE_ROUNDED_AT = (4096, 7168)
-SLOTS_AT = (0, 8192)
+AHEAD = 3
+VECTOR_PAGES = 2
+W1_CHUNKS = ((0, 128), (128, 256), (256, 512), (512, 1024))
+TURN_PAIRS = (0, 2, 4, 6)
+VECTOR_CHUNKS = 2
+TURN_COPIES = ((0, 1), (0, 1), (0, 1), (0, 1))
+KIB = 1024
+Z_CODES_AT = ((0, 2 * KIB, 4 * KIB, 6 * KIB), (8 * KIB, 10 * KIB, 12 * KIB, 14 * KIB))
+TABLE_AT = 0
+LAST_VALUES_AT = (0, 5 * KIB + 512)
+TABLE_SCALES_AT = 16 * KIB
+SLOTS_AT = (20 * KIB, 28 * KIB)
+GAINS_AT = (26 * KIB, 36 * KIB, 56 * KIB)
+SQUARE_ON_GPSIMD = ((3, 0), (4, 0), (5, 0), (6, 0))
+ROUNDED_AT = (30 * KIB, 31 * KIB, 32 * KIB, 20 * KIB)
+RAW_AT = 40 * KIB
 
 
 def tile_list_lag_rewind_features_kernel(
@@ -42,13 +55,12 @@ def tile_list_lag_rewind_features_kernel(
     with ExitStack() as ctx:
         keep = ctx.enter_context(tc.tile_pool(name="keep", bufs=1))
         shared = ctx.enter_context(tc.tile_pool(name="shared", bufs=1))
-        ring2 = ctx.enter_context(tc.tile_pool(name="ring2", bufs=2))
-        ring3 = ctx.enter_context(tc.tile_pool(name="ring3", bufs=3))
         ring4 = ctx.enter_context(tc.tile_pool(name="ring4", bufs=4))
         psum = ctx.enter_context(tc.psum_pool(name="psum", bufs=1))
 
         banks = [psum.tile([P, BANK], F32, name=f"bank{i}") for i in range(8)]
-        motion_banks, spread_banks, turn_banks = [banks[0:2], banks[2:4]], banks[4:6], banks[6:8]
+        product_banks, sum_banks = banks[0:4], banks[4:8]
+        spread_banks, motion_banks = banks[0:2], banks[2:4]
 
         def load_scale_rows(plane, rows):
             for q in range(4):
@@ -65,7 +77,7 @@ def tile_list_lag_rewind_features_kernel(
         def half_of(hf):
             return slice(hf * BANK, (hf + 1) * BANK)
 
-        tab_sc = keep.tile([P, T], U8, name="tab_sc", align_bytes=64)
+        tab_sc = shared.tile([P, T], U8, name="tab_sc", align_bytes=64, offset=TABLE_SCALES_AT)
         nc.vector.memset(tab_sc[:].bitcast(I32), 0)
         w2_sc = keep.tile([P, H], U8, name="w2_sc", align_bytes=64)
         nc.gpsimd.memset(w2_sc[:].bitcast(I32), 0)
@@ -74,24 +86,28 @@ def tile_list_lag_rewind_features_kernel(
         w1_raw = []
 
         def load_w1(k):
-            raw = ring4.tile([P, PACK, W1_CHUNK], F32, name="w1_raw", tag="quarter")
-            nc.sync.dma_start(out=raw[:], in_=w1_rows[:, :, k * W1_CHUNK : (k + 1) * W1_CHUNK])
+            lo, hi = W1_CHUNKS[k]
+            raw = shared.tile([P, PACK, hi - lo], F32, name=f"w1_raw{k}", offset=RAW_AT + 4 * PACK * lo)
+            nc.sync.dma_start(out=raw[:], in_=w1_rows[:, :, lo:hi])
             w1_raw.append(raw)
 
         idx = load_list("idx", offs)
-        tab_w = shared.tile([P, T], I32, name="tab_w", offset=0)
+        tab_w = shared.tile([P, T], I32, name="tab_w", offset=TABLE_AT)
         tab_rows = tab_words[0].rearrange("p c t -> p (c t)").bitcast(I32)
-        nc.sync.dma_start(out=tab_w[:, : T // 2], in_=tab_rows[:, : T // 2])
+        nc.sync.dma_start(out=tab_w[:, : T // 4], in_=tab_rows[:, : T // 4])
         load_scale_rows(tab_sc, lambda q: tab_scales[0, 4 * q : 4 * q + 4, :])
-        nc.sync.dma_start(out=tab_w[:, T // 2 :], in_=tab_rows[:, T // 2 :])
+        nc.sync.dma_start(out=tab_w[:, T // 4 :], in_=tab_rows[:, T // 4 :])
         w2_w = keep.tile([P, 2 * H], U8, name="w2_w", align_bytes=64)
         nc.sync.dma_start(out=w2_w[:].bitcast(I32), in_=w2_words[0].bitcast(I32))
         load_scale_rows(w2_sc, lambda q: w2_scales[0, 4 * q : 4 * q + 4, :])
-        for k in range(EARLY_CHUNKS):
+        for k in range(VECTOR_CHUNKS):
             load_w1(k)
-        wgs_sb = keep.tile([P, S], F32, name="wgs_sb")
-        nc.sync.dma_start(out=wgs_sb[:], in_=wgs)
+        wgs_sb = [keep.tile([P, BANK], F32, name=f"wgs_sb{hf}") for hf in range(2)]
+        nc.sync.dma_start(out=wgs_sb[0][:], in_=wgs[:, half_of(0)])
         idx2 = load_list("idx2", offs2)
+        nc.sync.dma_start(out=wgs_sb[1][:], in_=wgs[:, half_of(1)])
+        for k in range(VECTOR_CHUNKS, len(W1_CHUNKS)):
+            load_w1(k)
 
         half = keep.tile([P, 1], F32, name="half")
         nc.gpsimd.memset(half[:], 0.5)
@@ -99,12 +115,12 @@ def tile_list_lag_rewind_features_kernel(
         nc.scalar.activation(warm[:], half[:], ACT.Abs_reciprocal_sqrt)
         ident = keep.tile([P, P], F32, name="ident")
         make_identity(nc, ident[:])
+        w3_sc = keep.tile([P, PASSES, N], U8, name="w3_sc", align_bytes=64)
+        nc.gpsimd.memset(w3_sc[:].rearrange("p a n -> p (a n)").bitcast(I32), 0)
 
         pages = [keep.tile([P, T2], F32, name=f"page{i}") for i in range(PAGE_TILES)]
         for page in pages:
             nc.vector.memset(page[:], 0.0)
-        w3_sc = keep.tile([P, PASSES, N], U8, name="w3_sc", align_bytes=64)
-        nc.gpsimd.memset(w3_sc[:].rearrange("p a n -> p (a n)").bitcast(I32), 0)
 
         hist_sb = []
 
@@ -113,10 +129,8 @@ def tile_list_lag_rewind_features_kernel(
             nc.sync.dma_start(out=rows[:], in_=hist[c * P : (c + 1) * P, :])
             hist_sb.append(rows)
 
-        for k in range(EARLY_CHUNKS, H // W1_CHUNK):
-            load_w1(k)
-        load_hist(0)
-        load_hist(1)
+        for c in range(PAGES_PER_PASS):
+            load_hist(c)
 
         v_sc = keep.tile([P, S], U8, name="v_sc", align_bytes=64)
         nc.vector.tensor_copy(v_sc[:], tab_sc[:].indirect(idx[:]))
@@ -130,91 +144,87 @@ def tile_list_lag_rewind_features_kernel(
         w1_sc = keep.tile([P, H], U8, name="w1_sc", align_bytes=64)
 
         def quantize_w1(k):
-            cols = slice(k * W1_CHUNK, (k + 1) * W1_CHUNK)
-            if k < EARLY_CHUNKS:
-                rounded = ring2.tile([P, W1_CHUNK, PACK], BF16, name="w1_rounded", align_bytes=64)
+            lo, hi = W1_CHUNKS[k]
+            rounded = shared.tile([P, hi - lo, PACK], BF16, name=f"w1_rounded{k}", align_bytes=64, offset=ROUNDED_AT[k])
+            if k < VECTOR_CHUNKS:
                 nc.vector.tensor_copy(out=rounded[:], in_=w1_raw[k][:].rearrange("p t c -> p c t"))
             else:
-                rounded = shared.tile(
-                    [P, W1_CHUNK, PACK], BF16, name=f"w1_rounded{k}", align_bytes=64,
-                    offset=LATE_ROUNDED_AT[k - EARLY_CHUNKS],
-                )
-                nc.scalar.copy(out=rounded[:], in_=w1_raw[k][:].rearrange("p t c -> p c t"))
+                for at in range(0, hi - lo, P):
+                    nc.gpsimd.tensor_scalar(
+                        rounded[:, at : at + P, :], w1_raw[k][:, :, at : at + P].rearrange("p t c -> p c t"),
+                        1.0, 0.0, ALU.mult, ALU.add,
+                    )
             nc.vector.quantize_mx(
-                out=w1_w[:, cols].bitcast(FP8X4), scales=w1_sc[:, cols],
+                out=w1_w[:, lo:hi].bitcast(FP8X4), scales=w1_sc[:, lo:hi],
                 in_=rounded[:].rearrange("p c t -> p (c t)"),
             )
 
-        def step_halves(step):
-            return [divmod(unit, 2) for unit in (2 * step - 1, 2 * step) if 0 <= unit < 2 * PAGES]
+        def spread(c, hf):
+            nc.tensor.matmul_mx(
+                out=spread_banks[hf][:],
+                lhsT=w2_w[:, 2 * c * P : 2 * (c + 1) * P].bitcast(FP4X4),
+                lhsT_scale=w2_sc[:, c * P : (c + 1) * P],
+                rhs=v_w[:, half_of(hf)].bitcast(FP8X4), rhs_scale=v_sc[:, half_of(hf)],
+                start=True, stop=True,
+            )
 
-        damp = {}
+        def motion(c, lo, hi, bank):
+            nc.tensor.matmul_mx(
+                out=bank[:, : hi - lo],
+                lhsT=w1_w[:, c * P : (c + 1) * P].bitcast(FP8X4),
+                lhsT_scale=w1_sc[:, c * P : (c + 1) * P],
+                rhs=v_w[:, lo:hi].bitcast(FP8X4), rhs_scale=v_sc[:, lo:hi],
+                start=True, stop=True,
+            )
 
-        def damping(step):
-            damp[step] = ring3.tile([P, 2, BANK], F32, name="damp")
-            halves = step_halves(step)
-            sums = spread_banks[::-1] if step == 1 else spread_banks
-            for n, (c, hf) in enumerate(halves):
-                nc.tensor.matmul_mx(
-                    out=sums[n][:],
-                    lhsT=w2_w[:, 2 * c * P : 2 * (c + 1) * P].bitcast(FP4X4),
-                    lhsT_scale=w2_sc[:, c * P : (c + 1) * P],
-                    rhs=v_w[:, half_of(hf)].bitcast(FP8X4), rhs_scale=v_sc[:, half_of(hf)],
-                    start=True, stop=True,
-                )
-            if len(halves) == 2:
-                runs = [(n, slice(0, BANK)) for n in range(2)]
-            else:
-                runs = [(0, slice(0, BANK // 2)), (0, slice(BANK // 2, BANK))]
-            for n, cols in runs:
-                nc.scalar.activation(damp[step][:, n, cols], sums[n][:, cols], ACT.Abs)
-            for n, cols in runs:
-                nc.scalar.activation(
-                    damp[step][:, n, cols], damp[step][:, n, cols], ACT.Abs_reciprocal_sqrt, bias=half[:]
-                )
-            for n, cols in runs:
-                nc.scalar.activation(damp[step][:, n, cols], damp[step][:, n, cols], ACT.Square)
-            for n, cols in runs:
-                first = halves[n][1] * BANK
+        gains = {}
+
+        def make_gains(c, runs):
+            if c not in gains:
+                gains[c] = shared.tile([P, S], F32, name=f"gains{c}", offset=GAINS_AT[c % len(GAINS_AT)])
+            for lo, hi in runs:
+                nc.scalar.activation(gains[c][:, lo:hi], spread_banks[lo // BANK][:, lo % BANK : lo % BANK + hi - lo], ACT.Abs)
+            for lo, hi in runs:
+                nc.scalar.activation(gains[c][:, lo:hi], gains[c][:, lo:hi], ACT.Abs_reciprocal_sqrt, bias=half[:])
+            for lo, hi in runs:
+                if (c, lo // BANK) in SQUARE_ON_GPSIMD:
+                    nc.gpsimd.tensor_tensor(gains[c][:, lo:hi], gains[c][:, lo:hi], gains[c][:, lo:hi], ALU.mult)
+                else:
+                    nc.scalar.activation(gains[c][:, lo:hi], gains[c][:, lo:hi], ACT.Square)
+            for lo, hi in runs:
                 nc.gpsimd.tensor_tensor(
-                    damp[step][:, n, cols], damp[step][:, n, cols],
-                    wgs_sb[:, first + cols.start : first + cols.stop], ALU.mult,
+                    gains[c][:, lo:hi], gains[c][:, lo:hi],
+                    wgs_sb[lo // BANK][:, lo % BANK : lo % BANK + hi - lo], ALU.mult,
                 )
 
-        def motion(step):
-            for n, (c, hf) in enumerate(step_halves(step)):
-                nc.tensor.matmul_mx(
-                    out=motion_banks[step % 2][n][:],
-                    lhsT=w1_w[:, c * P : (c + 1) * P].bitcast(FP8X4),
-                    lhsT_scale=w1_sc[:, c * P : (c + 1) * P],
-                    rhs=v_w[:, half_of(hf)].bitcast(FP8X4), rhs_scale=v_sc[:, half_of(hf)],
-                    start=True, stop=True,
-                )
+        def apply_gains(c, lo, hi, sums, values):
+            if c < VECTOR_PAGES:
+                nc.vector.tensor_tensor(values, sums, gains[c][:, lo:hi], ALU.mult)
+            else:
+                nc.scalar.copy(out=values, in_=sums)
+                nc.gpsimd.tensor_tensor(values, values, gains[c][:, lo:hi], ALU.mult)
 
-        h_sb = {}
+        def scatter(c, lo, hi, values):
+            nc.vector.tensor_copy(pages[c % PAGE_TILES][:].indirect(entries(idx2, lo, hi)), values)
 
-        def damp_motion(step, lo, hi):
-            for n, (c, hf) in enumerate(step_halves(step)):
-                if c not in h_sb:
-                    h_sb[c] = ring2.tile([P, S], F32, name="h", tag="listed")
-                nc.vector.tensor_tensor(
-                    h_sb[c][:, hf * BANK + lo : hf * BANK + hi],
-                    motion_banks[step % 2][n][:, lo:hi], damp[step][:, n, lo:hi], ALU.mult,
-                )
+        halves = [(0, BANK), (BANK, S)]
 
-        def scatter_page(c, lo, hi):
-            nc.vector.tensor_copy(pages[c % PAGE_TILES][:].indirect(entries(idx2, lo, hi)), h_sb[c][:, lo:hi])
+        def whole_page(c, a_banks):
+            for hf in range(2):
+                spread(c, hf)
+            make_gains(c, halves)
+            values = ring4.tile([P, S], F32, name="values", tag="listed")
+            for hf, (lo, hi) in enumerate(halves):
+                motion(c, lo, hi, a_banks[hf])
+                apply_gains(c, lo, hi, a_banks[hf][:], values[:, lo:hi])
+            scatter(c, 0, S, values[:])
 
         z_turned = [
             [keep.tile([P, BLOCKS, 2, P, 2], BF16, name=f"z_turned{a}_{g}") for g in range(GROUPS)]
             for a in range(PASSES)
         ]
 
-        def history_banks(c):
-            return spread_banks + motion_banks[c % 2 if c < PAGES - 1 else 0]
-
-        def turn_into_sum(c, g, rows, opens):
-            bank = history_banks(c)[g]
+        def turn_into_sum(bank, g, rows, opens):
             for k in range(BLOCKS):
                 tick = g * BANK + k * P
                 nc.tensor.matmul(
@@ -222,20 +232,22 @@ def tile_list_lag_rewind_features_kernel(
                     start=(opens and k == 0), stop=(not opens and k == BLOCKS - 1),
                 )
 
-        def close_sum(c, g, copy):
-            turn_into_sum(c, g, pages[c % PAGE_TILES], False)
+        def open_sums(c, sums, groups):
+            for g in groups:
+                turn_into_sum(sums[g], g, hist_sb[c], True)
+
+        def close_sums(c, sums, groups, copies):
             a, quarter = divmod(c, PAGES_PER_PASS)
-            copy(
-                out=z_turned[a][g][:, :, :, 32 * quarter : 32 * quarter + 32, :],
-                in_=history_banks(c)[g][:].rearrange("p (k i u e) -> p k u i e", k=BLOCKS, u=2, e=2),
-            )
+            for g in groups:
+                turn_into_sum(sums[g], g, pages[c % PAGE_TILES], False)
+                copies[g](
+                    out=z_turned[a][g][:, :, :, 32 * quarter : 32 * quarter + 32, :],
+                    in_=sums[g][:].rearrange("p (k i u e) -> p k u i e", k=BLOCKS, u=2, e=2),
+                )
 
-        z_w = [keep.tile([P, T2], U32, name=f"z_w{a}", align_bytes=64) for a in range(PASSES)]
-        z_sc = [keep.tile([P, T2], U8, name=f"z_sc{a}", align_bytes=64) for a in range(PASSES)]
-
-        def quantize_z(a, g, pair, copies):
+        def turn_back(a, g, pair, copies):
             words = z_turned[a][g][:].rearrange("p k u r e -> p (k u r e)").bitcast(F32)
-            grouped = ring3.tile([P, BANK, 2], F32, name="z_grouped", align_bytes=64)
+            grouped = ring4.tile([P, BANK, 2], F32, name="z_grouped", align_bytes=64)
             for j in range(2):
                 for u in range(2):
                     for kk in range(2):
@@ -246,9 +258,17 @@ def tile_list_lag_rewind_features_kernel(
                     out=grouped[:, j * BANK // 2 : (j + 1) * BANK // 2, :],
                     in_=pair[j][:].rearrange("p (u n) -> p n u", u=2),
                 )
-            cols = slice(g * BANK, (g + 1) * BANK)
+            return grouped
+
+        z_w, z_sc = {}, {}
+
+        def quantize_z(a, g, grouped):
+            z_w[a, g] = shared.tile(
+                [P, BANK], U32, name=f"z_w{a}_{g}", align_bytes=64, offset=Z_CODES_AT[a][g]
+            )
+            z_sc[a, g] = keep.tile([P, BANK], U8, name=f"z_sc{a}_{g}", align_bytes=64)
             nc.vector.quantize_mx(
-                out=z_w[a][:, cols].bitcast(FP8X4), scales=z_sc[a][:, cols],
+                out=z_w[a, g][:].bitcast(FP8X4), scales=z_sc[a, g][:],
                 in_=grouped[:].rearrange("p n u -> p (n u)").bitcast(BF16),
             )
 
@@ -266,78 +286,133 @@ def tile_list_lag_rewind_features_kernel(
             with nc.allow_non_contiguous_dma(reason="one value of lam for each partition and row tile"):
                 nc.sync.dma_start(out=lam_sb[:], in_=lam.rearrange("(i p) -> p i", p=P))
             for i in range(N // P):
-                rows = ring4.tile([P, M], F32, name="snap_sb", tag="quarter")
+                rows = shared.tile([P, M], F32, name=f"snap_sb{i}", offset=RAW_AT + 4 * M * i)
                 nc.sync.dma_start(out=rows[:], in_=snap[i * P : (i + 1) * P, :])
                 snap_sb.append(rows)
 
+        on_scalar = [nc.scalar.copy] * GROUPS
+
+        for k in range(VECTOR_CHUNKS):
+            quantize_w1(k)
+        values = ring4.tile([P, S], F32, name="values", tag="listed")
+        for hf, runs in enumerate(([(0, QUARTER), (QUARTER, BANK)], [(BANK, S)])):
+            spread(0, hf)
+            make_gains(0, runs)
+            motion(0, hf * BANK, (hf + 1) * BANK, motion_banks[hf])
+            for lo, hi in runs:
+                apply_gains(0, lo, hi, motion_banks[hf][:, lo % BANK : lo % BANK + hi - lo], values[:, lo:hi])
+                scatter(0, lo, hi, values[:, lo:hi])
+        quantize_w1(2)
+        quantize_w1(3)
+        whole_page(1, sum_banks[0:2])
+        whole_page(2, motion_banks)
+        preload_second_stage()
+
+        def make_values(c, a_banks):
+            if c < LAST:
+                pieces = [(0, S, ring4.tile([P, S], F32, name="values", tag="listed"))]
+            else:
+                pieces = [
+                    (lo, hi, shared.tile([P, hi - lo], F32, name=f"last_values{lo}", offset=at))
+                    for (lo, hi), at in zip(((0, S - QUARTER), (S - QUARTER, S)), LAST_VALUES_AT)
+                ]
+            for hf, (first, stop) in enumerate(halves):
+                motion(c, first, stop, a_banks[hf])
+                for lo, hi, values in pieces:
+                    a, b = max(lo, first), min(hi, stop)
+                    if a < b:
+                        apply_gains(c, a, b, a_banks[hf][:, a - first : b - first], values[:, a - lo : b - lo])
+            return pieces
+
+        def page_gains(c):
+            for hf in range(2):
+                spread(c, hf)
+            make_gains(c, halves)
+
+        def history_sums(c, groups):
+            sums = product_banks if c == LAST - 2 else sum_banks
+            open_sums(c, sums, groups)
+            close_sums(c, sums, groups, on_scalar)
+
         slots = []
-        quantize_w1(0)
-        damping(0)
-        motion(0)
-        damping(1)
-        motion(1)
-        damp_motion(0, 0, FIRST_PIECE)
-        scatter_page(0, 0, FIRST_PIECE)
-        damp_motion(0, FIRST_PIECE, BANK)
-        quantize_w1(1)
-        damping(2)
-        for c in range(PAGES):
-            if c + 2 < PAGES:
-                load_hist(c + 2)
-            if c == 2:
-                preload_second_stage()
-            damp_motion(c + 1, 0, BANK)
-            scatter_page(c, FIRST_PIECE if c == 0 else 0, S)
-            if c == 0:
-                for k in range(EARLY_CHUNKS, H // W1_CHUNK):
-                    quantize_w1(k)
+        first_pass = []
+        for c in range(LAST):
+            ahead = c + AHEAD
+            if ahead == LAST:
+                for g, pair in enumerate(TURN_PAIRS):
+                    first_pass.append(turn_back(0, g, banks[pair : pair + 2], on_scalar))
                 for i, offset in enumerate(SLOTS_AT):
                     slots.append(shared.tile([P, T2], F32, name=f"slots{i}", offset=offset))
                     nc.gpsimd.memset(slots[i][:], 0.0)
-            if c + 2 <= PAGES:
-                motion(c + 2)
-            if c >= 1:
-                for g in range(GROUPS):
-                    turn_into_sum(c - 1, g, hist_sb[c - 1], True)
-                    close_sum(c - 1, g, nc.scalar.copy)
-            if c + 3 <= PAGES:
-                damping(c + 3)
-            if c >= PAGES_PER_PASS:
-                quantize_z(0, c - PAGES_PER_PASS, turn_banks, (nc.scalar.copy, nc.scalar.copy))
+            if ahead < PAGES:
+                page_gains(ahead)
+            split = GROUPS // 2 if ahead < LAST else 0
+            history_sums(c, range(split))
+            if ahead < PAGES:
+                pieces = make_values(ahead, motion_banks)
+            history_sums(c, range(split, GROUPS))
+            if c + PAGES_PER_PASS < PAGES:
+                load_hist(c + PAGES_PER_PASS)
+            if ahead < PAGES:
+                lo, hi, values = pieces[0]
+                scatter(ahead, lo, hi, values[:])
 
-        for g in range(GROUPS):
-            turn_into_sum(PAGES - 1, g, hist_sb[PAGES - 1], True)
-        for g in range(GROUPS):
-            close_sum(PAGES - 1, g, (nc.scalar.copy, nc.vector.tensor_copy)[g % 2])
+        y_sb = [ring4.tile([P, T2], F32, name="y_sb", tag="rows") for i in range(2)]
+        last_sum = ring4.tile([P, T2], BF16, name="last_sum", tag="rows")
+        y_sb.extend(ring4.tile([P, T2], F32, name="y_sb", tag="rows") for i in range(2))
+        y_banks = [banks[4:6] + banks[2:4]] + [banks[2:4] * 2] * 3
 
-        y_banks = motion_banks[1] + spread_banks
-        y_sb = [ring4.tile([P, T2], F32, name="y_sb", tag="rows") for i in range(N // P)]
-
-        def product_pass(i, g, a):
-            cols = slice(g * BANK, (g + 1) * BANK)
+        def product_pass(i, g, a, opens):
             nc.tensor.matmul_mx(
-                out=y_banks[g][:],
+                out=y_banks[i][g][:],
                 lhsT=w3_w[:, a, i * P : (i + 1) * P].bitcast(FP8X4),
                 lhsT_scale=w3_sc[:, a, i * P : (i + 1) * P],
-                rhs=z_w[a][:, cols].bitcast(FP8X4), rhs_scale=z_sc[a][:, cols],
-                start=(a == 0), stop=(a == PASSES - 1),
+                rhs=z_w[a, g][:].bitcast(FP8X4), rhs_scale=z_sc[a, g][:],
+                start=opens, stop=not opens,
             )
 
         def leave_bank(i, g):
             nc.scalar.activation(
-                y_sb[i][:, g * BANK : (g + 1) * BANK], y_banks[g][:], ACT.Copy, scale=lam_sb[:, i : i + 1]
+                y_sb[i][:, g * BANK : (g + 1) * BANK], y_banks[i][g][:], ACT.Copy, scale=lam_sb[:, i : i + 1]
             )
 
-        free_groups = len(motion_banks[1])
-        turn_pairs = (turn_banks, spread_banks, motion_banks[0])
-        for g in range(free_groups):
-            product_pass(0, g, 0)
+        def first_pass_of_y(g):
+            quantize_z(0, g, first_pass[g])
+            product_pass(0, g, 0, True)
+
+        def add_last_page(g):
+            ticks = slice(g * BANK, (g + 1) * BANK)
+            nc.vector.tensor_tensor(
+                last_sum[:, ticks].rearrange("p (j n e) -> p j n e", j=2, e=2),
+                pages[LAST % PAGE_TILES][:, ticks].rearrange("p (j e n) -> p j n e", j=2, e=2),
+                hist_sb[LAST][:, ticks].rearrange("p (j e n) -> p j n e", j=2, e=2),
+                ALU.add,
+            )
+            words = last_sum[:, ticks].bitcast(F32)
+            bank = banks[6 + g % 2]
+            for j in range(2):
+                nc.tensor.transpose(bank[:, j * P : (j + 1) * P], words[:, j * P : (j + 1) * P], ident[:])
+            for j in range(2):
+                nc.scalar.copy(
+                    out=z_turned[1][g][:, 2 * j : 2 * j + 2, :, 96:128, :],
+                    in_=bank[:, j * P : (j + 1) * P].bitcast(BF16).rearrange("p (i u c e) -> p e u i c", u=2, c=2, e=2),
+                )
+
+        for g in range(GROUPS // 2):
+            first_pass_of_y(g)
+        lo, hi, values = pieces[1]
+        scatter(LAST, lo, hi, values[:])
         for g in range(GROUPS):
-            quantize_z(1, g, turn_pairs[g % len(turn_pairs)], (nc.vector.tensor_copy, nc.scalar.copy))
+            add_last_page(g)
+        for g in range(GROUPS // 2, GROUPS):
+            quantize_z(0, g, first_pass[g])
         for g in range(GROUPS):
-            if g >= free_groups:
-                product_pass(0, g, 0)
-            product_pass(0, g, 1)
+            pair = (banks[0:2], banks[2:4], banks[6:8], banks[0:2])[g]
+            copies = [(nc.vector.tensor_copy, nc.scalar.copy)[e] for e in TURN_COPIES[g]]
+            quantize_z(1, g, turn_back(1, g, pair, copies))
+            if g >= GROUPS // 2:
+                product_pass(0, g, 0, True)
+            product_pass(0, g, 1, False)
             leave_bank(0, g)
 
         idx3, idx4 = late_lists
@@ -345,9 +420,9 @@ def tile_list_lag_rewind_features_kernel(
             if i + 1 < N // P:
                 for g in range(GROUPS):
                     for a in range(PASSES):
-                        product_pass(i + 1, g, a)
+                        product_pass(i + 1, g, a, a == 0)
                     leave_bank(i + 1, g)
-            x = ring2.tile([P, M], F32, name="x", tag="listed")
+            x = ring4.tile([P, M], F32, name="x", tag="listed")
             nc.vector.tensor_tensor(x[:], y_sb[i][:].indirect(idx3[:]), snap_sb[i][:], ALU.add)
             nc.vector.tensor_tensor(slots[i % 2][:].indirect(idx4[:]), x[:], wgo_sb[:], ALU.mult)
             for hf in range(2):

@@ -30,19 +30,26 @@ GROUPS = T2 // BANK
 BLOCKS = BANK // P
 PAGE_TILES = 3
 AHEAD = 3
-VECTOR_PAGES = 2
+VECTOR_PAGES = (0, 1)
 W1_CHUNKS = ((0, 128), (128, 256), (256, 512), (512, 1024))
 TURN_PAIRS = (0, 2, 4, 6)
 VECTOR_CHUNKS = 2
 TURN_COPIES = ((0, 1), (0, 1), (0, 1), (0, 1))
+LAST_CHUNK_BEFORE = 2
+TURNS_BEFORE = 4
+LAST_TURN_PAIRS = (0, 2, 0, 2)
+FIRST_PASS_AT = 2
+Y_BANKS = (6, 7, 4, 5)
+ADD_BANKS = (6, 7, 6, 7)
+Y_ON_VECTOR = (3,)
 KIB = 1024
-Z_CODES_AT = ((0, 2 * KIB, 4 * KIB, 6 * KIB), (8 * KIB, 10 * KIB, 12 * KIB, 14 * KIB))
+WGS_AT = 60 * KIB
+Z_CODES_AT = ((60 * KIB, 62 * KIB, 4 * KIB, 6 * KIB), (8 * KIB, 10 * KIB, 12 * KIB, 14 * KIB))
 TABLE_AT = 0
-LAST_VALUES_AT = (0, 5 * KIB + 512)
+LAST_VALUES_AT = (4 * KIB,)
 TABLE_SCALES_AT = 16 * KIB
 SLOTS_AT = (20 * KIB, 28 * KIB)
-GAINS_AT = (26 * KIB, 36 * KIB, 56 * KIB)
-SQUARE_ON_GPSIMD = ((3, 0), (4, 0), (5, 0), (6, 0))
+GAINS_AT = (36 * KIB, 26 * KIB, 56 * KIB)
 ROUNDED_AT = (30 * KIB, 31 * KIB, 32 * KIB, 20 * KIB)
 RAW_AT = 40 * KIB
 
@@ -102,10 +109,10 @@ def tile_list_lag_rewind_features_kernel(
         load_scale_rows(w2_sc, lambda q: w2_scales[0, 4 * q : 4 * q + 4, :])
         for k in range(VECTOR_CHUNKS):
             load_w1(k)
-        wgs_sb = [keep.tile([P, BANK], F32, name=f"wgs_sb{hf}") for hf in range(2)]
-        nc.sync.dma_start(out=wgs_sb[0][:], in_=wgs[:, half_of(0)])
+        wgs_sb = shared.tile([P, S], F32, name="wgs_sb", offset=WGS_AT)
+        nc.sync.dma_start(out=wgs_sb[:, half_of(0)], in_=wgs[:, half_of(0)])
         idx2 = load_list("idx2", offs2)
-        nc.sync.dma_start(out=wgs_sb[1][:], in_=wgs[:, half_of(1)])
+        nc.sync.dma_start(out=wgs_sb[:, half_of(1)], in_=wgs[:, half_of(1)])
         for k in range(VECTOR_CHUNKS, len(W1_CHUNKS)):
             load_w1(k)
 
@@ -119,8 +126,9 @@ def tile_list_lag_rewind_features_kernel(
         nc.gpsimd.memset(w3_sc[:].rearrange("p a n -> p (a n)").bitcast(I32), 0)
 
         pages = [keep.tile([P, T2], F32, name=f"page{i}") for i in range(PAGE_TILES)]
-        for page in pages:
+        for page in pages[:-1]:
             nc.vector.memset(page[:], 0.0)
+        nc.gpsimd.memset(pages[-1][:], 0.0)
 
         hist_sb = []
 
@@ -187,37 +195,27 @@ def tile_list_lag_rewind_features_kernel(
             for lo, hi in runs:
                 nc.scalar.activation(gains[c][:, lo:hi], gains[c][:, lo:hi], ACT.Abs_reciprocal_sqrt, bias=half[:])
             for lo, hi in runs:
-                if (c, lo // BANK) in SQUARE_ON_GPSIMD:
-                    nc.gpsimd.tensor_tensor(gains[c][:, lo:hi], gains[c][:, lo:hi], gains[c][:, lo:hi], ALU.mult)
-                else:
-                    nc.scalar.activation(gains[c][:, lo:hi], gains[c][:, lo:hi], ACT.Square)
-            for lo, hi in runs:
-                nc.gpsimd.tensor_tensor(
-                    gains[c][:, lo:hi], gains[c][:, lo:hi],
-                    wgs_sb[lo // BANK][:, lo % BANK : lo % BANK + hi - lo], ALU.mult,
-                )
+                nc.scalar.activation(gains[c][:, lo:hi], gains[c][:, lo:hi], ACT.Square)
+            damping = gains[c]
+            if AHEAD <= c < LAST:
+                gains[c] = shared.tile([P, S], F32, name=f"gains_moved{c}", offset=ROUNDED_AT[-1])
+            for lo, hi in runs if c == 0 else [(0, S)] if c < LAST else []:
+                nc.gpsimd.tensor_tensor(gains[c][:, lo:hi], damping[:, lo:hi], wgs_sb[:, lo:hi], ALU.mult)
 
         def apply_gains(c, lo, hi, sums, values):
-            if c < VECTOR_PAGES:
+            if c in VECTOR_PAGES:
                 nc.vector.tensor_tensor(values, sums, gains[c][:, lo:hi], ALU.mult)
             else:
                 nc.scalar.copy(out=values, in_=sums)
-                nc.gpsimd.tensor_tensor(values, values, gains[c][:, lo:hi], ALU.mult)
 
         def scatter(c, lo, hi, values):
-            nc.vector.tensor_copy(pages[c % PAGE_TILES][:].indirect(entries(idx2, lo, hi)), values)
+            window = pages[c % PAGE_TILES][:].indirect(entries(idx2, lo, hi))
+            if c < LAST:
+                nc.vector.tensor_copy(window, values)
+            else:
+                nc.vector.tensor_tensor(window, values, wgs_sb[:, lo:hi], ALU.mult)
 
         halves = [(0, BANK), (BANK, S)]
-
-        def whole_page(c, a_banks):
-            for hf in range(2):
-                spread(c, hf)
-            make_gains(c, halves)
-            values = ring4.tile([P, S], F32, name="values", tag="listed")
-            for hf, (lo, hi) in enumerate(halves):
-                motion(c, lo, hi, a_banks[hf])
-                apply_gains(c, lo, hi, a_banks[hf][:], values[:, lo:hi])
-            scatter(c, 0, S, values[:])
 
         z_turned = [
             [keep.tile([P, BLOCKS, 2, P, 2], BF16, name=f"z_turned{a}_{g}") for g in range(GROUPS)]
@@ -303,10 +301,6 @@ def tile_list_lag_rewind_features_kernel(
                 apply_gains(0, lo, hi, motion_banks[hf][:, lo % BANK : lo % BANK + hi - lo], values[:, lo:hi])
                 scatter(0, lo, hi, values[:, lo:hi])
         quantize_w1(2)
-        quantize_w1(3)
-        whole_page(1, sum_banks[0:2])
-        whole_page(2, motion_banks)
-        preload_second_stage()
 
         def make_values(c, a_banks):
             if c < LAST:
@@ -314,7 +308,7 @@ def tile_list_lag_rewind_features_kernel(
             else:
                 pieces = [
                     (lo, hi, shared.tile([P, hi - lo], F32, name=f"last_values{lo}", offset=at))
-                    for (lo, hi), at in zip(((0, S - QUARTER), (S - QUARTER, S)), LAST_VALUES_AT)
+                    for (lo, hi), at in zip(((0, S),), LAST_VALUES_AT)
                 ]
             for hf, (first, stop) in enumerate(halves):
                 motion(c, first, stop, a_banks[hf])
@@ -322,6 +316,9 @@ def tile_list_lag_rewind_features_kernel(
                     a, b = max(lo, first), min(hi, stop)
                     if a < b:
                         apply_gains(c, a, b, a_banks[hf][:, a - first : b - first], values[:, a - lo : b - lo])
+            if c not in VECTOR_PAGES:
+                for lo, hi, values in pieces:
+                    nc.gpsimd.tensor_tensor(values[:], values[:], gains[c][:, lo:hi], ALU.mult)
             return pieces
 
         def page_gains(c):
@@ -334,33 +331,44 @@ def tile_list_lag_rewind_features_kernel(
             open_sums(c, sums, groups)
             close_sums(c, sums, groups, on_scalar)
 
+        for c, a_banks in ((1, sum_banks[0:2]), (2, motion_banks)):
+            page_gains(c)
+            if c == LAST_CHUNK_BEFORE:
+                quantize_w1(3)
+            scatter(c, 0, S, make_values(c, a_banks)[0][2][:])
+        preload_second_stage()
+
         slots = []
         first_pass = []
         for c in range(LAST):
             ahead = c + AHEAD
             if ahead == LAST:
-                for g, pair in enumerate(TURN_PAIRS):
+                for g, pair in enumerate(TURN_PAIRS[:TURNS_BEFORE]):
                     first_pass.append(turn_back(0, g, banks[pair : pair + 2], on_scalar))
-                for i, offset in enumerate(SLOTS_AT):
-                    slots.append(shared.tile([P, T2], F32, name=f"slots{i}", offset=offset))
-                    nc.gpsimd.memset(slots[i][:], 0.0)
             if ahead < PAGES:
                 page_gains(ahead)
             split = GROUPS // 2 if ahead < LAST else 0
             history_sums(c, range(split))
             if ahead < PAGES:
                 pieces = make_values(ahead, motion_banks)
+            if ahead == LAST:
+                for pair in TURN_PAIRS[TURNS_BEFORE:]:
+                    first_pass.append(turn_back(0, len(first_pass), banks[pair : pair + 2], on_scalar))
             history_sums(c, range(split, GROUPS))
             if c + PAGES_PER_PASS < PAGES:
                 load_hist(c + PAGES_PER_PASS)
-            if ahead < PAGES:
+            if ahead < LAST:
                 lo, hi, values = pieces[0]
                 scatter(ahead, lo, hi, values[:])
+
+        for i, offset in enumerate(SLOTS_AT):
+            slots.append(shared.tile([P, T2], F32, name=f"slots{i}", offset=offset))
+            nc.gpsimd.memset(slots[i][:], 0.0)
 
         y_sb = [ring4.tile([P, T2], F32, name="y_sb", tag="rows") for i in range(2)]
         last_sum = ring4.tile([P, T2], BF16, name="last_sum", tag="rows")
         y_sb.extend(ring4.tile([P, T2], F32, name="y_sb", tag="rows") for i in range(2))
-        y_banks = [banks[4:6] + banks[2:4]] + [banks[2:4] * 2] * 3
+        y_banks = [[banks[b] for b in Y_BANKS]] + [[banks[b] for b in Y_BANKS[2:]] * 2] * 3
 
         def product_pass(i, g, a, opens):
             nc.tensor.matmul_mx(
@@ -372,9 +380,11 @@ def tile_list_lag_rewind_features_kernel(
             )
 
         def leave_bank(i, g):
-            nc.scalar.activation(
-                y_sb[i][:, g * BANK : (g + 1) * BANK], y_banks[i][g][:], ACT.Copy, scale=lam_sb[:, i : i + 1]
-            )
+            cols = slice(g * BANK, (g + 1) * BANK)
+            if i == 0 and g in Y_ON_VECTOR:
+                nc.vector.tensor_scalar(y_sb[i][:, cols], y_banks[i][g][:], lam_sb[:, i : i + 1], None, ALU.mult)
+            else:
+                nc.scalar.activation(y_sb[i][:, cols], y_banks[i][g][:], ACT.Copy, scale=lam_sb[:, i : i + 1])
 
         def first_pass_of_y(g):
             quantize_z(0, g, first_pass[g])
@@ -389,7 +399,7 @@ def tile_list_lag_rewind_features_kernel(
                 ALU.add,
             )
             words = last_sum[:, ticks].bitcast(F32)
-            bank = banks[6 + g % 2]
+            bank = banks[ADD_BANKS[g]]
             for j in range(2):
                 nc.tensor.transpose(bank[:, j * P : (j + 1) * P], words[:, j * P : (j + 1) * P], ident[:])
             for j in range(2):
@@ -398,20 +408,21 @@ def tile_list_lag_rewind_features_kernel(
                     in_=bank[:, j * P : (j + 1) * P].bitcast(BF16).rearrange("p (i u c e) -> p e u i c", u=2, c=2, e=2),
                 )
 
-        for g in range(GROUPS // 2):
+        scatter(LAST, 0, S, pieces[0][2][:])
+        for g in range(GROUPS // 2, GROUPS):
             first_pass_of_y(g)
-        lo, hi, values = pieces[1]
-        scatter(LAST, lo, hi, values[:])
         for g in range(GROUPS):
             add_last_page(g)
-        for g in range(GROUPS // 2, GROUPS):
+        for g in range(GROUPS // 2):
             quantize_z(0, g, first_pass[g])
         for g in range(GROUPS):
-            pair = (banks[0:2], banks[2:4], banks[6:8], banks[0:2])[g]
+            pair = banks[LAST_TURN_PAIRS[g] : LAST_TURN_PAIRS[g] + 2]
             copies = [(nc.vector.tensor_copy, nc.scalar.copy)[e] for e in TURN_COPIES[g]]
+            if g == FIRST_PASS_AT:
+                product_pass(0, 0, 0, True)
+                product_pass(0, 1, 0, True)
             quantize_z(1, g, turn_back(1, g, pair, copies))
-            if g >= GROUPS // 2:
-                product_pass(0, g, 0, True)
+        for g in range(GROUPS):
             product_pass(0, g, 1, False)
             leave_bank(0, g)
 

@@ -122,6 +122,8 @@ def tile_list_lag_rewind_features_kernel(
         nc.scalar.activation(warm[:], half[:], ACT.Abs_reciprocal_sqrt)
         ident = keep.tile([P, P], F32, name="ident")
         make_identity(nc, ident[:])
+        ident16 = keep.tile([P, P], BF16, name="ident16")
+        make_identity(nc, ident16[:])
         w3_sc = keep.tile([P, PASSES, N], U8, name="w3_sc", align_bytes=64)
         nc.gpsimd.memset(w3_sc[:].rearrange("p a n -> p (a n)").bitcast(I32), 0)
 
@@ -392,21 +394,16 @@ def tile_list_lag_rewind_features_kernel(
 
         def add_last_page(g):
             ticks = slice(g * BANK, (g + 1) * BANK)
-            nc.vector.tensor_tensor(
-                last_sum[:, ticks].rearrange("p (j n e) -> p j n e", j=2, e=2),
-                pages[LAST % PAGE_TILES][:, ticks].rearrange("p (j e n) -> p j n e", j=2, e=2),
-                hist_sb[LAST][:, ticks].rearrange("p (j e n) -> p j n e", j=2, e=2),
-                ALU.add,
-            )
-            words = last_sum[:, ticks].bitcast(F32)
+            nc.vector.tensor_tensor(last_sum[:, ticks], pages[LAST % PAGE_TILES][:, ticks], hist_sb[LAST][:, ticks], ALU.add)
             bank = banks[ADD_BANKS[g]]
-            for j in range(2):
-                nc.tensor.transpose(bank[:, j * P : (j + 1) * P], words[:, j * P : (j + 1) * P], ident[:])
-            for j in range(2):
-                nc.scalar.copy(
-                    out=z_turned[1][g][:, 2 * j : 2 * j + 2, :, 96:128, :],
-                    in_=bank[:, j * P : (j + 1) * P].bitcast(BF16).rearrange("p (i u c e) -> p e u i c", u=2, c=2, e=2),
-                )
+            for k in range(BLOCKS):
+                tick = g * BANK + k * P
+                nc.tensor.transpose(bank[:].bitcast(BF16)[:, k * P : (k + 1) * P], last_sum[:, tick : tick + P], ident16[:])
+            words = z_turned[1][g][:].rearrange("p k u r e -> p (k u r e)").bitcast(F32)
+            nc.scalar.copy(
+                out=words.rearrange("p (k u r) -> p k u r", k=BLOCKS, u=2)[:, :, :, 96:128],
+                in_=bank[:, : BANK // 2].rearrange("p (k i u) -> p k u i", k=BLOCKS, u=2),
+            )
 
         scatter(LAST, 0, S, pieces[0][2][:])
         for g in range(GROUPS // 2, GROUPS):

@@ -32,25 +32,24 @@ PAGE_TILES = 3
 AHEAD = 3
 VECTOR_PAGES = (0, 1)
 W1_CHUNKS = ((0, 128), (128, 256), (256, 512), (512, 1024))
-TURN_PAIRS = (0, 2, 4, 6)
+TURN_PAIRS = (4, 6, 0, 2)
 VECTOR_CHUNKS = 2
 TURN_COPIES = ((0, 1), (0, 1), (0, 1), (0, 1))
 LAST_CHUNK_BEFORE = 2
-TURNS_BEFORE = 4
+TURNS_BEFORE = 2
 LAST_TURN_PAIRS = (0, 2, 0, 2)
 FIRST_PASS_AT = 2
 Y_BANKS = (6, 7, 4, 5)
 ADD_BANKS = (6, 7, 6, 7)
 Y_ON_VECTOR = (3,)
 KIB = 1024
-WGS_AT = 60 * KIB
-Z_CODES_AT = ((60 * KIB, 62 * KIB, 4 * KIB, 6 * KIB), (8 * KIB, 10 * KIB, 12 * KIB, 14 * KIB))
+WGS_AT = 56 * KIB
+Z_CODES_AT = ((56 * KIB, 58 * KIB, 4 * KIB, 6 * KIB), (8 * KIB, 10 * KIB, 12 * KIB, 14 * KIB))
 TABLE_AT = 0
 LAST_VALUES_AT = (4 * KIB,)
 TABLE_SCALES_AT = 16 * KIB
-SLOTS_AT = (20 * KIB, 28 * KIB)
-GAINS_AT = (36 * KIB, 26 * KIB, 56 * KIB)
-ROUNDED_AT = (30 * KIB, 31 * KIB, 32 * KIB, 20 * KIB)
+GAINS_AT = (24 * KIB, 28 * KIB, 36 * KIB)
+ROUNDED_AT = (32 * KIB, 33 * KIB, 34 * KIB, 20 * KIB)
 RAW_AT = 40 * KIB
 
 
@@ -131,6 +130,9 @@ def tile_list_lag_rewind_features_kernel(
         for page in pages[:-1]:
             nc.vector.memset(page[:], 0.0)
         nc.gpsimd.memset(pages[-1][:], 0.0)
+        slots = [keep.tile([P, T2], F32, name=f"slots{i}") for i in range(2)]
+        for tile in slots:
+            nc.gpsimd.memset(tile[:], 0.0)
 
         hist_sb = []
 
@@ -340,7 +342,6 @@ def tile_list_lag_rewind_features_kernel(
             scatter(c, 0, S, make_values(c, a_banks)[0][2][:])
         preload_second_stage()
 
-        slots = []
         first_pass = []
         for c in range(LAST):
             ahead = c + AHEAD
@@ -362,10 +363,6 @@ def tile_list_lag_rewind_features_kernel(
             if ahead < LAST:
                 lo, hi, values = pieces[0]
                 scatter(ahead, lo, hi, values[:])
-
-        for i, offset in enumerate(SLOTS_AT):
-            slots.append(shared.tile([P, T2], F32, name=f"slots{i}", offset=offset))
-            nc.gpsimd.memset(slots[i][:], 0.0)
 
         y_sb = [ring4.tile([P, T2], F32, name="y_sb", tag="rows") for i in range(2)]
         last_sum = ring4.tile([P, T2], BF16, name="last_sum", tag="rows")

@@ -39,12 +39,13 @@ LAST_CHUNK_BEFORE = 2
 TURNS_BEFORE = 2
 LAST_TURN_PAIRS = (0, 2, 0, 2)
 FIRST_PASS_AT = 2
-Y_BANKS = (6, 7, 4, 5)
+Y_BANKS = (4, 5, 6, 7)
 ADD_BANKS = (6, 7, 6, 7)
 Y_ON_VECTOR = (3,)
 KIB = 1024
+PAGES_AT = 60 * KIB
 WGS_AT = 56 * KIB
-Z_CODES_AT = ((56 * KIB, 58 * KIB, 4 * KIB, 6 * KIB), (8 * KIB, 10 * KIB, 12 * KIB, 14 * KIB))
+Z_CODES_AT = ((4 * KIB, 6 * KIB, 68 * KIB, 70 * KIB), (8 * KIB, 10 * KIB, 12 * KIB, 14 * KIB))
 TABLE_AT = 0
 LAST_VALUES_AT = (4 * KIB,)
 TABLE_SCALES_AT = 16 * KIB
@@ -121,12 +122,10 @@ def tile_list_lag_rewind_features_kernel(
         nc.scalar.activation(warm[:], half[:], ACT.Abs_reciprocal_sqrt)
         ident = keep.tile([P, P], F32, name="ident")
         make_identity(nc, ident[:])
-        ident16 = keep.tile([P, P], BF16, name="ident16")
-        make_identity(nc, ident16[:])
         w3_sc = keep.tile([P, PASSES, N], U8, name="w3_sc", align_bytes=64)
         nc.gpsimd.memset(w3_sc[:].rearrange("p a n -> p (a n)").bitcast(I32), 0)
 
-        pages = [keep.tile([P, T2], F32, name=f"page{i}") for i in range(PAGE_TILES)]
+        pages = [shared.tile([P, T2], F32, name=f"page{i}", offset=PAGES_AT + 4 * T2 * i) for i in range(PAGE_TILES)]
         for page in pages[:-1]:
             nc.vector.memset(page[:], 0.0)
         nc.gpsimd.memset(pages[-1][:], 0.0)
@@ -391,30 +390,35 @@ def tile_list_lag_rewind_features_kernel(
 
         def add_last_page(g):
             ticks = slice(g * BANK, (g + 1) * BANK)
-            nc.vector.tensor_tensor(last_sum[:, ticks], pages[LAST % PAGE_TILES][:, ticks], hist_sb[LAST][:, ticks], ALU.add)
-            bank = banks[ADD_BANKS[g]]
-            for k in range(BLOCKS):
-                tick = g * BANK + k * P
-                nc.tensor.transpose(bank[:].bitcast(BF16)[:, k * P : (k + 1) * P], last_sum[:, tick : tick + P], ident16[:])
-            words = z_turned[1][g][:].rearrange("p k u r e -> p (k u r e)").bitcast(F32)
-            nc.scalar.copy(
-                out=words.rearrange("p (k u r) -> p k u r", k=BLOCKS, u=2)[:, :, :, 96:128],
-                in_=bank[:, : BANK // 2].rearrange("p (k i u) -> p k u i", k=BLOCKS, u=2),
+            nc.vector.tensor_tensor(
+                last_sum[:, ticks].rearrange("p (j n e) -> p j n e", j=2, e=2),
+                pages[LAST % PAGE_TILES][:, ticks].rearrange("p (j e n) -> p j n e", j=2, e=2),
+                hist_sb[LAST][:, ticks].rearrange("p (j e n) -> p j n e", j=2, e=2),
+                ALU.add,
             )
+            words = last_sum[:, ticks].bitcast(F32)
+            bank = banks[ADD_BANKS[g]]
+            for j in range(2):
+                nc.tensor.transpose(bank[:, j * P : (j + 1) * P], words[:, j * P : (j + 1) * P], ident[:])
+            for j in range(2):
+                nc.scalar.copy(
+                    out=z_turned[1][g][:, 2 * j : 2 * j + 2, :, 96:128, :],
+                    in_=bank[:, j * P : (j + 1) * P].bitcast(BF16).rearrange("p (i u c e) -> p e u i c", u=2, c=2, e=2),
+                )
 
         scatter(LAST, 0, S, pieces[0][2][:])
-        for g in range(GROUPS // 2, GROUPS):
+        for g in range(GROUPS // 2):
             first_pass_of_y(g)
         for g in range(GROUPS):
             add_last_page(g)
-        for g in range(GROUPS // 2):
+        for g in range(GROUPS // 2, GROUPS):
             quantize_z(0, g, first_pass[g])
         for g in range(GROUPS):
             pair = banks[LAST_TURN_PAIRS[g] : LAST_TURN_PAIRS[g] + 2]
             copies = [(nc.vector.tensor_copy, nc.scalar.copy)[e] for e in TURN_COPIES[g]]
             if g == FIRST_PASS_AT:
-                product_pass(0, 0, 0, True)
-                product_pass(0, 1, 0, True)
+                product_pass(0, 2, 0, True)
+                product_pass(0, 3, 0, True)
             quantize_z(1, g, turn_back(1, g, pair, copies))
         for g in range(GROUPS):
             product_pass(0, g, 1, False)

@@ -44,13 +44,13 @@ ADD_BANKS = (6, 7, 6, 7)
 Y_ON_VECTOR = (3,)
 KIB = 1024
 PAGES_AT = 60 * KIB
-WGS_AT = 56 * KIB
 Z_CODES_AT = ((4 * KIB, 6 * KIB, 68 * KIB, 70 * KIB), (8 * KIB, 10 * KIB, 12 * KIB, 14 * KIB))
 TABLE_AT = 0
 LAST_VALUES_AT = (4 * KIB,)
 TABLE_SCALES_AT = 16 * KIB
-GAINS_AT = (24 * KIB, 28 * KIB, 36 * KIB)
-ROUNDED_AT = (32 * KIB, 33 * KIB, 34 * KIB, 20 * KIB)
+SLOTS_AT = (20 * KIB, 28 * KIB)
+GAINS_AT = (36 * KIB, 26 * KIB, 56 * KIB)
+ROUNDED_AT = (30 * KIB, 31 * KIB, 32 * KIB, 20 * KIB)
 RAW_AT = 40 * KIB
 
 
@@ -109,7 +109,7 @@ def tile_list_lag_rewind_features_kernel(
         load_scale_rows(w2_sc, lambda q: w2_scales[0, 4 * q : 4 * q + 4, :])
         for k in range(VECTOR_CHUNKS):
             load_w1(k)
-        wgs_sb = shared.tile([P, S], F32, name="wgs_sb", offset=WGS_AT)
+        wgs_sb = keep.tile([P, S], F32, name="wgs_sb")
         nc.sync.dma_start(out=wgs_sb[:, half_of(0)], in_=wgs[:, half_of(0)])
         idx2 = load_list("idx2", offs2)
         nc.sync.dma_start(out=wgs_sb[:, half_of(1)], in_=wgs[:, half_of(1)])
@@ -129,9 +129,6 @@ def tile_list_lag_rewind_features_kernel(
         for page in pages[:-1]:
             nc.vector.memset(page[:], 0.0)
         nc.gpsimd.memset(pages[-1][:], 0.0)
-        slots = [keep.tile([P, T2], F32, name=f"slots{i}") for i in range(2)]
-        for tile in slots:
-            nc.gpsimd.memset(tile[:], 0.0)
 
         hist_sb = []
 
@@ -188,7 +185,7 @@ def tile_list_lag_rewind_features_kernel(
                 start=True, stop=True,
             )
 
-        gains = {}
+        gains, moved = {}, {}
 
         def make_gains(c, runs):
             if c not in gains:
@@ -199,11 +196,14 @@ def tile_list_lag_rewind_features_kernel(
                 nc.scalar.activation(gains[c][:, lo:hi], gains[c][:, lo:hi], ACT.Abs_reciprocal_sqrt, bias=half[:])
             for lo, hi in runs:
                 nc.scalar.activation(gains[c][:, lo:hi], gains[c][:, lo:hi], ACT.Square)
-            damping = gains[c]
-            if AHEAD <= c < LAST:
-                gains[c] = shared.tile([P, S], F32, name=f"gains_moved{c}", offset=ROUNDED_AT[-1])
-            for lo, hi in runs if c == 0 else [(0, S)] if c < LAST else []:
-                nc.gpsimd.tensor_tensor(gains[c][:, lo:hi], damping[:, lo:hi], wgs_sb[:, lo:hi], ALU.mult)
+            if c < AHEAD:
+                for lo, hi in runs:
+                    nc.gpsimd.tensor_tensor(gains[c][:, lo:hi], gains[c][:, lo:hi], wgs_sb[:, lo:hi], ALU.mult)
+            elif c < LAST:
+                for hf, (lo, hi) in enumerate(runs):
+                    at = ROUNDED_AT[-1] + 4 * lo
+                    moved[c, hf] = shared.tile([P, BANK], F32, name=f"gains_moved{c}_{hf}", offset=at)
+                    nc.gpsimd.tensor_tensor(moved[c, hf][:], gains[c][:, lo:hi], wgs_sb[:, lo:hi], ALU.mult)
 
         def apply_gains(c, lo, hi, sums, values):
             if c in VECTOR_PAGES:
@@ -320,8 +320,10 @@ def tile_list_lag_rewind_features_kernel(
                     if a < b:
                         apply_gains(c, a, b, a_banks[hf][:, a - first : b - first], values[:, a - lo : b - lo])
             if c not in VECTOR_PAGES:
-                for lo, hi, values in pieces:
-                    nc.gpsimd.tensor_tensor(values[:], values[:], gains[c][:, lo:hi], ALU.mult)
+                values = pieces[0][2]
+                for hf, (lo, hi) in enumerate(halves):
+                    factor = moved[c, hf][:] if (c, hf) in moved else gains[c][:, lo:hi]
+                    nc.gpsimd.tensor_tensor(values[:, lo:hi], values[:, lo:hi], factor, ALU.mult)
             return pieces
 
         def page_gains(c):
@@ -362,6 +364,10 @@ def tile_list_lag_rewind_features_kernel(
             if ahead < LAST:
                 lo, hi, values = pieces[0]
                 scatter(ahead, lo, hi, values[:])
+
+        slots = [shared.tile([P, T2], F32, name=f"slots{i}", offset=at) for i, at in enumerate(SLOTS_AT)]
+        for tile in slots:
+            nc.gpsimd.memset(tile[:], 0.0)
 
         y_sb = [ring4.tile([P, T2], F32, name="y_sb", tag="rows") for i in range(2)]
         last_sum = ring4.tile([P, T2], BF16, name="last_sum", tag="rows")

@@ -31,11 +31,10 @@ BLOCKS = BANK // P
 PAGE_TILES = 3
 AHEAD = 3
 VECTOR_PAGES = (0, 1)
-W1_CHUNKS = ((0, 128), (128, 256), (256, 512), (512, 1024))
+W1_CHUNKS = ((0, 128), (128, 256), (256, 1024))
 TURN_PAIRS = (4, 6, 0, 2)
 VECTOR_CHUNKS = 2
 TURN_COPIES = ((0, 1), (0, 1), (0, 1), (0, 1))
-LAST_CHUNK_BEFORE = 2
 TURNS_BEFORE = 2
 LAST_TURN_PAIRS = (0, 2, 0, 2)
 FIRST_PASS_AT = 2
@@ -50,7 +49,9 @@ LAST_VALUES_AT = (4 * KIB,)
 TABLE_SCALES_AT = 16 * KIB
 SLOTS_AT = (20 * KIB, 28 * KIB)
 GAINS_AT = (36 * KIB, 26 * KIB, 56 * KIB)
-ROUNDED_AT = (30 * KIB, 31 * KIB, 32 * KIB, 20 * KIB)
+ROUNDED_AT = (30 * KIB, 31 * KIB, 20 * KIB)
+MOVED_AT = (32 * KIB, 34 * KIB)
+FIRST_MOVED_AT = (20 * KIB, 22 * KIB)
 RAW_AT = 40 * KIB
 
 
@@ -154,18 +155,14 @@ def tile_list_lag_rewind_features_kernel(
         def quantize_w1(k):
             lo, hi = W1_CHUNKS[k]
             rounded = shared.tile([P, hi - lo, PACK], BF16, name=f"w1_rounded{k}", align_bytes=64, offset=ROUNDED_AT[k])
-            if k < VECTOR_CHUNKS:
-                nc.vector.tensor_copy(out=rounded[:], in_=w1_raw[k][:].rearrange("p t c -> p c t"))
-            else:
-                for at in range(0, hi - lo, P):
-                    nc.gpsimd.tensor_scalar(
-                        rounded[:, at : at + P, :], w1_raw[k][:, :, at : at + P].rearrange("p t c -> p c t"),
-                        1.0, 0.0, ALU.mult, ALU.add,
-                    )
-            nc.vector.quantize_mx(
-                out=w1_w[:, lo:hi].bitcast(FP8X4), scales=w1_sc[:, lo:hi],
-                in_=rounded[:].rearrange("p c t -> p (c t)"),
-            )
+            nc.vector.tensor_copy(out=rounded[:], in_=w1_raw[k][:].rearrange("p t c -> p c t"))
+            while lo < hi:
+                stop = min(hi, max(2 * lo, P))
+                nc.vector.quantize_mx(
+                    out=w1_w[:, lo:stop].bitcast(FP8X4), scales=w1_sc[:, lo:stop],
+                    in_=rounded[:, lo - W1_CHUNKS[k][0] : stop - W1_CHUNKS[k][0], :].rearrange("p c t -> p (c t)"),
+                )
+                lo = stop
 
         def spread(c, hf):
             nc.tensor.matmul_mx(
@@ -196,24 +193,27 @@ def tile_list_lag_rewind_features_kernel(
                 nc.scalar.activation(gains[c][:, lo:hi], gains[c][:, lo:hi], ACT.Abs_reciprocal_sqrt, bias=half[:])
             for lo, hi in runs:
                 nc.scalar.activation(gains[c][:, lo:hi], gains[c][:, lo:hi], ACT.Square)
-            if c < AHEAD:
+            if c == 0:
                 for lo, hi in runs:
+                    if lo == 0:
+                        continue
                     nc.gpsimd.tensor_tensor(gains[c][:, lo:hi], gains[c][:, lo:hi], wgs_sb[:, lo:hi], ALU.mult)
             elif c < LAST:
                 for hf, (lo, hi) in enumerate(runs):
-                    at = ROUNDED_AT[-1] + 4 * lo
+                    at = MOVED_AT[hf] if c > 1 else FIRST_MOVED_AT[hf]
                     moved[c, hf] = shared.tile([P, BANK], F32, name=f"gains_moved{c}_{hf}", offset=at)
                     nc.gpsimd.tensor_tensor(moved[c, hf][:], gains[c][:, lo:hi], wgs_sb[:, lo:hi], ALU.mult)
 
         def apply_gains(c, lo, hi, sums, values):
             if c in VECTOR_PAGES:
-                nc.vector.tensor_tensor(values, sums, gains[c][:, lo:hi], ALU.mult)
+                factor = moved[c, lo // BANK][:] if c else gains[c][:, lo:hi]
+                nc.vector.tensor_tensor(values, sums, factor, ALU.mult)
             else:
                 nc.scalar.copy(out=values, in_=sums)
 
         def scatter(c, lo, hi, values):
             window = pages[c % PAGE_TILES][:].indirect(entries(idx2, lo, hi))
-            if c < LAST:
+            if c < LAST and (c, lo) != (0, 0):
                 nc.vector.tensor_copy(window, values)
             else:
                 nc.vector.tensor_tensor(window, values, wgs_sb[:, lo:hi], ALU.mult)
@@ -295,15 +295,19 @@ def tile_list_lag_rewind_features_kernel(
 
         for k in range(VECTOR_CHUNKS):
             quantize_w1(k)
-        values = ring4.tile([P, S], F32, name="values", tag="listed")
         for hf, runs in enumerate(([(0, QUARTER), (QUARTER, BANK)], [(BANK, S)])):
             spread(0, hf)
-            make_gains(0, runs)
+            make_gains(0, runs[::-1] if hf == 0 else runs)
             motion(0, hf * BANK, (hf + 1) * BANK, motion_banks[hf])
+            if hf == 0:
+                values = ring4.tile([P, BANK], F32, name="values", tag="listed")
+            else:
+                quantize_w1(2)
+                values = shared.tile([P, BANK], F32, name="values_behind_w1", offset=RAW_AT + 4 * PACK * W1_CHUNKS[2][0])
             for lo, hi in runs:
-                apply_gains(0, lo, hi, motion_banks[hf][:, lo % BANK : lo % BANK + hi - lo], values[:, lo:hi])
-                scatter(0, lo, hi, values[:, lo:hi])
-        quantize_w1(2)
+                cols = slice(lo % BANK, lo % BANK + hi - lo)
+                apply_gains(0, lo, hi, motion_banks[hf][:, cols], values[:, cols])
+                scatter(0, lo, hi, values[:, cols])
 
         def make_values(c, a_banks):
             if c < LAST:
@@ -338,8 +342,6 @@ def tile_list_lag_rewind_features_kernel(
 
         for c, a_banks in ((1, sum_banks[0:2]), (2, motion_banks)):
             page_gains(c)
-            if c == LAST_CHUNK_BEFORE:
-                quantize_w1(3)
             scatter(c, 0, S, make_values(c, a_banks)[0][2][:])
         preload_second_stage()
 

@@ -31,25 +31,25 @@ BLOCKS = BANK // P
 PAGE_TILES = 3
 AHEAD = 3
 VECTOR_PAGES = (0, 1)
-W1_CHUNKS = ((0, 128), (128, 256), (256, 1024))
+W1_CHUNKS = ((0, 128), (128, 256), (256, 512), (512, 1024))
 TURN_PAIRS = (4, 6, 0, 2)
 VECTOR_CHUNKS = 2
-TURN_COPIES = ((0, 1), (0, 1), (0, 1), (0, 1))
+TURN_COPIES = ((1, 1), (1, 1), (0, 1), (0, 1))
 TURNS_BEFORE = 2
-LAST_TURN_PAIRS = (0, 2, 0, 2)
-FIRST_PASS_AT = 2
-Y_BANKS = (4, 5, 6, 7)
+LAST_PAIRS = (0, 2, 4, 6)
+Y_BANKS = (0, 1, 2, 3)
 ADD_BANKS = (6, 7, 6, 7)
 Y_ON_VECTOR = (3,)
 KIB = 1024
+SQUARE_ON_GPSIMD = (5, 6)
 PAGES_AT = 60 * KIB
-Z_CODES_AT = ((4 * KIB, 6 * KIB, 68 * KIB, 70 * KIB), (8 * KIB, 10 * KIB, 12 * KIB, 14 * KIB))
+Z_CODES_AT = ((68 * KIB, 70 * KIB, 72 * KIB, 74 * KIB), (8 * KIB, 10 * KIB, 12 * KIB, 14 * KIB))
 TABLE_AT = 0
 LAST_VALUES_AT = (4 * KIB,)
 TABLE_SCALES_AT = 16 * KIB
 SLOTS_AT = (20 * KIB, 28 * KIB)
 GAINS_AT = (36 * KIB, 26 * KIB, 56 * KIB)
-ROUNDED_AT = (30 * KIB, 31 * KIB, 20 * KIB)
+ROUNDED_AT = (30 * KIB, 31 * KIB, 21 * KIB, 32 * KIB)
 MOVED_AT = (32 * KIB, 34 * KIB)
 FIRST_MOVED_AT = (20 * KIB, 22 * KIB)
 RAW_AT = 40 * KIB
@@ -135,7 +135,12 @@ def tile_list_lag_rewind_features_kernel(
 
         def load_hist(c):
             rows = ring4.tile([P, T2], F32, name="hist_sb", tag="rows")
-            nc.sync.dma_start(out=rows[:], in_=hist[c * P : (c + 1) * P, :])
+            if c < PAGES_PER_PASS:
+                nc.sync.dma_start(out=rows[:], in_=hist[c * P : (c + 1) * P, :])
+            else:
+                u, h = divmod(c - PAGES_PER_PASS, 2)
+                dealt = hist[H // 2 :, :].rearrange("(h i u e) t -> u h i e t", h=2, u=2, e=2)
+                nc.sync.dma_start(out=rows[:], in_=dealt[u, h])
             hist_sb.append(rows)
 
         for c in range(PAGES_PER_PASS):
@@ -155,20 +160,39 @@ def tile_list_lag_rewind_features_kernel(
         def quantize_w1(k):
             lo, hi = W1_CHUNKS[k]
             rounded = shared.tile([P, hi - lo, PACK], BF16, name=f"w1_rounded{k}", align_bytes=64, offset=ROUNDED_AT[k])
-            nc.vector.tensor_copy(out=rounded[:], in_=w1_raw[k][:].rearrange("p t c -> p c t"))
-            while lo < hi:
-                stop = min(hi, max(2 * lo, P))
-                nc.vector.quantize_mx(
-                    out=w1_w[:, lo:stop].bitcast(FP8X4), scales=w1_sc[:, lo:stop],
-                    in_=rounded[:, lo - W1_CHUNKS[k][0] : stop - W1_CHUNKS[k][0], :].rearrange("p c t -> p (c t)"),
+            if k < len(W1_CHUNKS) - 1:
+                nc.vector.tensor_copy(out=rounded[:], in_=w1_raw[k][:].rearrange("p t c -> p c t"))
+            else:
+                nc.scalar.copy(
+                    out=rounded[:].rearrange("p (u i e) t -> p u i e t", u=2, e=2),
+                    in_=w1_raw[k][:].rearrange("p t (i u e) -> p u i e t", u=2, e=2),
                 )
-                lo = stop
+            nc.vector.quantize_mx(
+                out=w1_w[:, lo:hi].bitcast(FP8X4), scales=w1_sc[:, lo:hi],
+                in_=rounded[:].rearrange("p c t -> p (c t)"),
+            )
+
+        w2_parts = [(w2_w, w2_sc)]
+
+        def deal_w2():
+            words = keep.tile([P, H], U8, name="w2_dealt", align_bytes=64)
+            scales = keep.tile([P, H // 2], U8, name="w2_sc_dealt", align_bytes=64)
+            nc.scalar.copy(
+                out=words[:].bitcast(U32).rearrange("p (u i) -> p u i", u=2),
+                in_=w2_w[:, H:].bitcast(U32).rearrange("p (i u) -> p u i", u=2),
+            )
+            nc.scalar.copy(
+                out=scales[:].bitcast(U16).rearrange("p (u i) -> p u i", u=2),
+                in_=w2_sc[:, H // 2 :].bitcast(U16).rearrange("p (i u) -> p u i", u=2),
+            )
+            w2_parts.append((words, scales))
 
         def spread(c, hf):
+            a, n = divmod(c, PAGES_PER_PASS)
             nc.tensor.matmul_mx(
                 out=spread_banks[hf][:],
-                lhsT=w2_w[:, 2 * c * P : 2 * (c + 1) * P].bitcast(FP4X4),
-                lhsT_scale=w2_sc[:, c * P : (c + 1) * P],
+                lhsT=w2_parts[a][0][:, 2 * n * P : 2 * (n + 1) * P].bitcast(FP4X4),
+                lhsT_scale=w2_parts[a][1][:, n * P : (n + 1) * P],
                 rhs=v_w[:, half_of(hf)].bitcast(FP8X4), rhs_scale=v_sc[:, half_of(hf)],
                 start=True, stop=True,
             )
@@ -183,6 +207,18 @@ def tile_list_lag_rewind_features_kernel(
             )
 
         gains, moved = {}, {}
+        wgs_dealt = []
+
+        def wgs_of(c):
+            return wgs_sb if c < PAGES_PER_PASS else wgs_dealt[(c - PAGES_PER_PASS) // 2]
+
+        def load_dealt_wgs():
+            rows = wgs.rearrange("(i u e) j -> u i e j", u=2, e=2)
+            for u in range(2):
+                wgs_dealt.append(keep.tile([P, S], F32, name=f"wgs_dealt{u}"))
+                for twice in range(2):
+                    nc.sync.dma_start(out=wgs_dealt[u][twice * P // 2 : (twice + 1) * P // 2], in_=rows[u])
+
 
         def make_gains(c, runs):
             if c not in gains:
@@ -192,17 +228,20 @@ def tile_list_lag_rewind_features_kernel(
             for lo, hi in runs:
                 nc.scalar.activation(gains[c][:, lo:hi], gains[c][:, lo:hi], ACT.Abs_reciprocal_sqrt, bias=half[:])
             for lo, hi in runs:
-                nc.scalar.activation(gains[c][:, lo:hi], gains[c][:, lo:hi], ACT.Square)
+                if lo == 0 and c in SQUARE_ON_GPSIMD:
+                    nc.gpsimd.tensor_tensor(gains[c][:, lo:hi], gains[c][:, lo:hi], gains[c][:, lo:hi], ALU.mult)
+                else:
+                    nc.scalar.activation(gains[c][:, lo:hi], gains[c][:, lo:hi], ACT.Square)
             if c == 0:
                 for lo, hi in runs:
                     if lo == 0:
                         continue
                     nc.gpsimd.tensor_tensor(gains[c][:, lo:hi], gains[c][:, lo:hi], wgs_sb[:, lo:hi], ALU.mult)
             elif c < LAST:
-                for hf, (lo, hi) in enumerate(runs):
+                for hf, (lo, hi) in list(enumerate(runs))[:: -1 if c in SQUARE_ON_GPSIMD else 1]:
                     at = MOVED_AT[hf] if c > 1 else FIRST_MOVED_AT[hf]
                     moved[c, hf] = shared.tile([P, BANK], F32, name=f"gains_moved{c}_{hf}", offset=at)
-                    nc.gpsimd.tensor_tensor(moved[c, hf][:], gains[c][:, lo:hi], wgs_sb[:, lo:hi], ALU.mult)
+                    nc.gpsimd.tensor_tensor(moved[c, hf][:], gains[c][:, lo:hi], wgs_of(c)[:, lo:hi], ALU.mult)
 
         def apply_gains(c, lo, hi, sums, values):
             if c in VECTOR_PAGES:
@@ -216,13 +255,13 @@ def tile_list_lag_rewind_features_kernel(
             if c < LAST and (c, lo) != (0, 0):
                 nc.vector.tensor_copy(window, values)
             else:
-                nc.vector.tensor_tensor(window, values, wgs_sb[:, lo:hi], ALU.mult)
+                nc.vector.tensor_tensor(window, values, wgs_of(c)[:, lo:hi], ALU.mult)
 
         halves = [(0, BANK), (BANK, S)]
 
-        z_turned = [
-            [keep.tile([P, BLOCKS, 2, P, 2], BF16, name=f"z_turned{a}_{g}") for g in range(GROUPS)]
-            for a in range(PASSES)
+        z_turned = [keep.tile([P, BLOCKS, 2, P, 2], BF16, name=f"z_turned0_{g}") for g in range(GROUPS)]
+        z_dealt = [
+            [keep.tile([P, BLOCKS, P, 2], BF16, name=f"z_turned1_{g}{u}") for g in range(GROUPS)] for u in range(2)
         ]
 
         def turn_into_sum(bank, g, rows, opens):
@@ -241,20 +280,33 @@ def tile_list_lag_rewind_features_kernel(
             a, quarter = divmod(c, PAGES_PER_PASS)
             for g in groups:
                 turn_into_sum(sums[g], g, pages[c % PAGE_TILES], False)
-                copies[g](
-                    out=z_turned[a][g][:, :, :, 32 * quarter : 32 * quarter + 32, :],
-                    in_=sums[g][:].rearrange("p (k i u e) -> p k u i e", k=BLOCKS, u=2, e=2),
-                )
+                if a == 0:
+                    copies[g](
+                        out=z_turned[g][:, :, :, 32 * quarter : 32 * quarter + 32, :],
+                        in_=sums[g][:].rearrange("p (k i u e) -> p k u i e", k=BLOCKS, u=2, e=2),
+                    )
+                else:
+                    u, h = divmod(quarter, 2)
+                    copies[g](
+                        out=z_dealt[u][g][:, :, 64 * h : 64 * h + 64, :],
+                        in_=sums[g][:].rearrange("p (k i e) -> p k i e", k=BLOCKS, e=2),
+                    )
 
-        def turn_back(a, g, pair, copies):
-            words = z_turned[a][g][:].rearrange("p k u r e -> p (k u r e)").bitcast(F32)
+        def turn_words(a, g, bank, j, u):
+            if a == 0:
+                words = z_turned[g][:].rearrange("p k u r e -> p (k u r e)").bitcast(F32)
+            else:
+                words = z_dealt[u][g][:].rearrange("p k r e -> p (k r e)").bitcast(F32)
+            for kk in range(2):
+                source = ((2 * j + kk) * 2 + u) * P if a == 0 else (2 * j + kk) * P
+                target = (u * 2 + kk) * P
+                nc.tensor.transpose(bank[:, target : target + P], words[:, source : source + P], ident[:])
+
+        def turn_back(a, g, pair, copies, left=(0, 1)):
             grouped = ring4.tile([P, BANK, 2], F32, name="z_grouped", align_bytes=64)
             for j in range(2):
-                for u in range(2):
-                    for kk in range(2):
-                        source = ((2 * j + kk) * 2 + u) * P
-                        target = (u * 2 + kk) * P
-                        nc.tensor.transpose(pair[j][:, target : target + P], words[:, source : source + P], ident[:])
+                for u in left:
+                    turn_words(a, g, pair[j], j, u)
                 copies[j](
                     out=grouped[:, j * BANK // 2 : (j + 1) * BANK // 2, :],
                     in_=pair[j][:].rearrange("p (u n) -> p n u", u=2),
@@ -311,7 +363,11 @@ def tile_list_lag_rewind_features_kernel(
 
         def make_values(c, a_banks):
             if c < LAST:
-                pieces = [(0, S, ring4.tile([P, S], F32, name="values", tag="listed"))]
+                if c == 1:
+                    values = shared.tile([P, S], F32, name="values_behind_last_w1", offset=RAW_AT + 4 * PACK * W1_CHUNKS[3][0])
+                else:
+                    values = ring4.tile([P, S], F32, name="values", tag="listed")
+                pieces = [(0, S, values)]
             else:
                 pieces = [
                     (lo, hi, shared.tile([P, hi - lo], F32, name=f"last_values{lo}", offset=at))
@@ -342,7 +398,11 @@ def tile_list_lag_rewind_features_kernel(
 
         for c, a_banks in ((1, sum_banks[0:2]), (2, motion_banks)):
             page_gains(c)
+            if c == 1:
+                quantize_w1(3)
+                deal_w2()
             scatter(c, 0, S, make_values(c, a_banks)[0][2][:])
+        load_dealt_wgs()
         preload_second_stage()
 
         first_pass = []
@@ -392,43 +452,36 @@ def tile_list_lag_rewind_features_kernel(
             else:
                 nc.scalar.activation(y_sb[i][:, cols], y_banks[i][g][:], ACT.Copy, scale=lam_sb[:, i : i + 1])
 
-        def first_pass_of_y(g):
-            quantize_z(0, g, first_pass[g])
-            product_pass(0, g, 0, True)
-
         def add_last_page(g):
             ticks = slice(g * BANK, (g + 1) * BANK)
             nc.vector.tensor_tensor(
-                last_sum[:, ticks].rearrange("p (j n e) -> p j n e", j=2, e=2),
-                pages[LAST % PAGE_TILES][:, ticks].rearrange("p (j e n) -> p j n e", j=2, e=2),
-                hist_sb[LAST][:, ticks].rearrange("p (j e n) -> p j n e", j=2, e=2),
+                last_sum[:, ticks].rearrange("p (j n c) -> p j n c", j=2, c=2),
+                pages[LAST % PAGE_TILES][:, ticks].rearrange("p (j c n) -> p j n c", j=2, c=2),
+                hist_sb[LAST][:, ticks].rearrange("p (j c n) -> p j n c", j=2, c=2),
                 ALU.add,
             )
             words = last_sum[:, ticks].bitcast(F32)
             bank = banks[ADD_BANKS[g]]
             for j in range(2):
                 nc.tensor.transpose(bank[:, j * P : (j + 1) * P], words[:, j * P : (j + 1) * P], ident[:])
-            for j in range(2):
-                nc.scalar.copy(
-                    out=z_turned[1][g][:, 2 * j : 2 * j + 2, :, 96:128, :],
-                    in_=bank[:, j * P : (j + 1) * P].bitcast(BF16).rearrange("p (i u c e) -> p e u i c", u=2, c=2, e=2),
-                )
+            nc.scalar.copy(
+                out=z_dealt[1][g][:, :, P // 2 :, :].rearrange("p (j c) i e -> p j c (i e)", j=2),
+                in_=bank[:, : BANK // 2].bitcast(BF16).rearrange("p (j q c) -> p j c q", j=2, c=2),
+            )
 
+        pairs = [banks[b : b + 2] for b in LAST_PAIRS]
+        for g in range(GROUPS - 1):
+            for j in range(2):
+                turn_words(1, g, pairs[g][j], j, 0)
         scatter(LAST, 0, S, pieces[0][2][:])
-        for g in range(GROUPS // 2):
-            first_pass_of_y(g)
         for g in range(GROUPS):
             add_last_page(g)
-        for g in range(GROUPS // 2, GROUPS):
-            quantize_z(0, g, first_pass[g])
         for g in range(GROUPS):
-            pair = banks[LAST_TURN_PAIRS[g] : LAST_TURN_PAIRS[g] + 2]
             copies = [(nc.vector.tensor_copy, nc.scalar.copy)[e] for e in TURN_COPIES[g]]
-            if g == FIRST_PASS_AT:
-                product_pass(0, 2, 0, True)
-                product_pass(0, 3, 0, True)
-            quantize_z(1, g, turn_back(1, g, pair, copies))
+            quantize_z(0, g, first_pass[g])
+            quantize_z(1, g, turn_back(1, g, pairs[g], copies, (1,) if g < GROUPS - 1 else (0, 1)))
         for g in range(GROUPS):
+            product_pass(0, g, 0, True)
             product_pass(0, g, 1, False)
             leave_bank(0, g)
 

@@ -41,6 +41,7 @@ Y_BANKS = (0, 1, 2, 3)
 ADD_BANKS = (6, 7, 6, 7)
 Y_ON_VECTOR = (3,)
 KIB = 1024
+PICKS_AT = {1: 10 * KIB + 512, 2: 15 * KIB}
 SQUARE_ON_GPSIMD = (5, 6)
 PAGES_AT = 60 * KIB
 Z_CODES_AT = ((68 * KIB, 70 * KIB, 72 * KIB, 74 * KIB), (8 * KIB, 10 * KIB, 12 * KIB, 14 * KIB))
@@ -434,7 +435,7 @@ def tile_list_lag_rewind_features_kernel(
         y_sb = [ring4.tile([P, T2], F32, name="y_sb", tag="rows") for i in range(2)]
         last_sum = ring4.tile([P, T2], BF16, name="last_sum", tag="rows")
         y_sb.extend(ring4.tile([P, T2], F32, name="y_sb", tag="rows") for i in range(2))
-        y_banks = [[banks[b] for b in Y_BANKS]] + [[banks[b] for b in Y_BANKS[2:]] * 2] * 3
+        y_banks = [[banks[b] for b in Y_BANKS]] + [[banks[b] for b in Y_BANKS[2:] + Y_BANKS[:2]]] * 3
 
         def product_pass(i, g, a, opens):
             nc.tensor.matmul_mx(
@@ -485,16 +486,30 @@ def tile_list_lag_rewind_features_kernel(
             product_pass(0, g, 1, False)
             leave_bank(0, g)
 
+        for i in range(1, N // P):
+            for g in range(GROUPS):
+                for a in range(PASSES):
+                    product_pass(i, g, a, a == 0)
+                leave_bank(i, g)
+
         idx3, idx4 = late_lists
-        for i in range(N // P):
-            if i + 1 < N // P:
-                for g in range(GROUPS):
-                    for a in range(PASSES):
-                        product_pass(i + 1, g, a, a == 0)
-                    leave_bank(i + 1, g)
-            x = ring4.tile([P, M], F32, name="x", tag="listed")
+        picked = []
+
+        def pick(i):
+            if i in PICKS_AT:
+                x = shared.tile([P, M], F32, name=f"x_behind_z{i}", offset=PICKS_AT[i])
+            else:
+                x = ring4.tile([P, M], F32, name="x", tag="listed")
             nc.vector.tensor_tensor(x[:], y_sb[i][:].indirect(idx3[:]), snap_sb[i][:], ALU.add)
-            nc.vector.tensor_tensor(slots[i % 2][:].indirect(idx4[:]), x[:], wgo_sb[:], ALU.mult)
+            picked.append(x)
+
+        pick(0)
+        for i in range(N // P):
+            if 0 < i < N // P - 1:
+                pick(i + 1)
+            nc.vector.tensor_tensor(slots[i % 2][:].indirect(idx4[:]), picked[i][:], wgo_sb[:], ALU.mult)
             for hf in range(2):
                 cols = slice(hf * T2 // 2, (hf + 1) * T2 // 2)
                 nc.sync.dma_start(out=out[i * P : (i + 1) * P, cols], in_=slots[i % 2][:, cols])
+            if i == 0:
+                pick(1)

@@ -18,6 +18,7 @@ ACT = mybir.ActivationFunctionType
 ALU = mybir.AluOpType
 
 P = 128
+QUAD = 32
 PACK = 4
 PER_COLUMN = 16
 BANK = 512
@@ -26,34 +27,30 @@ PAGES = H // P
 LAST = PAGES - 1
 PAGES_PER_PASS = PACK
 PASSES = PAGES // PAGES_PER_PASS
+EARLY = P - QUAD
 GROUPS = T2 // BANK
 BLOCKS = BANK // P
 PAGE_TILES = 3
 AHEAD = 3
 VECTOR_PAGES = (0, 1)
 W1_CHUNKS = ((0, 128), (128, 256), (256, 512), (512, 1024))
-TURN_PAIRS = (4, 6, 0, 2)
 VECTOR_CHUNKS = 2
-TURN_COPIES = ((1, 1), (1, 1), (0, 1), (0, 1))
+TURN_PAIRS = (4, 6, 0, 2)
 TURNS_BEFORE = 2
-LAST_PAIRS = (0, 2, 4, 6)
-Y_BANKS = (0, 1, 2, 3)
-ADD_BANKS = (6, 7, 6, 7)
+SQUARE_ON_GPSIMD = (5, 6)
 Y_ON_VECTOR = (3,)
 KIB = 1024
-PICKS_AT = {1: 10 * KIB + 512, 2: 15 * KIB}
-SQUARE_ON_GPSIMD = (5, 6)
-PAGES_AT = 60 * KIB
-Z_CODES_AT = ((68 * KIB, 70 * KIB, 72 * KIB, 74 * KIB), (8 * KIB, 10 * KIB, 12 * KIB, 14 * KIB))
 TABLE_AT = 0
-LAST_VALUES_AT = (4 * KIB,)
 TABLE_SCALES_AT = 16 * KIB
+LAST_VALUES_AT = 16 * KIB
 SLOTS_AT = (20 * KIB, 28 * KIB)
 GAINS_AT = (36 * KIB, 26 * KIB, 56 * KIB)
 ROUNDED_AT = (30 * KIB, 31 * KIB, 21 * KIB, 32 * KIB)
 MOVED_AT = (32 * KIB, 34 * KIB)
 FIRST_MOVED_AT = (20 * KIB, 22 * KIB)
 RAW_AT = 40 * KIB
+PAGES_AT = 60 * KIB
+PICKS_AT = {1: 0, 2: 4 * KIB}
 
 
 def tile_list_lag_rewind_features_kernel(
@@ -136,12 +133,7 @@ def tile_list_lag_rewind_features_kernel(
 
         def load_hist(c):
             rows = ring4.tile([P, T2], F32, name="hist_sb", tag="rows")
-            if c < PAGES_PER_PASS:
-                nc.sync.dma_start(out=rows[:], in_=hist[c * P : (c + 1) * P, :])
-            else:
-                u, h = divmod(c - PAGES_PER_PASS, 2)
-                dealt = hist[H // 2 :, :].rearrange("(h i u e) t -> u h i e t", h=2, u=2, e=2)
-                nc.sync.dma_start(out=rows[:], in_=dealt[u, h])
+            nc.sync.dma_start(out=rows[:], in_=hist[c * P : (c + 1) * P, :])
             hist_sb.append(rows)
 
         for c in range(PAGES_PER_PASS):
@@ -161,39 +153,18 @@ def tile_list_lag_rewind_features_kernel(
         def quantize_w1(k):
             lo, hi = W1_CHUNKS[k]
             rounded = shared.tile([P, hi - lo, PACK], BF16, name=f"w1_rounded{k}", align_bytes=64, offset=ROUNDED_AT[k])
-            if k < len(W1_CHUNKS) - 1:
-                nc.vector.tensor_copy(out=rounded[:], in_=w1_raw[k][:].rearrange("p t c -> p c t"))
-            else:
-                nc.scalar.copy(
-                    out=rounded[:].rearrange("p (u i e) t -> p u i e t", u=2, e=2),
-                    in_=w1_raw[k][:].rearrange("p t (i u e) -> p u i e t", u=2, e=2),
-                )
+            copy = nc.vector.tensor_copy if k < len(W1_CHUNKS) - 1 else nc.scalar.copy
+            copy(out=rounded[:], in_=w1_raw[k][:].rearrange("p t c -> p c t"))
             nc.vector.quantize_mx(
                 out=w1_w[:, lo:hi].bitcast(FP8X4), scales=w1_sc[:, lo:hi],
                 in_=rounded[:].rearrange("p c t -> p (c t)"),
             )
 
-        w2_parts = [(w2_w, w2_sc)]
-
-        def deal_w2():
-            words = keep.tile([P, H], U8, name="w2_dealt", align_bytes=64)
-            scales = keep.tile([P, H // 2], U8, name="w2_sc_dealt", align_bytes=64)
-            nc.scalar.copy(
-                out=words[:].bitcast(U32).rearrange("p (u i) -> p u i", u=2),
-                in_=w2_w[:, H:].bitcast(U32).rearrange("p (i u) -> p u i", u=2),
-            )
-            nc.scalar.copy(
-                out=scales[:].bitcast(U16).rearrange("p (u i) -> p u i", u=2),
-                in_=w2_sc[:, H // 2 :].bitcast(U16).rearrange("p (i u) -> p u i", u=2),
-            )
-            w2_parts.append((words, scales))
-
         def spread(c, hf):
-            a, n = divmod(c, PAGES_PER_PASS)
             nc.tensor.matmul_mx(
                 out=spread_banks[hf][:],
-                lhsT=w2_parts[a][0][:, 2 * n * P : 2 * (n + 1) * P].bitcast(FP4X4),
-                lhsT_scale=w2_parts[a][1][:, n * P : (n + 1) * P],
+                lhsT=w2_w[:, 2 * c * P : 2 * (c + 1) * P].bitcast(FP4X4),
+                lhsT_scale=w2_sc[:, c * P : (c + 1) * P],
                 rhs=v_w[:, half_of(hf)].bitcast(FP8X4), rhs_scale=v_sc[:, half_of(hf)],
                 start=True, stop=True,
             )
@@ -208,18 +179,6 @@ def tile_list_lag_rewind_features_kernel(
             )
 
         gains, moved = {}, {}
-        wgs_dealt = []
-
-        def wgs_of(c):
-            return wgs_sb if c < PAGES_PER_PASS else wgs_dealt[(c - PAGES_PER_PASS) // 2]
-
-        def load_dealt_wgs():
-            rows = wgs.rearrange("(i u e) j -> u i e j", u=2, e=2)
-            for u in range(2):
-                wgs_dealt.append(keep.tile([P, S], F32, name=f"wgs_dealt{u}"))
-                for twice in range(2):
-                    nc.sync.dma_start(out=wgs_dealt[u][twice * P // 2 : (twice + 1) * P // 2], in_=rows[u])
-
 
         def make_gains(c, runs):
             if c not in gains:
@@ -242,7 +201,7 @@ def tile_list_lag_rewind_features_kernel(
                 for hf, (lo, hi) in list(enumerate(runs))[:: -1 if c in SQUARE_ON_GPSIMD else 1]:
                     at = MOVED_AT[hf] if c > 1 else FIRST_MOVED_AT[hf]
                     moved[c, hf] = shared.tile([P, BANK], F32, name=f"gains_moved{c}_{hf}", offset=at)
-                    nc.gpsimd.tensor_tensor(moved[c, hf][:], gains[c][:, lo:hi], wgs_of(c)[:, lo:hi], ALU.mult)
+                    nc.gpsimd.tensor_tensor(moved[c, hf][:], gains[c][:, lo:hi], wgs_sb[:, lo:hi], ALU.mult)
 
         def apply_gains(c, lo, hi, sums, values):
             if c in VECTOR_PAGES:
@@ -256,14 +215,12 @@ def tile_list_lag_rewind_features_kernel(
             if c < LAST and (c, lo) != (0, 0):
                 nc.vector.tensor_copy(window, values)
             else:
-                nc.vector.tensor_tensor(window, values, wgs_of(c)[:, lo:hi], ALU.mult)
+                nc.vector.tensor_tensor(window, values, wgs_sb[:, lo:hi], ALU.mult)
 
         halves = [(0, BANK), (BANK, S)]
 
-        z_turned = [keep.tile([P, BLOCKS, 2, P, 2], BF16, name=f"z_turned0_{g}") for g in range(GROUPS)]
-        z_dealt = [
-            [keep.tile([P, BLOCKS, P, 2], BF16, name=f"z_turned1_{g}{u}") for g in range(GROUPS)] for u in range(2)
-        ]
+        z_turned = [keep.tile([P, BLOCKS, 2, P, 2], BF16, name=f"z_turned{g}") for g in range(GROUPS)]
+        z_grouped = [keep.tile([P, PASSES, BANK, 2], F32, name=f"z_grouped{g}", align_bytes=64) for g in range(GROUPS)]
 
         def turn_into_sum(bank, g, rows, opens):
             for k in range(BLOCKS):
@@ -277,56 +234,48 @@ def tile_list_lag_rewind_features_kernel(
             for g in groups:
                 turn_into_sum(sums[g], g, hist_sb[c], True)
 
-        def close_sums(c, sums, groups, copies):
-            a, quarter = divmod(c, PAGES_PER_PASS)
+        def close_sums(c, sums, groups):
+            quarter = c % PAGES_PER_PASS
             for g in groups:
                 turn_into_sum(sums[g], g, pages[c % PAGE_TILES], False)
-                if a == 0:
-                    copies[g](
-                        out=z_turned[g][:, :, :, 32 * quarter : 32 * quarter + 32, :],
-                        in_=sums[g][:].rearrange("p (k i u e) -> p k u i e", k=BLOCKS, u=2, e=2),
-                    )
-                else:
-                    u, h = divmod(quarter, 2)
-                    copies[g](
-                        out=z_dealt[u][g][:, :, 64 * h : 64 * h + 64, :],
-                        in_=sums[g][:].rearrange("p (k i e) -> p k i e", k=BLOCKS, e=2),
-                    )
+                nc.scalar.copy(
+                    out=z_turned[g][:, :, :, QUAD * quarter : QUAD * (quarter + 1), :],
+                    in_=sums[g][:].rearrange("p (k i u e) -> p k u i e", k=BLOCKS, u=2, e=2),
+                )
 
-        def turn_words(a, g, bank, j, u):
-            if a == 0:
-                words = z_turned[g][:].rearrange("p k u r e -> p (k u r e)").bitcast(F32)
-            else:
-                words = z_dealt[u][g][:].rearrange("p k r e -> p (k r e)").bitcast(F32)
-            for kk in range(2):
-                source = ((2 * j + kk) * 2 + u) * P if a == 0 else (2 * j + kk) * P
-                target = (u * 2 + kk) * P
-                nc.tensor.transpose(bank[:, target : target + P], words[:, source : source + P], ident[:])
-
-        def turn_back(a, g, pair, copies, left=(0, 1)):
-            grouped = ring4.tile([P, BANK, 2], F32, name="z_grouped", align_bytes=64)
+        def turn_words(g, pair):
+            words = z_turned[g][:].rearrange("p k u r e -> p (k u r e)").bitcast(F32)
             for j in range(2):
-                for u in left:
-                    turn_words(a, g, pair[j], j, u)
-                copies[j](
-                    out=grouped[:, j * BANK // 2 : (j + 1) * BANK // 2, :],
+                for u in range(2):
+                    for kk in range(2):
+                        source = ((2 * j + kk) * 2 + u) * P
+                        target = (u * 2 + kk) * P
+                        nc.tensor.transpose(pair[j][:, target : target + P], words[:, source : source + P], ident[:])
+
+        def lay_words(a, g, pair):
+            for j in range(2):
+                nc.scalar.copy(
+                    out=z_grouped[g][:, a, j * BANK // 2 : (j + 1) * BANK // 2, :],
                     in_=pair[j][:].rearrange("p (u n) -> p n u", u=2),
                 )
-            return grouped
 
-        z_w, z_sc = {}, {}
+        def turn_first_pass(groups):
+            for g in groups:
+                pair = banks[TURN_PAIRS[g] : TURN_PAIRS[g] + 2]
+                turn_words(g, pair)
+                lay_words(0, g, pair)
 
-        def quantize_z(a, g, grouped):
-            z_w[a, g] = shared.tile(
-                [P, BANK], U32, name=f"z_w{a}_{g}", align_bytes=64, offset=Z_CODES_AT[a][g]
-            )
-            z_sc[a, g] = keep.tile([P, BANK], U8, name=f"z_sc{a}_{g}", align_bytes=64)
+        def quantize(words, scales, grouped):
             nc.vector.quantize_mx(
-                out=z_w[a, g][:].bitcast(FP8X4), scales=z_sc[a, g][:],
-                in_=grouped[:].rearrange("p n u -> p (n u)").bitcast(BF16),
+                out=words.bitcast(FP8X4), scales=scales, in_=grouped.bitcast(BF16)
             )
 
         w3_w = keep.tile([P, PASSES, N], I32, name="w3_w", align_bytes=64)
+        w3_apart = keep.tile([P, BLOCKS + 1, P], I32, name="w3_apart", align_bytes=64)
+        w3_last, w3_early = w3_apart[:, :BLOCKS], w3_apart[:, BLOCKS]
+        w3_last_sc = keep.tile([P, P], U8, name="w3_last_sc", align_bytes=64)
+        nc.gpsimd.memset(w3_apart[:], 0)
+        nc.gpsimd.memset(w3_last_sc[:].bitcast(I32), 0)
         wgo_sb = keep.tile([P, M], F32, name="wgo_sb")
         lam_sb = keep.tile([P, N // P], F32, name="lam_sb")
         snap_sb = []
@@ -335,6 +284,11 @@ def tile_list_lag_rewind_features_kernel(
         def preload_second_stage():
             nc.sync.dma_start(out=w3_w[:], in_=w3_words.rearrange("a p c t -> p a (c t)").bitcast(I32))
             load_scale_rows(w3_sc, lambda q: w3_scales[:, 4 * q : 4 * q + 4, :].rearrange("a q n -> q a n"))
+            second = w3_words[1].rearrange("p c t -> p (c t)").bitcast(I32)
+            for k in range(BLOCKS):
+                nc.sync.dma_start(out=w3_last[QUAD * k : QUAD * (k + 1), k, :], in_=second[EARLY:, :P])
+            load_scale_rows(w3_last_sc, lambda q: w3_scales[1, 12:16, :P])
+            nc.sync.dma_start(out=w3_early[:EARLY], in_=second[:EARLY, :P])
             nc.sync.dma_start(out=wgo_sb[:], in_=wgo)
             late_lists.extend([load_list("idx3", offs3), load_list("idx4", offs4)])
             with nc.allow_non_contiguous_dma(reason="one value of lam for each partition and row tile"):
@@ -343,8 +297,6 @@ def tile_list_lag_rewind_features_kernel(
                 rows = shared.tile([P, M], F32, name=f"snap_sb{i}", offset=RAW_AT + 4 * M * i)
                 nc.sync.dma_start(out=rows[:], in_=snap[i * P : (i + 1) * P, :])
                 snap_sb.append(rows)
-
-        on_scalar = [nc.scalar.copy] * GROUPS
 
         for k in range(VECTOR_CHUNKS):
             quantize_w1(k)
@@ -370,10 +322,7 @@ def tile_list_lag_rewind_features_kernel(
                     values = ring4.tile([P, S], F32, name="values", tag="listed")
                 pieces = [(0, S, values)]
             else:
-                pieces = [
-                    (lo, hi, shared.tile([P, hi - lo], F32, name=f"last_values{lo}", offset=at))
-                    for (lo, hi), at in zip(((0, S),), LAST_VALUES_AT)
-                ]
+                pieces = [(0, S, shared.tile([P, S], F32, name="last_values", offset=LAST_VALUES_AT))]
             for hf, (first, stop) in enumerate(halves):
                 motion(c, first, stop, a_banks[hf])
                 for lo, hi, values in pieces:
@@ -395,23 +344,19 @@ def tile_list_lag_rewind_features_kernel(
         def history_sums(c, groups):
             sums = product_banks if c == LAST - 2 else sum_banks
             open_sums(c, sums, groups)
-            close_sums(c, sums, groups, on_scalar)
+            close_sums(c, sums, groups)
 
         for c, a_banks in ((1, sum_banks[0:2]), (2, motion_banks)):
             page_gains(c)
             if c == 1:
                 quantize_w1(3)
-                deal_w2()
             scatter(c, 0, S, make_values(c, a_banks)[0][2][:])
-        load_dealt_wgs()
         preload_second_stage()
 
-        first_pass = []
         for c in range(LAST):
             ahead = c + AHEAD
             if ahead == LAST:
-                for g, pair in enumerate(TURN_PAIRS[:TURNS_BEFORE]):
-                    first_pass.append(turn_back(0, g, banks[pair : pair + 2], on_scalar))
+                turn_first_pass(range(TURNS_BEFORE))
             if ahead < PAGES:
                 page_gains(ahead)
             split = GROUPS // 2 if ahead < LAST else 0
@@ -419,8 +364,7 @@ def tile_list_lag_rewind_features_kernel(
             if ahead < PAGES:
                 pieces = make_values(ahead, motion_banks)
             if ahead == LAST:
-                for pair in TURN_PAIRS[TURNS_BEFORE:]:
-                    first_pass.append(turn_back(0, len(first_pass), banks[pair : pair + 2], on_scalar))
+                turn_first_pass(range(TURNS_BEFORE, GROUPS))
             history_sums(c, range(split, GROUPS))
             if c + PAGES_PER_PASS < PAGES:
                 load_hist(c + PAGES_PER_PASS)
@@ -432,65 +376,89 @@ def tile_list_lag_rewind_features_kernel(
         for tile in slots:
             nc.gpsimd.memset(tile[:], 0.0)
 
-        y_sb = [ring4.tile([P, T2], F32, name="y_sb", tag="rows") for i in range(2)]
-        last_sum = ring4.tile([P, T2], BF16, name="last_sum", tag="rows")
-        y_sb.extend(ring4.tile([P, T2], F32, name="y_sb", tag="rows") for i in range(2))
-        y_banks = [[banks[b] for b in Y_BANKS]] + [[banks[b] for b in Y_BANKS[2:] + Y_BANKS[:2]]] * 3
-
-        def product_pass(i, g, a, opens):
-            nc.tensor.matmul_mx(
-                out=y_banks[i][g][:],
-                lhsT=w3_w[:, a, i * P : (i + 1) * P].bitcast(FP8X4),
-                lhsT_scale=w3_sc[:, a, i * P : (i + 1) * P],
-                rhs=z_w[a, g][:].bitcast(FP8X4), rhs_scale=z_sc[a, g][:],
-                start=opens, stop=not opens,
-            )
-
-        def leave_bank(i, g):
-            cols = slice(g * BANK, (g + 1) * BANK)
-            if i == 0 and g in Y_ON_VECTOR:
-                nc.vector.tensor_scalar(y_sb[i][:, cols], y_banks[i][g][:], lam_sb[:, i : i + 1], None, ALU.mult)
-            else:
-                nc.scalar.activation(y_sb[i][:, cols], y_banks[i][g][:], ACT.Copy, scale=lam_sb[:, i : i + 1])
-
-        def add_last_page(g):
-            ticks = slice(g * BANK, (g + 1) * BANK)
-            nc.vector.tensor_tensor(
-                last_sum[:, ticks].rearrange("p (j n c) -> p j n c", j=2, c=2),
-                pages[LAST % PAGE_TILES][:, ticks].rearrange("p (j c n) -> p j n c", j=2, c=2),
-                hist_sb[LAST][:, ticks].rearrange("p (j c n) -> p j n c", j=2, c=2),
-                ALU.add,
-            )
-            words = last_sum[:, ticks].bitcast(F32)
-            bank = banks[ADD_BANKS[g]]
-            for j in range(2):
-                nc.tensor.transpose(bank[:, j * P : (j + 1) * P], words[:, j * P : (j + 1) * P], ident[:])
-            nc.scalar.copy(
-                out=z_dealt[1][g][:, :, P // 2 :, :].rearrange("p (j c) i e -> p j c (i e)", j=2),
-                in_=bank[:, : BANK // 2].bitcast(BF16).rearrange("p (j q c) -> p j c q", j=2, c=2),
-            )
-
-        pairs = [banks[b : b + 2] for b in LAST_PAIRS]
-        for g in range(GROUPS - 1):
-            for j in range(2):
-                turn_words(1, g, pairs[g][j], j, 0)
+        pairs = [banks[2 * g : 2 * g + 2] for g in range(GROUPS)]
+        for g in range(GROUPS):
+            turn_words(g, pairs[g])
+        for g in range(GROUPS):
+            lay_words(1, g, pairs[g])
+        open_sums(LAST, product_banks, range(GROUPS))
         scatter(LAST, 0, S, pieces[0][2][:])
-        for g in range(GROUPS):
-            add_last_page(g)
-        for g in range(GROUPS):
-            copies = [(nc.vector.tensor_copy, nc.scalar.copy)[e] for e in TURN_COPIES[g]]
-            quantize_z(0, g, first_pass[g])
-            quantize_z(1, g, turn_back(1, g, pairs[g], copies, (1,) if g < GROUPS - 1 else (0, 1)))
-        for g in range(GROUPS):
-            product_pass(0, g, 0, True)
-            product_pass(0, g, 1, False)
-            leave_bank(0, g)
 
+        last_turned, last_grouped = [], []
+        for g in range(GROUPS):
+            turn_into_sum(product_banks[g], g, pages[LAST % PAGE_TILES], False)
+            turned = keep.tile([P, 2, P, 2], BF16, name=f"last_turned{g}")
+            nc.scalar.copy(out=turned[:], in_=product_banks[g][:].rearrange("p (r u e) -> p u r e", u=2, e=2))
+            last_turned.append(turned)
+        for g in range(GROUPS):
+            words = last_turned[g][:].rearrange("p u r e -> p (u r e)").bitcast(F32)
+            for u in range(2):
+                nc.tensor.transpose(product_banks[g][:, u * P : (u + 1) * P], words[:, u * P : (u + 1) * P], ident[:])
+            grouped = keep.tile([P, P, 2], F32, name=f"last_grouped{g}", align_bytes=64)
+            nc.scalar.copy(out=grouped[:], in_=product_banks[g][:, : 2 * P].rearrange("p (u n) -> p n u", u=2))
+            last_grouped.append(grouped)
+
+        z_w = shared.tile([P, GROUPS, PASSES, BANK], U32, name="z_w", align_bytes=64, offset=TABLE_AT)
+        z_sc = keep.tile([P, GROUPS, PASSES, BANK], U8, name="z_sc", align_bytes=64)
+        last_w = keep.tile([P, BANK], U32, name="last_w", align_bytes=64)
+        last_sc = keep.tile([P, BANK], U8, name="last_sc", align_bytes=64)
+
+        def ticks_of(g):
+            return slice(g * BANK, (g + 1) * BANK)
+
+        def block_of(k):
+            return slice(k * P, (k + 1) * P)
+
+        for g in range(GROUPS):
+            quantize(
+                z_w[:, g].rearrange("p a n -> p (a n)"), z_sc[:, g].rearrange("p a n -> p (a n)"),
+                z_grouped[g][:].rearrange("p a n u -> p (a n u)"),
+            )
+        for g in range(GROUPS):
+            quantize(last_w[:, block_of(g)], last_sc[:, block_of(g)], last_grouped[g][:].rearrange("p n u -> p (n u)"))
+
+        y_sb = [ring4.tile([P, T2], F32, name="y_sb", tag="rows") for i in range(N // P)]
+
+        def product(out_columns, weights, weight_scales, words, scales, start, stop):
+            nc.tensor.matmul_mx(
+                out=out_columns, lhsT=weights.bitcast(FP8X4), lhsT_scale=weight_scales,
+                rhs=words.bitcast(FP8X4), rhs_scale=scales, start=start, stop=stop,
+            )
+
+        def leave_bank(i, g, bank):
+            if i == 0 and g in Y_ON_VECTOR:
+                nc.vector.tensor_scalar(y_sb[i][:, ticks_of(g)], bank[:], lam_sb[:, i : i + 1], None, ALU.mult)
+            else:
+                nc.scalar.activation(y_sb[i][:, ticks_of(g)], bank[:], ACT.Copy, scale=lam_sb[:, i : i + 1])
+
+        for g in range(GROUPS):
+            bank = sum_banks[g]
+            product(bank[:], w3_w[:, 0, :P], w3_sc[:, 0, :P], z_w[:, g, 0], z_sc[:, g, 0], True, False)
+            product(bank[:], w3_early, w3_sc[:, 1, :P], z_w[:, g, 1], z_sc[:, g, 1], False, False)
+        for g in range(GROUPS):
+            bank = sum_banks[g]
+            for k in range(BLOCKS):
+                product(
+                    bank[:, block_of(k)], w3_last[:, k, :], w3_last_sc[:],
+                    last_w[:, block_of(g)], last_sc[:, block_of(g)], False, k == BLOCKS - 1,
+                )
+            leave_bank(0, g, bank)
+
+        for k in range(BLOCKS):
+            nc.sync.dma_start(
+                out=z_w[EARLY:, :, 1, block_of(k)].bitcast(I32),
+                in_=last_w[QUAD * k : QUAD * (k + 1)].bitcast(I32).rearrange("p (g n) -> p g n", g=GROUPS),
+            )
+            nc.sync.dma_start(
+                out=z_sc[EARLY : EARLY + 4, :, 1, block_of(k)].bitcast(I32),
+                in_=last_sc[QUAD * k : QUAD * k + 4].bitcast(I32).rearrange("p (g n) -> p g n", g=GROUPS),
+            )
         for i in range(1, N // P):
             for g in range(GROUPS):
-                for a in range(PASSES):
-                    product_pass(i, g, a, a == 0)
-                leave_bank(i, g)
+                bank = product_banks[g]
+                product(bank[:], w3_w[:, 0, block_of(i)], w3_sc[:, 0, block_of(i)], z_w[:, g, 0], z_sc[:, g, 0], True, False)
+                product(bank[:], w3_w[:, 1, block_of(i)], w3_sc[:, 1, block_of(i)], z_w[:, g, 1], z_sc[:, g, 1], False, True)
+                leave_bank(i, g, bank)
 
         idx3, idx4 = late_lists
         picked = []

@@ -23,6 +23,7 @@ PACK = 4
 PER_COLUMN = 16
 BANK = 512
 QUARTER = 256
+FIRST_RUNS = ((0, QUARTER), (QUARTER, BANK), (BANK, S))
 PAGES = H // P
 LAST = PAGES - 1
 PAGES_PER_PASS = PACK
@@ -33,20 +34,26 @@ BLOCKS = BANK // P
 PAGE_TILES = 3
 AHEAD = 3
 VECTOR_PAGES = (0, 1)
-W1_CHUNKS = ((0, 128), (128, 256), (256, 512), (512, 1024))
+W1_CHUNKS = ((0, 128), (128, 512), (512, 1024))
 VECTOR_CHUNKS = 2
+ROUNDED_BY_GPSIMD = (0, 2)
 TURN_PAIRS = (4, 6, 0, 2)
 TURNS_BEFORE = 2
-SQUARE_ON_GPSIMD = (5, 6)
-Y_ON_VECTOR = (3,)
+SQUARE_ON_GPSIMD = (5, 6, 7)
+Y_ON_VECTOR = (1, 3)
+FIRST_Y_BANKS = (4, 5, 1, 3)
+LAST_TURN_BANKS = (6, 7, 0, 2)
+LATER_Y_BANKS = (6, 7, 0, 2)
 KIB = 1024
 TABLE_AT = 0
 TABLE_SCALES_AT = 16 * KIB
 LAST_VALUES_AT = 16 * KIB
-SLOTS_AT = (20 * KIB, 28 * KIB)
-GAINS_AT = (36 * KIB, 26 * KIB, 56 * KIB)
-ROUNDED_AT = (30 * KIB, 31 * KIB, 21 * KIB, 32 * KIB)
-MOVED_AT = (32 * KIB, 34 * KIB)
+SLOTS_AT = (84 * KIB, 28 * KIB)
+GAINS_AT = (36 * KIB, 84 * KIB, 56 * KIB)
+SECOND_GAINS_AT = 26 * KIB
+FIRST_ROOTS_AT = 34 * KIB
+ROUNDED_AT = (30 * KIB, 16 * KIB, 26 * KIB)
+MOVED_AT = (32 * KIB, 26 * KIB)
 FIRST_MOVED_AT = (20 * KIB, 22 * KIB)
 RAW_AT = 40 * KIB
 PAGES_AT = 60 * KIB
@@ -104,16 +111,17 @@ def tile_list_lag_rewind_features_kernel(
         load_scale_rows(tab_sc, lambda q: tab_scales[0, 4 * q : 4 * q + 4, :])
         nc.sync.dma_start(out=tab_w[:, T // 4 :], in_=tab_rows[:, T // 4 :])
         w2_w = keep.tile([P, 2 * H], U8, name="w2_w", align_bytes=64)
-        nc.sync.dma_start(out=w2_w[:].bitcast(I32), in_=w2_words[0].bitcast(I32))
+        w2_rows = w2_words[0].bitcast(I32)
+        nc.sync.dma_start(out=w2_w[:].bitcast(I32)[:, :P], in_=w2_rows[:, :P])
         load_scale_rows(w2_sc, lambda q: w2_scales[0, 4 * q : 4 * q + 4, :])
-        for k in range(VECTOR_CHUNKS):
-            load_w1(k)
+        load_w1(0)
+        load_w1(1)
         wgs_sb = keep.tile([P, S], F32, name="wgs_sb")
         nc.sync.dma_start(out=wgs_sb[:, half_of(0)], in_=wgs[:, half_of(0)])
         idx2 = load_list("idx2", offs2)
         nc.sync.dma_start(out=wgs_sb[:, half_of(1)], in_=wgs[:, half_of(1)])
-        for k in range(VECTOR_CHUNKS, len(W1_CHUNKS)):
-            load_w1(k)
+        nc.sync.dma_start(out=w2_w[:].bitcast(I32)[:, P:], in_=w2_rows[:, P:])
+        load_w1(2)
 
         half = keep.tile([P, 1], F32, name="half")
         nc.gpsimd.memset(half[:], 0.5)
@@ -142,66 +150,76 @@ def tile_list_lag_rewind_features_kernel(
         v_sc = keep.tile([P, S], U8, name="v_sc", align_bytes=64)
         nc.vector.tensor_copy(v_sc[:], tab_sc[:].indirect(idx[:]))
         v_w = keep.tile([P, S], U32, name="v_w", align_bytes=64)
-        for hf in range(2):
-            nc.vector.tensor_copy(
-                v_w[:, half_of(hf)], tab_w[:].bitcast(U32).indirect(entries(idx, hf * BANK, (hf + 1) * BANK))
-            )
+        for lo, hi in FIRST_RUNS:
+            nc.vector.tensor_copy(v_w[:, lo:hi], tab_w[:].bitcast(U32).indirect(entries(idx, lo, hi)))
 
-        w1_w = keep.tile([P, H], U32, name="w1_w", align_bytes=64)
-        w1_sc = keep.tile([P, H], U8, name="w1_sc", align_bytes=64)
+        w1_rounded, w1_w, w1_sc = {}, {}, {}
+
+        def round_w1(k):
+            lo, hi = W1_CHUNKS[k]
+            w1_rounded[k] = shared.tile([P, hi - lo, PACK], BF16, name=f"w1_rounded{k}", align_bytes=64, offset=ROUNDED_AT[k])
+            raw = w1_raw[k][:].rearrange("p t c -> p c t")
+            if k in ROUNDED_BY_GPSIMD:
+                nc.gpsimd.tensor_scalar(w1_rounded[k][:], raw, 1.0, 0.0, ALU.mult, ALU.add)
+            else:
+                nc.vector.tensor_copy(out=w1_rounded[k][:], in_=raw)
 
         def quantize_w1(k):
             lo, hi = W1_CHUNKS[k]
-            rounded = shared.tile([P, hi - lo, PACK], BF16, name=f"w1_rounded{k}", align_bytes=64, offset=ROUNDED_AT[k])
-            copy = nc.vector.tensor_copy if k < len(W1_CHUNKS) - 1 else nc.scalar.copy
-            copy(out=rounded[:], in_=w1_raw[k][:].rearrange("p t c -> p c t"))
+            words = keep.tile([P, hi - lo], U32, name=f"w1_w{k}", align_bytes=64)
+            scales = keep.tile([P, hi - lo], U8, name=f"w1_sc{k}", align_bytes=64)
             nc.vector.quantize_mx(
-                out=w1_w[:, lo:hi].bitcast(FP8X4), scales=w1_sc[:, lo:hi],
-                in_=rounded[:].rearrange("p c t -> p (c t)"),
+                out=words[:].bitcast(FP8X4), scales=scales[:], in_=w1_rounded[k][:].rearrange("p c t -> p (c t)")
             )
+            for c in range(lo // P, hi // P):
+                w1_w[c], w1_sc[c] = words[:, c * P - lo : (c + 1) * P - lo], scales[:, c * P - lo : (c + 1) * P - lo]
 
-        def spread(c, hf):
+        def spread(c, lo, hi, bank):
             nc.tensor.matmul_mx(
-                out=spread_banks[hf][:],
+                out=bank[:, : hi - lo],
                 lhsT=w2_w[:, 2 * c * P : 2 * (c + 1) * P].bitcast(FP4X4),
                 lhsT_scale=w2_sc[:, c * P : (c + 1) * P],
-                rhs=v_w[:, half_of(hf)].bitcast(FP8X4), rhs_scale=v_sc[:, half_of(hf)],
+                rhs=v_w[:, lo:hi].bitcast(FP8X4), rhs_scale=v_sc[:, lo:hi],
                 start=True, stop=True,
             )
 
         def motion(c, lo, hi, bank):
             nc.tensor.matmul_mx(
                 out=bank[:, : hi - lo],
-                lhsT=w1_w[:, c * P : (c + 1) * P].bitcast(FP8X4),
-                lhsT_scale=w1_sc[:, c * P : (c + 1) * P],
+                lhsT=w1_w[c].bitcast(FP8X4), lhsT_scale=w1_sc[c],
                 rhs=v_w[:, lo:hi].bitcast(FP8X4), rhs_scale=v_sc[:, lo:hi],
                 start=True, stop=True,
             )
 
         gains, moved = {}, {}
 
-        def make_gains(c, runs):
+        def make_gains(c, runs, b_banks):
             if c not in gains:
-                gains[c] = shared.tile([P, S], F32, name=f"gains{c}", offset=GAINS_AT[c % len(GAINS_AT)])
-            for lo, hi in runs:
-                nc.scalar.activation(gains[c][:, lo:hi], spread_banks[lo // BANK][:, lo % BANK : lo % BANK + hi - lo], ACT.Abs)
-            for lo, hi in runs:
-                nc.scalar.activation(gains[c][:, lo:hi], gains[c][:, lo:hi], ACT.Abs_reciprocal_sqrt, bias=half[:])
-            for lo, hi in runs:
-                if lo == 0 and c in SQUARE_ON_GPSIMD:
-                    nc.gpsimd.tensor_tensor(gains[c][:, lo:hi], gains[c][:, lo:hi], gains[c][:, lo:hi], ALU.mult)
-                else:
-                    nc.scalar.activation(gains[c][:, lo:hi], gains[c][:, lo:hi], ACT.Square)
+                gains[c] = shared.tile([P, S], F32, name=f"gains{c}", offset=SECOND_GAINS_AT if c == 1 else GAINS_AT[c % len(GAINS_AT)])
+            for (lo, hi), bank in zip(runs, b_banks):
+                spread(c, lo, hi, bank)
+                nc.scalar.activation(gains[c][:, lo:hi], bank[:, : hi - lo], ACT.Abs)
+            wide = runs if c in VECTOR_PAGES else [(0, S)]
+            roots = gains[c]
+            if runs == FIRST_RUNS[:2]:
+                roots = shared.tile([P, BANK], F32, name="first_roots", offset=FIRST_ROOTS_AT)
+            for lo, hi in wide:
+                nc.scalar.activation(roots[:, lo:hi], gains[c][:, lo:hi], ACT.Abs_reciprocal_sqrt, bias=half[:])
+            if c in SQUARE_ON_GPSIMD:
+                nc.gpsimd.tensor_tensor(gains[c][:, :BANK], gains[c][:, :BANK], gains[c][:, :BANK], ALU.mult)
+                nc.scalar.activation(gains[c][:, BANK:], gains[c][:, BANK:], ACT.Square)
+            else:
+                for lo, hi in wide:
+                    nc.scalar.activation(gains[c][:, lo:hi], roots[:, lo:hi], ACT.Square)
             if c == 0:
-                for lo, hi in runs:
-                    if lo == 0:
-                        continue
-                    nc.gpsimd.tensor_tensor(gains[c][:, lo:hi], gains[c][:, lo:hi], wgs_sb[:, lo:hi], ALU.mult)
-            elif c < LAST:
-                for hf, (lo, hi) in list(enumerate(runs))[:: -1 if c in SQUARE_ON_GPSIMD else 1]:
-                    at = MOVED_AT[hf] if c > 1 else FIRST_MOVED_AT[hf]
-                    moved[c, hf] = shared.tile([P, BANK], F32, name=f"gains_moved{c}_{hf}", offset=at)
+                pass
+            elif c in VECTOR_PAGES:
+                for hf, (lo, hi) in enumerate(runs):
+                    moved[c, hf] = shared.tile([P, BANK], F32, name=f"gains_moved{c}_{hf}", offset=FIRST_MOVED_AT[hf])
                     nc.gpsimd.tensor_tensor(moved[c, hf][:], gains[c][:, lo:hi], wgs_sb[:, lo:hi], ALU.mult)
+            elif c < LAST:
+                moved[c] = shared.tile([P, S], F32, name=f"gains_moved{c}", offset=MOVED_AT[c == 3])
+                nc.gpsimd.tensor_tensor(moved[c][:], gains[c][:], wgs_sb[:], ALU.mult)
 
         def apply_gains(c, lo, hi, sums, values):
             if c in VECTOR_PAGES:
@@ -298,29 +316,32 @@ def tile_list_lag_rewind_features_kernel(
                 nc.sync.dma_start(out=rows[:], in_=snap[i * P : (i + 1) * P, :])
                 snap_sb.append(rows)
 
+        (a_lo, a_hi), (b_lo, b_hi), (c_lo, c_hi) = FIRST_RUNS
         for k in range(VECTOR_CHUNKS):
+            round_w1(k)
             quantize_w1(k)
-        for hf, runs in enumerate(([(0, QUARTER), (QUARTER, BANK)], [(BANK, S)])):
-            spread(0, hf)
-            make_gains(0, runs[::-1] if hf == 0 else runs)
-            motion(0, hf * BANK, (hf + 1) * BANK, motion_banks[hf])
-            if hf == 0:
-                values = ring4.tile([P, BANK], F32, name="values", tag="listed")
-            else:
-                quantize_w1(2)
-                values = shared.tile([P, BANK], F32, name="values_behind_w1", offset=RAW_AT + 4 * PACK * W1_CHUNKS[2][0])
-            for lo, hi in runs:
-                cols = slice(lo % BANK, lo % BANK + hi - lo)
-                apply_gains(0, lo, hi, motion_banks[hf][:, cols], values[:, cols])
-                scatter(0, lo, hi, values[:, cols])
+        make_gains(0, FIRST_RUNS[:2], banks[0:2])
+        first_gains = gains[0]
+        for (lo, hi), bank in zip(FIRST_RUNS[:2], banks[2:4]):
+            motion(0, lo, hi, bank)
+        values = ring4.tile([P, BANK], F32, name="values", tag="listed")
+        nc.vector.tensor_tensor(values[:, a_lo:a_hi], banks[2][:, :QUARTER], first_gains[:, a_lo:a_hi], ALU.mult)
+        nc.vector.tensor_tensor(first_gains[:, b_lo:b_hi], first_gains[:, b_lo:b_hi], wgs_sb[:, b_lo:b_hi], ALU.mult)
+        scatter(0, a_lo, a_hi, values[:, a_lo:a_hi])
+        nc.vector.tensor_tensor(values[:, b_lo:b_hi], banks[3][:, :QUARTER], first_gains[:, b_lo:b_hi], ALU.mult)
+        scatter(0, b_lo, b_hi, values[:, b_lo:b_hi])
+        gains[0] = shared.tile([P, S], F32, name="third_gains", offset=FIRST_ROOTS_AT - 2 * KIB)
+        make_gains(0, FIRST_RUNS[2:], banks[4:5])
+        motion(0, c_lo, c_hi, banks[5])
+        factor = shared.tile([P, BANK], F32, name="third_factor", offset=ROUNDED_AT[1])
+        nc.gpsimd.tensor_tensor(factor[:], gains[0][:, c_lo:c_hi], wgs_sb[:, c_lo:c_hi], ALU.mult)
+        values = ring4.tile([P, BANK], F32, name="values", tag="listed")
+        nc.vector.tensor_tensor(values[:], banks[5][:], factor[:], ALU.mult)
+        scatter(0, c_lo, c_hi, values[:])
 
         def make_values(c, a_banks):
             if c < LAST:
-                if c == 1:
-                    values = shared.tile([P, S], F32, name="values_behind_last_w1", offset=RAW_AT + 4 * PACK * W1_CHUNKS[3][0])
-                else:
-                    values = ring4.tile([P, S], F32, name="values", tag="listed")
-                pieces = [(0, S, values)]
+                pieces = [(0, S, ring4.tile([P, S], F32, name="values", tag="listed"))]
             else:
                 pieces = [(0, S, shared.tile([P, S], F32, name="last_values", offset=LAST_VALUES_AT))]
             for hf, (first, stop) in enumerate(halves):
@@ -331,26 +352,23 @@ def tile_list_lag_rewind_features_kernel(
                         apply_gains(c, a, b, a_banks[hf][:, a - first : b - first], values[:, a - lo : b - lo])
             if c not in VECTOR_PAGES:
                 values = pieces[0][2]
-                for hf, (lo, hi) in enumerate(halves):
-                    factor = moved[c, hf][:] if (c, hf) in moved else gains[c][:, lo:hi]
-                    nc.gpsimd.tensor_tensor(values[:, lo:hi], values[:, lo:hi], factor, ALU.mult)
+                nc.gpsimd.tensor_tensor(values[:], values[:], moved.get(c, gains[c])[:], ALU.mult)
             return pieces
 
         def page_gains(c):
-            for hf in range(2):
-                spread(c, hf)
-            make_gains(c, halves)
+            make_gains(c, halves, (banks[2], banks[4]) if c == 1 else spread_banks)
 
         def history_sums(c, groups):
             sums = product_banks if c == LAST - 2 else sum_banks
             open_sums(c, sums, groups)
             close_sums(c, sums, groups)
 
-        for c, a_banks in ((1, sum_banks[0:2]), (2, motion_banks)):
+        for c, a_banks in ((1, banks[6:8]), (2, motion_banks)):
             page_gains(c)
-            if c == 1:
-                quantize_w1(3)
             scatter(c, 0, S, make_values(c, a_banks)[0][2][:])
+            if c == 1:
+                round_w1(2)
+                quantize_w1(2)
         preload_second_stage()
 
         for c in range(LAST):
@@ -384,19 +402,11 @@ def tile_list_lag_rewind_features_kernel(
         open_sums(LAST, product_banks, range(GROUPS))
         scatter(LAST, 0, S, pieces[0][2][:])
 
-        last_turned, last_grouped = [], []
         for g in range(GROUPS):
             turn_into_sum(product_banks[g], g, pages[LAST % PAGE_TILES], False)
-            turned = keep.tile([P, 2, P, 2], BF16, name=f"last_turned{g}")
-            nc.scalar.copy(out=turned[:], in_=product_banks[g][:].rearrange("p (r u e) -> p u r e", u=2, e=2))
-            last_turned.append(turned)
+        last_turned = [keep.tile([P, 2, P, 2], BF16, name=f"last_turned{g}") for g in range(GROUPS)]
         for g in range(GROUPS):
-            words = last_turned[g][:].rearrange("p u r e -> p (u r e)").bitcast(F32)
-            for u in range(2):
-                nc.tensor.transpose(product_banks[g][:, u * P : (u + 1) * P], words[:, u * P : (u + 1) * P], ident[:])
-            grouped = keep.tile([P, P, 2], F32, name=f"last_grouped{g}", align_bytes=64)
-            nc.scalar.copy(out=grouped[:], in_=product_banks[g][:, : 2 * P].rearrange("p (u n) -> p n u", u=2))
-            last_grouped.append(grouped)
+            nc.scalar.copy(out=last_turned[g][:], in_=product_banks[g][:].rearrange("p (r u e) -> p u r e", u=2, e=2))
 
         z_w = shared.tile([P, GROUPS, PASSES, BANK], U32, name="z_w", align_bytes=64, offset=TABLE_AT)
         z_sc = keep.tile([P, GROUPS, PASSES, BANK], U8, name="z_sc", align_bytes=64)
@@ -414,8 +424,6 @@ def tile_list_lag_rewind_features_kernel(
                 z_w[:, g].rearrange("p a n -> p (a n)"), z_sc[:, g].rearrange("p a n -> p (a n)"),
                 z_grouped[g][:].rearrange("p a n u -> p (a n u)"),
             )
-        for g in range(GROUPS):
-            quantize(last_w[:, block_of(g)], last_sc[:, block_of(g)], last_grouped[g][:].rearrange("p n u -> p (n u)"))
 
         y_sb = [ring4.tile([P, T2], F32, name="y_sb", tag="rows") for i in range(N // P)]
 
@@ -431,12 +439,28 @@ def tile_list_lag_rewind_features_kernel(
             else:
                 nc.scalar.activation(y_sb[i][:, ticks_of(g)], bank[:], ACT.Copy, scale=lam_sb[:, i : i + 1])
 
-        for g in range(GROUPS):
-            bank = sum_banks[g]
+        def early_passes(g):
+            bank = banks[FIRST_Y_BANKS[g]]
             product(bank[:], w3_w[:, 0, :P], w3_sc[:, 0, :P], z_w[:, g, 0], z_sc[:, g, 0], True, False)
             product(bank[:], w3_early, w3_sc[:, 1, :P], z_w[:, g, 1], z_sc[:, g, 1], False, False)
+
+        def turn_last(g):
+            words = last_turned[g][:].rearrange("p u r e -> p (u r e)").bitcast(F32)
+            for u in range(2):
+                nc.tensor.transpose(banks[LAST_TURN_BANKS[g]][:, block_of(u)], words[:, block_of(u)], ident[:])
+
+        early_passes(0)
+        for g in range(1, GROUPS - 1):
+            early_passes(g)
+            turn_last(2 * g - 2)
+            turn_last(2 * g - 1)
+        early_passes(GROUPS - 1)
         for g in range(GROUPS):
-            bank = sum_banks[g]
+            grouped = keep.tile([P, P, 2], F32, name=f"last_grouped{g}", align_bytes=64)
+            nc.scalar.copy(out=grouped[:], in_=banks[LAST_TURN_BANKS[g]][:, : 2 * P].rearrange("p (u n) -> p n u", u=2))
+            quantize(last_w[:, block_of(g)], last_sc[:, block_of(g)], grouped[:].rearrange("p n u -> p (n u)"))
+        for g in range(GROUPS):
+            bank = banks[FIRST_Y_BANKS[g]]
             for k in range(BLOCKS):
                 product(
                     bank[:, block_of(k)], w3_last[:, k, :], w3_last_sc[:],
@@ -455,7 +479,7 @@ def tile_list_lag_rewind_features_kernel(
             )
         for i in range(1, N // P):
             for g in range(GROUPS):
-                bank = product_banks[g]
+                bank = banks[LATER_Y_BANKS[g]]
                 product(bank[:], w3_w[:, 0, block_of(i)], w3_sc[:, 0, block_of(i)], z_w[:, g, 0], z_sc[:, g, 0], True, False)
                 product(bank[:], w3_w[:, 1, block_of(i)], w3_sc[:, 1, block_of(i)], z_w[:, g, 1], z_sc[:, g, 1], False, True)
                 leave_bank(i, g, bank)

@@ -36,10 +36,11 @@ AHEAD = 3
 VECTOR_PAGES = (0, 1)
 W1_CHUNKS = ((0, 128), (128, 512), (512, 1024))
 VECTOR_CHUNKS = 2
-ROUNDED_BY_GPSIMD = (0, 2)
+ROUNDED_BY_SCALAR = (2,)
+G_RUNS = ((0, BANK), (BANK, S))
 TURN_PAIRS = (4, 6, 0, 2)
 TURNS_BEFORE = 2
-SQUARE_ON_GPSIMD = (5, 6, 7)
+SQUARE_ON_GPSIMD = (2, 6, 7)
 Y_ON_VECTOR = (1, 3)
 FIRST_Y_BANKS = (4, 5, 1, 3)
 LAST_TURN_BANKS = (6, 7, 0, 2)
@@ -158,11 +159,11 @@ def tile_list_lag_rewind_features_kernel(
         def round_w1(k):
             lo, hi = W1_CHUNKS[k]
             w1_rounded[k] = shared.tile([P, hi - lo, PACK], BF16, name=f"w1_rounded{k}", align_bytes=64, offset=ROUNDED_AT[k])
-            raw = w1_raw[k][:].rearrange("p t c -> p c t")
-            if k in ROUNDED_BY_GPSIMD:
-                nc.gpsimd.tensor_scalar(w1_rounded[k][:], raw, 1.0, 0.0, ALU.mult, ALU.add)
-            else:
-                nc.vector.tensor_copy(out=w1_rounded[k][:], in_=raw)
+            copy = nc.scalar.copy if k in ROUNDED_BY_SCALAR else nc.vector.tensor_copy
+            copy(
+                out=w1_rounded[k][:].rearrange("p (c i) t -> p c t i", i=PACK),
+                in_=w1_raw[k][:].rearrange("p t (c i) -> p c t i", i=PACK),
+            )
 
         def quantize_w1(k):
             lo, hi = W1_CHUNKS[k]
@@ -219,7 +220,8 @@ def tile_list_lag_rewind_features_kernel(
                     nc.gpsimd.tensor_tensor(moved[c, hf][:], gains[c][:, lo:hi], wgs_sb[:, lo:hi], ALU.mult)
             elif c < LAST:
                 moved[c] = shared.tile([P, S], F32, name=f"gains_moved{c}", offset=MOVED_AT[c == 3])
-                nc.gpsimd.tensor_tensor(moved[c][:], gains[c][:], wgs_sb[:], ALU.mult)
+                for lo, hi in G_RUNS[:: -1 if c in SQUARE_ON_GPSIMD else 1]:
+                    nc.gpsimd.tensor_tensor(moved[c][:, lo:hi], gains[c][:, lo:hi], wgs_sb[:, lo:hi], ALU.mult)
 
         def apply_gains(c, lo, hi, sums, values):
             if c in VECTOR_PAGES:
@@ -352,7 +354,8 @@ def tile_list_lag_rewind_features_kernel(
                         apply_gains(c, a, b, a_banks[hf][:, a - first : b - first], values[:, a - lo : b - lo])
             if c not in VECTOR_PAGES:
                 values = pieces[0][2]
-                nc.gpsimd.tensor_tensor(values[:], values[:], moved.get(c, gains[c])[:], ALU.mult)
+                for lo, hi in G_RUNS[:: -1 if c in SQUARE_ON_GPSIMD else 1]:
+                    nc.gpsimd.tensor_tensor(values[:, lo:hi], values[:, lo:hi], moved.get(c, gains[c])[:, lo:hi], ALU.mult)
             return pieces
 
         def page_gains(c):
@@ -366,7 +369,7 @@ def tile_list_lag_rewind_features_kernel(
         for c, a_banks in ((1, banks[6:8]), (2, motion_banks)):
             page_gains(c)
             scatter(c, 0, S, make_values(c, a_banks)[0][2][:])
-            if c == 1:
+            if c == 2:
                 round_w1(2)
                 quantize_w1(2)
         preload_second_stage()

@@ -37,6 +37,7 @@ VECTOR_PAGES = (0, 1)
 W1_CHUNKS = ((0, 128), (128, 512), (512, 1024))
 VECTOR_CHUNKS = 2
 ROUNDED_BY_SCALAR = (2,)
+NARROW_PAGES = (0, 1, 2)
 G_RUNS = ((0, BANK), (BANK, S))
 TURN_PAIRS = (4, 6, 0, 2)
 TURNS_BEFORE = 2
@@ -53,8 +54,8 @@ SLOTS_AT = (84 * KIB, 28 * KIB)
 GAINS_AT = (36 * KIB, 84 * KIB, 56 * KIB)
 SECOND_GAINS_AT = 26 * KIB
 FIRST_ROOTS_AT = 34 * KIB
-ROUNDED_AT = (30 * KIB, 16 * KIB, 26 * KIB)
-MOVED_AT = (32 * KIB, 26 * KIB)
+ROUNDED_AT = (30 * KIB, 16 * KIB, 92 * KIB)
+MOVED_AT = (32 * KIB, 92 * KIB)
 FIRST_MOVED_AT = (20 * KIB, 22 * KIB)
 RAW_AT = 40 * KIB
 PAGES_AT = 60 * KIB
@@ -200,28 +201,29 @@ def tile_list_lag_rewind_features_kernel(
             for (lo, hi), bank in zip(runs, b_banks):
                 spread(c, lo, hi, bank)
                 nc.scalar.activation(gains[c][:, lo:hi], bank[:, : hi - lo], ACT.Abs)
-            wide = runs if c in VECTOR_PAGES else [(0, S)]
+            wide = runs if c in NARROW_PAGES else [(0, S)]
             roots = gains[c]
             if runs == FIRST_RUNS[:2]:
                 roots = shared.tile([P, BANK], F32, name="first_roots", offset=FIRST_ROOTS_AT)
             for lo, hi in wide:
                 nc.scalar.activation(roots[:, lo:hi], gains[c][:, lo:hi], ACT.Abs_reciprocal_sqrt, bias=half[:])
+            if c not in VECTOR_PAGES and c < LAST:
+                moved[c] = shared.tile([P, S], F32, name=f"gains_moved{c}", offset=MOVED_AT[c == 2])
+            squares = [gains[c][:, :BANK], gains[c][:, BANK:]]
             if c in SQUARE_ON_GPSIMD:
-                nc.gpsimd.tensor_tensor(gains[c][:, :BANK], gains[c][:, :BANK], gains[c][:, :BANK], ALU.mult)
+                squares[0] = moved.get(c, gains[c])[:, :BANK]
+                nc.gpsimd.tensor_tensor(squares[0], gains[c][:, :BANK], gains[c][:, :BANK], ALU.mult)
                 nc.scalar.activation(gains[c][:, BANK:], gains[c][:, BANK:], ACT.Square)
             else:
                 for lo, hi in wide:
                     nc.scalar.activation(gains[c][:, lo:hi], roots[:, lo:hi], ACT.Square)
-            if c == 0:
-                pass
-            elif c in VECTOR_PAGES:
+            if c == 1:
                 for hf, (lo, hi) in enumerate(runs):
                     moved[c, hf] = shared.tile([P, BANK], F32, name=f"gains_moved{c}_{hf}", offset=FIRST_MOVED_AT[hf])
                     nc.gpsimd.tensor_tensor(moved[c, hf][:], gains[c][:, lo:hi], wgs_sb[:, lo:hi], ALU.mult)
-            elif c < LAST:
-                moved[c] = shared.tile([P, S], F32, name=f"gains_moved{c}", offset=MOVED_AT[c == 3])
-                for lo, hi in G_RUNS[:: -1 if c in SQUARE_ON_GPSIMD else 1]:
-                    nc.gpsimd.tensor_tensor(moved[c][:, lo:hi], gains[c][:, lo:hi], wgs_sb[:, lo:hi], ALU.mult)
+            elif c in moved:
+                for hf in (1, 0) if c in SQUARE_ON_GPSIMD else (0, 1):
+                    nc.gpsimd.tensor_tensor(moved[c][:, half_of(hf)], squares[hf], wgs_sb[:, half_of(hf)], ALU.mult)
 
         def apply_gains(c, lo, hi, sums, values):
             if c in VECTOR_PAGES:
@@ -343,7 +345,11 @@ def tile_list_lag_rewind_features_kernel(
 
         def make_values(c, a_banks):
             if c < LAST:
-                pieces = [(0, S, ring4.tile([P, S], F32, name="values", tag="listed"))]
+                if c == 1:
+                    values = shared.tile([P, S], F32, name="values_behind_w1", offset=RAW_AT + 4 * PACK * W1_CHUNKS[2][0])
+                else:
+                    values = ring4.tile([P, S], F32, name="values", tag="listed")
+                pieces = [(0, S, values)]
             else:
                 pieces = [(0, S, shared.tile([P, S], F32, name="last_values", offset=LAST_VALUES_AT))]
             for hf, (first, stop) in enumerate(halves):
@@ -368,10 +374,10 @@ def tile_list_lag_rewind_features_kernel(
 
         for c, a_banks in ((1, banks[6:8]), (2, motion_banks)):
             page_gains(c)
-            scatter(c, 0, S, make_values(c, a_banks)[0][2][:])
-            if c == 2:
+            if c == 1:
                 round_w1(2)
                 quantize_w1(2)
+            scatter(c, 0, S, make_values(c, a_banks)[0][2][:])
         preload_second_stage()
 
         for c in range(LAST):

@@ -23,7 +23,7 @@ PACK = 4
 PER_COLUMN = 16
 BANK = 512
 QUARTER = 256
-FIRST_RUNS = ((0, QUARTER), (QUARTER, BANK), (BANK, S))
+FIRST_RUNS = ((QUARTER, BANK), (0, QUARTER), (BANK, S))
 PAGES = H // P
 LAST = PAGES - 1
 PAGES_PER_PASS = PACK
@@ -34,9 +34,9 @@ BLOCKS = BANK // P
 PAGE_TILES = 3
 AHEAD = 3
 VECTOR_PAGES = (0, 1)
-W1_CHUNKS = ((0, 128), (128, 512), (512, 1024))
-VECTOR_CHUNKS = 2
-ROUNDED_BY_SCALAR = (2,)
+W1_LOADS = ((0, 128), (128, 512), (512, 1024))
+W1_CHUNKS = ((0, 128), (128, 256), (256, 512), (512, 1024))
+ROUNDED_BY_SCALAR = (3,)
 NARROW_PAGES = (0, 1, 2)
 G_RUNS = ((0, BANK), (BANK, S))
 TURN_PAIRS = (4, 6, 0, 2)
@@ -50,12 +50,13 @@ KIB = 1024
 TABLE_AT = 0
 TABLE_SCALES_AT = 16 * KIB
 LAST_VALUES_AT = 16 * KIB
-SLOTS_AT = (84 * KIB, 28 * KIB)
-GAINS_AT = (36 * KIB, 84 * KIB, 56 * KIB)
-SECOND_GAINS_AT = 26 * KIB
+SLOTS_AT = (20 * KIB, 28 * KIB)
+GAINS_AT = (36 * KIB, 26 * KIB, 56 * KIB)
 FIRST_ROOTS_AT = 34 * KIB
-ROUNDED_AT = (30 * KIB, 16 * KIB, 92 * KIB)
-MOVED_AT = (32 * KIB, 92 * KIB)
+ROUNDED_AT = (30 * KIB, 16 * KIB, 21 * KIB, 84 * KIB)
+W1_CODES_AT = {1: 36 * KIB, 2: 34 * KIB}
+THIRD_FACTOR_AT = 15 * KIB
+MOVED_AT = (32 * KIB, 84 * KIB)
 FIRST_MOVED_AT = (20 * KIB, 22 * KIB)
 RAW_AT = 40 * KIB
 PAGES_AT = 60 * KIB
@@ -78,8 +79,8 @@ def tile_list_lag_rewind_features_kernel(
         spread_banks, motion_banks = banks[0:2], banks[2:4]
 
         def load_scale_rows(plane, rows):
-            for q in range(4):
-                nc.sync.dma_start(out=plane[32 * q : 32 * q + 4].bitcast(I32), in_=rows(q).bitcast(I32))
+            for r in range(4):
+                nc.sync.dma_start(out=plane[r:P:QUAD].bitcast(I32), in_=rows[r:16:4].bitcast(I32))
 
         def load_list(name, source):
             offsets = keep.tile([P, S // PER_COLUMN], U16, name=name)
@@ -101,21 +102,21 @@ def tile_list_lag_rewind_features_kernel(
         w1_raw = []
 
         def load_w1(k):
-            lo, hi = W1_CHUNKS[k]
+            lo, hi = W1_LOADS[k]
             raw = shared.tile([P, PACK, hi - lo], F32, name=f"w1_raw{k}", offset=RAW_AT + 4 * PACK * lo)
             nc.sync.dma_start(out=raw[:], in_=w1_rows[:, :, lo:hi])
             w1_raw.append(raw)
 
-        idx = load_list("idx", offs)
         tab_w = shared.tile([P, T], I32, name="tab_w", offset=TABLE_AT)
         tab_rows = tab_words[0].rearrange("p c t -> p (c t)").bitcast(I32)
         nc.sync.dma_start(out=tab_w[:, : T // 4], in_=tab_rows[:, : T // 4])
-        load_scale_rows(tab_sc, lambda q: tab_scales[0, 4 * q : 4 * q + 4, :])
+        idx = load_list("idx", offs)
+        load_scale_rows(tab_sc, tab_scales[0])
         nc.sync.dma_start(out=tab_w[:, T // 4 :], in_=tab_rows[:, T // 4 :])
         w2_w = keep.tile([P, 2 * H], U8, name="w2_w", align_bytes=64)
         w2_rows = w2_words[0].bitcast(I32)
         nc.sync.dma_start(out=w2_w[:].bitcast(I32)[:, :P], in_=w2_rows[:, :P])
-        load_scale_rows(w2_sc, lambda q: w2_scales[0, 4 * q : 4 * q + 4, :])
+        load_scale_rows(w2_sc, w2_scales[0])
         load_w1(0)
         load_w1(1)
         wgs_sb = keep.tile([P, S], F32, name="wgs_sb")
@@ -160,15 +161,19 @@ def tile_list_lag_rewind_features_kernel(
         def round_w1(k):
             lo, hi = W1_CHUNKS[k]
             w1_rounded[k] = shared.tile([P, hi - lo, PACK], BF16, name=f"w1_rounded{k}", align_bytes=64, offset=ROUNDED_AT[k])
+            first, raw = [(a, tile) for (a, b), tile in zip(W1_LOADS, w1_raw) if a <= lo < b][0]
             copy = nc.scalar.copy if k in ROUNDED_BY_SCALAR else nc.vector.tensor_copy
             copy(
                 out=w1_rounded[k][:].rearrange("p (c i) t -> p c t i", i=PACK),
-                in_=w1_raw[k][:].rearrange("p t (c i) -> p c t i", i=PACK),
+                in_=raw[:, :, lo - first : hi - first].rearrange("p t (c i) -> p c t i", i=PACK),
             )
 
         def quantize_w1(k):
             lo, hi = W1_CHUNKS[k]
-            words = keep.tile([P, hi - lo], U32, name=f"w1_w{k}", align_bytes=64)
+            if k in W1_CODES_AT:
+                words = shared.tile([P, hi - lo], U32, name=f"w1_w{k}", align_bytes=64, offset=W1_CODES_AT[k])
+            else:
+                words = keep.tile([P, hi - lo], U32, name=f"w1_w{k}", align_bytes=64)
             scales = keep.tile([P, hi - lo], U8, name=f"w1_sc{k}", align_bytes=64)
             nc.vector.quantize_mx(
                 out=words[:].bitcast(FP8X4), scales=scales[:], in_=w1_rounded[k][:].rearrange("p c t -> p (c t)")
@@ -197,7 +202,7 @@ def tile_list_lag_rewind_features_kernel(
 
         def make_gains(c, runs, b_banks):
             if c not in gains:
-                gains[c] = shared.tile([P, S], F32, name=f"gains{c}", offset=SECOND_GAINS_AT if c == 1 else GAINS_AT[c % len(GAINS_AT)])
+                gains[c] = shared.tile([P, S], F32, name=f"gains{c}", offset=GAINS_AT[c % len(GAINS_AT)])
             for (lo, hi), bank in zip(runs, b_banks):
                 spread(c, lo, hi, bank)
                 nc.scalar.activation(gains[c][:, lo:hi], bank[:, : hi - lo], ACT.Abs)
@@ -305,11 +310,12 @@ def tile_list_lag_rewind_features_kernel(
 
         def preload_second_stage():
             nc.sync.dma_start(out=w3_w[:], in_=w3_words.rearrange("a p c t -> p a (c t)").bitcast(I32))
-            load_scale_rows(w3_sc, lambda q: w3_scales[:, 4 * q : 4 * q + 4, :].rearrange("a q n -> q a n"))
+            load_scale_rows(w3_sc, w3_scales.rearrange("a q n -> q a n"))
             second = w3_words[1].rearrange("p c t -> p (c t)").bitcast(I32)
             for k in range(BLOCKS):
                 nc.sync.dma_start(out=w3_last[QUAD * k : QUAD * (k + 1), k, :], in_=second[EARLY:, :P])
-            load_scale_rows(w3_last_sc, lambda q: w3_scales[1, 12:16, :P])
+            for k in range(BLOCKS):
+                nc.sync.dma_start(out=w3_last_sc[QUAD * k : QUAD * k + 4].bitcast(I32), in_=w3_scales[1, 12:16, :P].bitcast(I32))
             nc.sync.dma_start(out=w3_early[:EARLY], in_=second[:EARLY, :P])
             nc.sync.dma_start(out=wgo_sb[:], in_=wgo)
             late_lists.extend([load_list("idx3", offs3), load_list("idx4", offs4)])
@@ -320,33 +326,36 @@ def tile_list_lag_rewind_features_kernel(
                 nc.sync.dma_start(out=rows[:], in_=snap[i * P : (i + 1) * P, :])
                 snap_sb.append(rows)
 
-        (a_lo, a_hi), (b_lo, b_hi), (c_lo, c_hi) = FIRST_RUNS
-        for k in range(VECTOR_CHUNKS):
-            round_w1(k)
-            quantize_w1(k)
+        (b_lo, b_hi), (a_lo, a_hi), (c_lo, c_hi) = FIRST_RUNS
+        round_w1(0)
+        quantize_w1(0)
+        round_w1(1)
+        round_w1(2)
         make_gains(0, FIRST_RUNS[:2], banks[0:2])
         first_gains = gains[0]
-        for (lo, hi), bank in zip(FIRST_RUNS[:2], banks[2:4]):
-            motion(0, lo, hi, bank)
+        motion(0, a_lo, a_hi, banks[2])
+        motion(0, b_lo, b_hi, banks[3])
         values = ring4.tile([P, BANK], F32, name="values", tag="listed")
-        nc.vector.tensor_tensor(values[:, a_lo:a_hi], banks[2][:, :QUARTER], first_gains[:, a_lo:a_hi], ALU.mult)
         nc.vector.tensor_tensor(first_gains[:, b_lo:b_hi], first_gains[:, b_lo:b_hi], wgs_sb[:, b_lo:b_hi], ALU.mult)
-        scatter(0, a_lo, a_hi, values[:, a_lo:a_hi])
+        nc.vector.tensor_tensor(values[:, a_lo:a_hi], banks[2][:, :QUARTER], first_gains[:, a_lo:a_hi], ALU.mult)
         nc.vector.tensor_tensor(values[:, b_lo:b_hi], banks[3][:, :QUARTER], first_gains[:, b_lo:b_hi], ALU.mult)
+        scatter(0, a_lo, a_hi, values[:, a_lo:a_hi])
+        quantize_w1(1)
         scatter(0, b_lo, b_hi, values[:, b_lo:b_hi])
         gains[0] = shared.tile([P, S], F32, name="third_gains", offset=FIRST_ROOTS_AT - 2 * KIB)
         make_gains(0, FIRST_RUNS[2:], banks[4:5])
         motion(0, c_lo, c_hi, banks[5])
-        factor = shared.tile([P, BANK], F32, name="third_factor", offset=ROUNDED_AT[1])
+        factor = shared.tile([P, BANK], F32, name="third_factor", offset=THIRD_FACTOR_AT)
         nc.gpsimd.tensor_tensor(factor[:], gains[0][:, c_lo:c_hi], wgs_sb[:, c_lo:c_hi], ALU.mult)
         values = ring4.tile([P, BANK], F32, name="values", tag="listed")
         nc.vector.tensor_tensor(values[:], banks[5][:], factor[:], ALU.mult)
+        quantize_w1(2)
         scatter(0, c_lo, c_hi, values[:])
 
         def make_values(c, a_banks):
             if c < LAST:
                 if c == 1:
-                    values = shared.tile([P, S], F32, name="values_behind_w1", offset=RAW_AT + 4 * PACK * W1_CHUNKS[2][0])
+                    values = shared.tile([P, S], F32, name="values_behind_w1", offset=RAW_AT + 4 * PACK * W1_LOADS[2][0])
                 else:
                     values = ring4.tile([P, S], F32, name="values", tag="listed")
                 pieces = [(0, S, values)]
@@ -375,8 +384,8 @@ def tile_list_lag_rewind_features_kernel(
         for c, a_banks in ((1, banks[6:8]), (2, motion_banks)):
             page_gains(c)
             if c == 1:
-                round_w1(2)
-                quantize_w1(2)
+                round_w1(3)
+                quantize_w1(3)
             scatter(c, 0, S, make_values(c, a_banks)[0][2][:])
         preload_second_stage()
 

@@ -22,6 +22,7 @@ QUAD = 32
 PACK = 4
 PER_COLUMN = 16
 BANK = 512
+FIRST_COLUMNS = 3 * T // 8
 QUARTER = 256
 FIRST_RUNS = ((QUARTER, BANK), (0, QUARTER), (BANK, S))
 PAGES = H // P
@@ -109,10 +110,10 @@ def tile_list_lag_rewind_features_kernel(
 
         tab_w = shared.tile([P, T], I32, name="tab_w", offset=TABLE_AT)
         tab_rows = tab_words[0].rearrange("p c t -> p (c t)").bitcast(I32)
-        nc.sync.dma_start(out=tab_w[:, : T // 4], in_=tab_rows[:, : T // 4])
+        nc.sync.dma_start(out=tab_w[:, : FIRST_COLUMNS], in_=tab_rows[:, : FIRST_COLUMNS])
         idx = load_list("idx", offs)
         load_scale_rows(tab_sc, tab_scales[0])
-        nc.sync.dma_start(out=tab_w[:, T // 4 :], in_=tab_rows[:, T // 4 :])
+        nc.sync.dma_start(out=tab_w[:, FIRST_COLUMNS :], in_=tab_rows[:, FIRST_COLUMNS :])
         w2_w = keep.tile([P, 2 * H], U8, name="w2_w", align_bytes=64)
         w2_rows = w2_words[0].bitcast(I32)
         nc.sync.dma_start(out=w2_w[:].bitcast(I32)[:, :P], in_=w2_rows[:, :P])

@@ -42,7 +42,7 @@ NARROW_PAGES = (0, 1, 2)
 G_RUNS = ((0, BANK), (BANK, S))
 TURN_PAIRS = (4, 6, 0, 2)
 TURNS_BEFORE = 2
-SQUARE_ON_GPSIMD = (2, 6, 7)
+SQUARE_ON_GPSIMD = (2, 4, 6, 7)
 Y_ON_VECTOR = (1, 3)
 FIRST_Y_BANKS = (4, 5, 1, 3)
 LAST_TURN_BANKS = (6, 7, 0, 2)
@@ -521,6 +521,7 @@ def tile_list_lag_rewind_features_kernel(
             nc.vector.tensor_tensor(slots[i % 2][:].indirect(idx4[:]), picked[i][:], wgo_sb[:], ALU.mult)
             for hf in range(2):
                 cols = slice(hf * T2 // 2, (hf + 1) * T2 // 2)
-                nc.sync.dma_start(out=out[i * P : (i + 1) * P, cols], in_=slots[i % 2][:, cols])
+                queue = nc.scalar if hf and i == N // P - 1 else nc.sync
+                queue.dma_start(out=out[i * P : (i + 1) * P, cols], in_=slots[i % 2][:, cols])
             if i == 0:
                 pick(1)

@@ -42,7 +42,7 @@ NARROW_PAGES = (0, 1, 2)
 G_RUNS = ((0, BANK), (BANK, S))
 TURN_PAIRS = (4, 6, 0, 2)
 TURNS_BEFORE = 2
-SQUARE_ON_GPSIMD = (2, 4, 6, 7)
+SQUARE_ON_GPSIMD = (3, 5, 6, 7)
 Y_ON_VECTOR = (1, 3)
 FIRST_Y_BANKS = (4, 5, 1, 3)
 LAST_TURN_BANKS = (6, 7, 0, 2)
@@ -386,8 +386,10 @@ def tile_list_lag_rewind_features_kernel(
             page_gains(c)
             if c == 1:
                 round_w1(3)
+            values = make_values(c, a_banks)[0][2]
+            if c == 1:
                 quantize_w1(3)
-            scatter(c, 0, S, make_values(c, a_banks)[0][2][:])
+            scatter(c, 0, S, values[:])
         preload_second_stage()
 
         for c in range(LAST):
@@ -468,12 +470,12 @@ def tile_list_lag_rewind_features_kernel(
             for u in range(2):
                 nc.tensor.transpose(banks[LAST_TURN_BANKS[g]][:, block_of(u)], words[:, block_of(u)], ident[:])
 
-        early_passes(0)
-        for g in range(1, GROUPS - 1):
+        for g in range(2):
             early_passes(g)
-            turn_last(2 * g - 2)
-            turn_last(2 * g - 1)
-        early_passes(GROUPS - 1)
+            turn_last(2 * g)
+            turn_last(2 * g + 1)
+        for g in range(2, GROUPS):
+            early_passes(g)
         for g in range(GROUPS):
             grouped = keep.tile([P, P, 2], F32, name=f"last_grouped{g}", align_bytes=64)
             nc.scalar.copy(out=grouped[:], in_=banks[LAST_TURN_BANKS[g]][:, : 2 * P].rearrange("p (u n) -> p n u", u=2))

@@ -498,10 +498,11 @@ def tile_list_lag_rewind_features_kernel(
                 out=z_sc[EARLY : EARLY + 4, :, 1, block_of(k)].bitcast(I32),
                 in_=last_sc[QUAD * k : QUAD * k + 4].bitcast(I32).rearrange("p (g n) -> p g n", g=GROUPS),
             )
-        for i in range(1, N // P):
-            for g in range(GROUPS):
-                bank = banks[LATER_Y_BANKS[g]]
+        for tiles in ((1, 2), (3,)):
+            later = [(i, g, banks[(FIRST_Y_BANKS, LATER_Y_BANKS)[i % 2][g]]) for i in tiles for g in range(GROUPS)]
+            for i, g, bank in later:
                 product(bank[:], w3_w[:, 0, block_of(i)], w3_sc[:, 0, block_of(i)], z_w[:, g, 0], z_sc[:, g, 0], True, False)
+            for i, g, bank in later:
                 product(bank[:], w3_w[:, 1, block_of(i)], w3_sc[:, 1, block_of(i)], z_w[:, g, 1], z_sc[:, g, 1], False, True)
                 leave_bank(i, g, bank)
 

from contextlib import ExitStack

import concourse.mybir as mybir
from concourse.masks import make_identity

K, H, N, T, S, T2, M = 512, 1024, 512, 4096, 1024, 2048, 1024
FLOPS = 2 * (2 * K * H * S + H * N * T2)

F32 = mybir.dt.float32
BF16 = mybir.dt.bfloat16
I32 = mybir.dt.int32
U32 = mybir.dt.uint32
U16 = mybir.dt.uint16
U8 = mybir.dt.uint8
FP8X4 = mybir.dt.float8_e4m3fn_x4
FP4X4 = mybir.dt.float4_e2m1fn_x4
ACT = mybir.ActivationFunctionType
ALU = mybir.AluOpType

P = 128
QUAD = 32
PACK = 4
PER_COLUMN = 16
BANK = 512
FIRST_COLUMNS = 3 * T // 8
QUARTER = 256
FIRST_RUNS = ((QUARTER, BANK), (0, QUARTER), (BANK, S))
PAGES = H // P
LAST = PAGES - 1
PAGES_PER_PASS = PACK
PASSES = PAGES // PAGES_PER_PASS
EARLY = P - QUAD
GROUPS = T2 // BANK
BLOCKS = BANK // P
PAGE_TILES = 3
AHEAD = 3
VECTOR_PAGES = (0, 1)
W1_LOADS = ((0, 128), (128, 512), (512, 1024))
W1_CHUNKS = ((0, 128), (128, 256), (256, 512), (512, 1024))
ROUNDED_BY_SCALAR = (3,)
NARROW_PAGES = (0, 1, 2)
G_RUNS = ((0, BANK), (BANK, S))
TURN_PAIRS = (4, 6, 0, 2)
TURNS_BEFORE = 2
SQUARE_ON_GPSIMD = (3, 5, 6, 7)
Y_ON_VECTOR = (1, 3)
FIRST_Y_BANKS = (4, 5, 1, 3)
LAST_TURN_BANKS = (6, 7, 0, 2)
LATER_Y_BANKS = (6, 7, 0, 2)
KIB = 1024
TABLE_AT = 0
TABLE_SCALES_AT = 16 * KIB
LAST_VALUES_AT = 16 * KIB
SLOTS_AT = (20 * KIB, 28 * KIB)
GAINS_AT = (36 * KIB, 26 * KIB, 56 * KIB)
FIRST_ROOTS_AT = 34 * KIB
ROUNDED_AT = (30 * KIB, 16 * KIB, 21 * KIB, 84 * KIB)
W1_CODES_AT = {1: 36 * KIB, 2: 34 * KIB}
THIRD_FACTOR_AT = 15 * KIB
MOVED_AT = (32 * KIB, 84 * KIB)
FIRST_MOVED_AT = (20 * KIB, 22 * KIB)
RAW_AT = 40 * KIB
PAGES_AT = 60 * KIB
PICKS_AT = {1: 0, 2: 4 * KIB}


def tile_list_lag_rewind_features_kernel(
    tc, tab_words, tab_scales, offs, offs2, offs3, offs4, w1, w2_words, w2_scales,
    wgs, hist, w3_words, w3_scales, lam, snap, wgo, out,
):
    nc = tc.nc
    with ExitStack() as ctx:
        keep = ctx.enter_context(tc.tile_pool(name="keep", bufs=1))
        shared = ctx.enter_context(tc.tile_pool(name="shared", bufs=1))
        ring4 = ctx.enter_context(tc.tile_pool(name="ring4", bufs=4))
        psum = ctx.enter_context(tc.psum_pool(name="psum", bufs=1))

        banks = [psum.tile([P, BANK], F32, name=f"bank{i}") for i in range(8)]
        product_banks, sum_banks = banks[0:4], banks[4:8]
        spread_banks, motion_banks = banks[0:2], banks[2:4]

        def load_scale_rows(plane, rows):
            for r in range(4):
                nc.sync.dma_start(out=plane[r:P:QUAD].bitcast(I32), in_=rows[r:16:4].bitcast(I32))

        def load_list(name, source):
            offsets = keep.tile([P, S // PER_COLUMN], U16, name=name)
            nc.sync.dma_start(offsets[:], source)
            return offsets

        def entries(offsets, lo, hi):
            return offsets[:, lo // PER_COLUMN : hi // PER_COLUMN]

        def half_of(hf):
            return slice(hf * BANK, (hf + 1) * BANK)

        tab_sc = shared.tile([P, T], U8, name="tab_sc", align_bytes=64, offset=TABLE_SCALES_AT)
        nc.vector.memset(tab_sc[:].bitcast(I32), 0)
        w2_sc = keep.tile([P, H], U8, name="w2_sc", align_bytes=64)
        nc.gpsimd.memset(w2_sc[:].bitcast(I32), 0)

        w1_rows = w1.rearrange("(p t) c -> p t c", t=PACK)
        w1_raw = []

        def load_w1(k):
            lo, hi = W1_LOADS[k]
            raw = shared.tile([P, PACK, hi - lo], F32, name=f"w1_raw{k}", offset=RAW_AT + 4 * PACK * lo)
            nc.sync.dma_start(out=raw[:], in_=w1_rows[:, :, lo:hi])
            w1_raw.append(raw)

        tab_w = shared.tile([P, T], I32, name="tab_w", offset=TABLE_AT)
        tab_rows = tab_words[0].rearrange("p c t -> p (c t)").bitcast(I32)
        nc.sync.dma_start(out=tab_w[:, : FIRST_COLUMNS], in_=tab_rows[:, : FIRST_COLUMNS])
        idx = load_list("idx", offs)
        load_scale_rows(tab_sc, tab_scales[0])
        nc.sync.dma_start(out=tab_w[:, FIRST_COLUMNS :], in_=tab_rows[:, FIRST_COLUMNS :])
        w2_w = keep.tile([P, 2 * H], U8, name="w2_w", align_bytes=64)
        w2_rows = w2_words[0].bitcast(I32)
        nc.sync.dma_start(out=w2_w[:].bitcast(I32)[:, :P], in_=w2_rows[:, :P])
        load_scale_rows(w2_sc, w2_scales[0])
        load_w1(0)
        load_w1(1)
        wgs_sb = keep.tile([P, S], F32, name="wgs_sb")
        nc.sync.dma_start(out=wgs_sb[:, half_of(0)], in_=wgs[:, half_of(0)])
        idx2 = load_list("idx2", offs2)
        nc.sync.dma_start(out=wgs_sb[:, half_of(1)], in_=wgs[:, half_of(1)])
        nc.sync.dma_start(out=w2_w[:].bitcast(I32)[:, P:], in_=w2_rows[:, P:])
        load_w1(2)

        half = keep.tile([P, 1], F32, name="half")
        nc.gpsimd.memset(half[:], 0.5)
        warm = keep.tile([P, 1], F32, name="warm")
        nc.scalar.activation(warm[:], half[:], ACT.Abs_reciprocal_sqrt)
        ident = keep.tile([P, P], F32, name="ident")
        make_identity(nc, ident[:])
        w3_sc = keep.tile([P, PASSES, N], U8, name="w3_sc", align_bytes=64)
        nc.gpsimd.memset(w3_sc[:].rearrange("p a n -> p (a n)").bitcast(I32), 0)

        pages = [shared.tile([P, T2], F32, name=f"page{i}", offset=PAGES_AT + 4 * T2 * i) for i in range(PAGE_TILES)]
        for page in pages[:-1]:
            nc.vector.memset(page[:], 0.0)
        nc.gpsimd.memset(pages[-1][:], 0.0)

        hist_sb = []

        def load_hist(c):
            rows = ring4.tile([P, T2], F32, name="hist_sb", tag="rows")
            nc.sync.dma_start(out=rows[:], in_=hist[c * P : (c + 1) * P, :])
            hist_sb.append(rows)

        for c in range(PAGES_PER_PASS):
            load_hist(c)

        v_sc = keep.tile([P, S], U8, name="v_sc", align_bytes=64)
        nc.vector.tensor_copy(v_sc[:], tab_sc[:].indirect(idx[:]))
        v_w = keep.tile([P, S], U32, name="v_w", align_bytes=64)
        for lo, hi in FIRST_RUNS:
            nc.vector.tensor_copy(v_w[:, lo:hi], tab_w[:].bitcast(U32).indirect(entries(idx, lo, hi)))

        w1_rounded, w1_w, w1_sc = {}, {}, {}

        def round_w1(k):
            lo, hi = W1_CHUNKS[k]
            w1_rounded[k] = shared.tile([P, hi - lo, PACK], BF16, name=f"w1_rounded{k}", align_bytes=64, offset=ROUNDED_AT[k])
            first, raw = [(a, tile) for (a, b), tile in zip(W1_LOADS, w1_raw) if a <= lo < b][0]
            copy = nc.scalar.copy if k in ROUNDED_BY_SCALAR else nc.vector.tensor_copy
            copy(
                out=w1_rounded[k][:].rearrange("p (c i) t -> p c t i", i=PACK),
                in_=raw[:, :, lo - first : hi - first].rearrange("p t (c i) -> p c t i", i=PACK),
            )

        def quantize_w1(k):
            lo, hi = W1_CHUNKS[k]
            if k in W1_CODES_AT:
                words = shared.tile([P, hi - lo], U32, name=f"w1_w{k}", align_bytes=64, offset=W1_CODES_AT[k])
            else:
                words = keep.tile([P, hi - lo], U32, name=f"w1_w{k}", align_bytes=64)
            scales = keep.tile([P, hi - lo], U8, name=f"w1_sc{k}", align_bytes=64)
            nc.vector.quantize_mx(
                out=words[:].bitcast(FP8X4), scales=scales[:], in_=w1_rounded[k][:].rearrange("p c t -> p (c t)")
            )
            for c in range(lo // P, hi // P):
                w1_w[c], w1_sc[c] = words[:, c * P - lo : (c + 1) * P - lo], scales[:, c * P - lo : (c + 1) * P - lo]

        def spread(c, lo, hi, bank):
            nc.tensor.matmul_mx(
                out=bank[:, : hi - lo],
                lhsT=w2_w[:, 2 * c * P : 2 * (c + 1) * P].bitcast(FP4X4),
                lhsT_scale=w2_sc[:, c * P : (c + 1) * P],
                rhs=v_w[:, lo:hi].bitcast(FP8X4), rhs_scale=v_sc[:, lo:hi],
                start=True, stop=True,
            )

        def motion(c, lo, hi, bank):
            nc.tensor.matmul_mx(
                out=bank[:, : hi - lo],
                lhsT=w1_w[c].bitcast(FP8X4), lhsT_scale=w1_sc[c],
                rhs=v_w[:, lo:hi].bitcast(FP8X4), rhs_scale=v_sc[:, lo:hi],
                start=True, stop=True,
            )

        gains, moved = {}, {}

        def make_gains(c, runs, b_banks):
            if c not in gains:
                gains[c] = shared.tile([P, S], F32, name=f"gains{c}", offset=GAINS_AT[c % len(GAINS_AT)])
            for (lo, hi), bank in zip(runs, b_banks):
                spread(c, lo, hi, bank)
                nc.scalar.activation(gains[c][:, lo:hi], bank[:, : hi - lo], ACT.Abs)
            wide = runs if c in NARROW_PAGES else [(0, S)]
            roots = gains[c]
            if runs == FIRST_RUNS[:2]:
                roots = shared.tile([P, BANK], F32, name="first_roots", offset=FIRST_ROOTS_AT)
            for lo, hi in wide:
                nc.scalar.activation(roots[:, lo:hi], gains[c][:, lo:hi], ACT.Abs_reciprocal_sqrt, bias=half[:])
            if c not in VECTOR_PAGES and c < LAST:
                moved[c] = shared.tile([P, S], F32, name=f"gains_moved{c}", offset=MOVED_AT[c == 2])
            squares = [gains[c][:, :BANK], gains[c][:, BANK:]]
            if c in SQUARE_ON_GPSIMD:
                squares[0] = moved.get(c, gains[c])[:, :BANK]
                nc.gpsimd.tensor_tensor(squares[0], gains[c][:, :BANK], gains[c][:, :BANK], ALU.mult)
                nc.scalar.activation(gains[c][:, BANK:], gains[c][:, BANK:], ACT.Square)
            else:
                for lo, hi in wide:
                    nc.scalar.activation(gains[c][:, lo:hi], roots[:, lo:hi], ACT.Square)
            if c == 1:
                for hf, (lo, hi) in enumerate(runs):
                    moved[c, hf] = shared.tile([P, BANK], F32, name=f"gains_moved{c}_{hf}", offset=FIRST_MOVED_AT[hf])
                    nc.gpsimd.tensor_tensor(moved[c, hf][:], gains[c][:, lo:hi], wgs_sb[:, lo:hi], ALU.mult)
            elif c in moved:
                for hf in (1, 0) if c in SQUARE_ON_GPSIMD else (0, 1):
                    nc.gpsimd.tensor_tensor(moved[c][:, half_of(hf)], squares[hf], wgs_sb[:, half_of(hf)], ALU.mult)

        def apply_gains(c, lo, hi, sums, values):
            if c in VECTOR_PAGES:
                factor = moved[c, lo // BANK][:] if c else gains[c][:, lo:hi]
                nc.vector.tensor_tensor(values, sums, factor, ALU.mult)
            else:
                nc.scalar.copy(out=values, in_=sums)

        def scatter(c, lo, hi, values):
            window = pages[c % PAGE_TILES][:].indirect(entries(idx2, lo, hi))
            if c < LAST and (c, lo) != (0, 0):
                nc.vector.tensor_copy(window, values)
            else:
                nc.vector.tensor_tensor(window, values, wgs_sb[:, lo:hi], ALU.mult)

        halves = [(0, BANK), (BANK, S)]

        z_turned = [keep.tile([P, BLOCKS, 2, P, 2], BF16, name=f"z_turned{g}") for g in range(GROUPS)]
        z_grouped = [keep.tile([P, PASSES, BANK, 2], F32, name=f"z_grouped{g}", align_bytes=64) for g in range(GROUPS)]

        def turn_into_sum(bank, g, rows, opens):
            for k in range(BLOCKS):
                tick = g * BANK + k * P
                nc.tensor.matmul(
                    bank[:, k * P : (k + 1) * P], lhsT=rows[:, tick : tick + P], rhs=ident[:], is_transpose=True,
                    start=(opens and k == 0), stop=(not opens and k == BLOCKS - 1),
                )

        def open_sums(c, sums, groups):
            for g in groups:
                turn_into_sum(sums[g], g, hist_sb[c], True)

        def close_sums(c, sums, groups):
            quarter = c % PAGES_PER_PASS
            for g in groups:
                turn_into_sum(sums[g], g, pages[c % PAGE_TILES], False)
                nc.scalar.copy(
                    out=z_turned[g][:, :, :, QUAD * quarter : QUAD * (quarter + 1), :],
                    in_=sums[g][:].rearrange("p (k i u e) -> p k u i e", k=BLOCKS, u=2, e=2),
                )

        def turn_words(g, pair):
            words = z_turned[g][:].rearrange("p k u r e -> p (k u r e)").bitcast(F32)
            for j in range(2):
                for u in range(2):
                    for kk in range(2):
                        source = ((2 * j + kk) * 2 + u) * P
                        target = (u * 2 + kk) * P
                        nc.tensor.transpose(pair[j][:, target : target + P], words[:, source : source + P], ident[:])

        def lay_words(a, g, pair):
            for j in range(2):
                nc.scalar.copy(
                    out=z_grouped[g][:, a, j * BANK // 2 : (j + 1) * BANK // 2, :],
                    in_=pair[j][:].rearrange("p (u n) -> p n u", u=2),
                )

        def turn_first_pass(groups):
            for g in groups:
                pair = banks[TURN_PAIRS[g] : TURN_PAIRS[g] + 2]
                turn_words(g, pair)
                lay_words(0, g, pair)

        def quantize(words, scales, grouped):
            nc.vector.quantize_mx(
                out=words.bitcast(FP8X4), scales=scales, in_=grouped.bitcast(BF16)
            )

        w3_w = keep.tile([P, PASSES, N], I32, name="w3_w", align_bytes=64)
        w3_apart = keep.tile([P, BLOCKS + 1, P], I32, name="w3_apart", align_bytes=64)
        w3_last, w3_early = w3_apart[:, :BLOCKS], w3_apart[:, BLOCKS]
        w3_last_sc = keep.tile([P, P], U8, name="w3_last_sc", align_bytes=64)
        nc.gpsimd.memset(w3_apart[:], 0)
        nc.gpsimd.memset(w3_last_sc[:].bitcast(I32), 0)
        wgo_sb = keep.tile([P, M], F32, name="wgo_sb")
        lam_sb = keep.tile([P, N // P], F32, name="lam_sb")
        snap_sb = []
        late_lists = []

        def preload_second_stage():
            nc.sync.dma_start(out=w3_w[:], in_=w3_words.rearrange("a p c t -> p a (c t)").bitcast(I32))
            load_scale_rows(w3_sc, w3_scales.rearrange("a q n -> q a n"))
            second = w3_words[1].rearrange("p c t -> p (c t)").bitcast(I32)
            for k in range(BLOCKS):
                nc.sync.dma_start(out=w3_last[QUAD * k : QUAD * (k + 1), k, :], in_=second[EARLY:, :P])
            for k in range(BLOCKS):
                nc.sync.dma_start(out=w3_last_sc[QUAD * k : QUAD * k + 4].bitcast(I32), in_=w3_scales[1, 12:16, :P].bitcast(I32))
            nc.sync.dma_start(out=w3_early[:EARLY], in_=second[:EARLY, :P])
            nc.sync.dma_start(out=wgo_sb[:], in_=wgo)
            late_lists.extend([load_list("idx3", offs3), load_list("idx4", offs4)])
            with nc.allow_non_contiguous_dma(reason="one value of lam for each partition and row tile"):
                nc.sync.dma_start(out=lam_sb[:], in_=lam.rearrange("(i p) -> p i", p=P))
            for i in range(N // P):
                rows = shared.tile([P, M], F32, name=f"snap_sb{i}", offset=RAW_AT + 4 * M * i)
                nc.sync.dma_start(out=rows[:], in_=snap[i * P : (i + 1) * P, :])
                snap_sb.append(rows)

        (b_lo, b_hi), (a_lo, a_hi), (c_lo, c_hi) = FIRST_RUNS
        round_w1(0)
        quantize_w1(0)
        round_w1(1)
        round_w1(2)
        make_gains(0, FIRST_RUNS[:2], banks[0:2])
        first_gains = gains[0]
        motion(0, a_lo, a_hi, banks[2])
        motion(0, b_lo, b_hi, banks[3])
        values = ring4.tile([P, BANK], F32, name="values", tag="listed")
        nc.vector.tensor_tensor(first_gains[:, b_lo:b_hi], first_gains[:, b_lo:b_hi], wgs_sb[:, b_lo:b_hi], ALU.mult)
        nc.vector.tensor_tensor(values[:, a_lo:a_hi], banks[2][:, :QUARTER], first_gains[:, a_lo:a_hi], ALU.mult)
        nc.vector.tensor_tensor(values[:, b_lo:b_hi], banks[3][:, :QUARTER], first_gains[:, b_lo:b_hi], ALU.mult)
        scatter(0, a_lo, a_hi, values[:, a_lo:a_hi])
        quantize_w1(1)
        scatter(0, b_lo, b_hi, values[:, b_lo:b_hi])
        gains[0] = shared.tile([P, S], F32, name="third_gains", offset=FIRST_ROOTS_AT - 2 * KIB)
        make_gains(0, FIRST_RUNS[2:], banks[4:5])
        motion(0, c_lo, c_hi, banks[5])
        factor = shared.tile([P, BANK], F32, name="third_factor", offset=THIRD_FACTOR_AT)
        nc.gpsimd.tensor_tensor(factor[:], gains[0][:, c_lo:c_hi], wgs_sb[:, c_lo:c_hi], ALU.mult)
        values = ring4.tile([P, BANK], F32, name="values", tag="listed")
        nc.vector.tensor_tensor(values[:], banks[5][:], factor[:], ALU.mult)
        quantize_w1(2)
        scatter(0, c_lo, c_hi, values[:])

        def make_values(c, a_banks):
            if c < LAST:
                if c == 1:
                    values = shared.tile([P, S], F32, name="values_behind_w1", offset=RAW_AT + 4 * PACK * W1_LOADS[2][0])
                else:
                    values = ring4.tile([P, S], F32, name="values", tag="listed")
                pieces = [(0, S, values)]
            else:
                pieces = [(0, S, shared.tile([P, S], F32, name="last_values", offset=LAST_VALUES_AT))]
            for hf, (first, stop) in enumerate(halves):
                motion(c, first, stop, a_banks[hf])
                for lo, hi, values in pieces:
                    a, b = max(lo, first), min(hi, stop)
                    if a < b:
                        apply_gains(c, a, b, a_banks[hf][:, a - first : b - first], values[:, a - lo : b - lo])
            if c not in VECTOR_PAGES:
                values = pieces[0][2]
                for lo, hi in G_RUNS[:: -1 if c in SQUARE_ON_GPSIMD else 1]:
                    nc.gpsimd.tensor_tensor(values[:, lo:hi], values[:, lo:hi], moved.get(c, gains[c])[:, lo:hi], ALU.mult)
            return pieces

        def page_gains(c):
            make_gains(c, halves, (banks[2], banks[4]) if c == 1 else spread_banks)

        def history_sums(c, groups):
            sums = product_banks if c == LAST - 2 else sum_banks
            open_sums(c, sums, groups)
            close_sums(c, sums, groups)

        for c, a_banks in ((1, banks[6:8]), (2, motion_banks)):
            page_gains(c)
            if c == 1:
                round_w1(3)
            values = make_values(c, a_banks)[0][2]
            if c == 1:
                quantize_w1(3)
            scatter(c, 0, S, values[:])
        preload_second_stage()

        for c in range(LAST):
            ahead = c + AHEAD
            if ahead == LAST:
                turn_first_pass(range(TURNS_BEFORE))
            if ahead < PAGES:
                page_gains(ahead)
            split = GROUPS // 2 if ahead < LAST else 0
            history_sums(c, range(split))
            if ahead < PAGES:
                pieces = make_values(ahead, motion_banks)
            if ahead == LAST:
                turn_first_pass(range(TURNS_BEFORE, GROUPS))
            history_sums(c, range(split, GROUPS))
            if c + PAGES_PER_PASS < PAGES:
                load_hist(c + PAGES_PER_PASS)
            if ahead < LAST:
                lo, hi, values = pieces[0]
                scatter(ahead, lo, hi, values[:])

        slots = [shared.tile([P, T2], F32, name=f"slots{i}", offset=at) for i, at in enumerate(SLOTS_AT)]
        for tile in slots:
            nc.gpsimd.memset(tile[:], 0.0)

        pairs = [banks[2 * g : 2 * g + 2] for g in range(GROUPS)]
        for g in range(GROUPS):
            turn_words(g, pairs[g])
        for g in range(GROUPS):
            lay_words(1, g, pairs[g])
        open_sums(LAST, product_banks, range(GROUPS))
        scatter(LAST, 0, S, pieces[0][2][:])

        for g in range(GROUPS):
            turn_into_sum(product_banks[g], g, pages[LAST % PAGE_TILES], False)
        last_turned = [keep.tile([P, 2, P, 2], BF16, name=f"last_turned{g}") for g in range(GROUPS)]
        for g in range(GROUPS):
            nc.scalar.copy(out=last_turned[g][:], in_=product_banks[g][:].rearrange("p (r u e) -> p u r e", u=2, e=2))

        z_w = shared.tile([P, GROUPS, PASSES, BANK], U32, name="z_w", align_bytes=64, offset=TABLE_AT)
        z_sc = keep.tile([P, GROUPS, PASSES, BANK], U8, name="z_sc", align_bytes=64)
        last_w = keep.tile([P, BANK], U32, name="last_w", align_bytes=64)
        last_sc = keep.tile([P, BANK], U8, name="last_sc", align_bytes=64)

        def ticks_of(g):
            return slice(g * BANK, (g + 1) * BANK)

        def block_of(k):
            return slice(k * P, (k + 1) * P)

        for g in range(GROUPS):
            quantize(
                z_w[:, g].rearrange("p a n -> p (a n)"), z_sc[:, g].rearrange("p a n -> p (a n)"),
                z_grouped[g][:].rearrange("p a n u -> p (a n u)"),
            )

        y_sb = [ring4.tile([P, T2], F32, name="y_sb", tag="rows") for i in range(N // P)]

        def product(out_columns, weights, weight_scales, words, scales, start, stop):
            nc.tensor.matmul_mx(
                out=out_columns, lhsT=weights.bitcast(FP8X4), lhsT_scale=weight_scales,
                rhs=words.bitcast(FP8X4), rhs_scale=scales, start=start, stop=stop,
            )

        def leave_bank(i, g, bank):
            if i == 0 and g in Y_ON_VECTOR:
                nc.vector.tensor_scalar(y_sb[i][:, ticks_of(g)], bank[:], lam_sb[:, i : i + 1], None, ALU.mult)
            else:
                nc.scalar.activation(y_sb[i][:, ticks_of(g)], bank[:], ACT.Copy, scale=lam_sb[:, i : i + 1])

        def early_passes(g):
            bank = banks[FIRST_Y_BANKS[g]]
            product(bank[:], w3_w[:, 0, :P], w3_sc[:, 0, :P], z_w[:, g, 0], z_sc[:, g, 0], True, False)
            product(bank[:], w3_early, w3_sc[:, 1, :P], z_w[:, g, 1], z_sc[:, g, 1], False, False)

        def turn_last(g):
            words = last_turned[g][:].rearrange("p u r e -> p (u r e)").bitcast(F32)
            for u in range(2):
                nc.tensor.transpose(banks[LAST_TURN_BANKS[g]][:, block_of(u)], words[:, block_of(u)], ident[:])

        for g in range(2):
            early_passes(g)
            turn_last(2 * g)
            turn_last(2 * g + 1)
        for g in range(2, GROUPS):
            early_passes(g)
        for g in range(GROUPS):
            grouped = keep.tile([P, P, 2], F32, name=f"last_grouped{g}", align_bytes=64)
            nc.scalar.copy(out=grouped[:], in_=banks[LAST_TURN_BANKS[g]][:, : 2 * P].rearrange("p (u n) -> p n u", u=2))
            quantize(last_w[:, block_of(g)], last_sc[:, block_of(g)], grouped[:].rearrange("p n u -> p (n u)"))
        for g in range(GROUPS):
            bank = banks[FIRST_Y_BANKS[g]]
            for k in range(BLOCKS):
                product(
                    bank[:, block_of(k)], w3_last[:, k, :], w3_last_sc[:],
                    last_w[:, block_of(g)], last_sc[:, block_of(g)], False, k == BLOCKS - 1,
                )
            leave_bank(0, g, bank)

        for k in range(BLOCKS):
            nc.sync.dma_start(
                out=z_w[EARLY:, :, 1, block_of(k)].bitcast(I32),
                in_=last_w[QUAD * k : QUAD * (k + 1)].bitcast(I32).rearrange("p (g n) -> p g n", g=GROUPS),
            )
            nc.sync.dma_start(
                out=z_sc[EARLY : EARLY + 4, :, 1, block_of(k)].bitcast(I32),
                in_=last_sc[QUAD * k : QUAD * k + 4].bitcast(I32).rearrange("p (g n) -> p g n", g=GROUPS),
            )
        for tiles in ((1, 2), (3,)):
            later = [(i, g, banks[(FIRST_Y_BANKS, LATER_Y_BANKS)[i % 2][g]]) for i in tiles for g in range(GROUPS)]
            for i, g, bank in later:
                product(bank[:], w3_w[:, 0, block_of(i)], w3_sc[:, 0, block_of(i)], z_w[:, g, 0], z_sc[:, g, 0], True, False)
            for i, g, bank in later:
                product(bank[:], w3_w[:, 1, block_of(i)], w3_sc[:, 1, block_of(i)], z_w[:, g, 1], z_sc[:, g, 1], False, True)
                leave_bank(i, g, bank)

        idx3, idx4 = late_lists
        picked = []

        def pick(i):
            if i in PICKS_AT:
                x = shared.tile([P, M], F32, name=f"x_behind_z{i}", offset=PICKS_AT[i])
            else:
                x = ring4.tile([P, M], F32, name="x", tag="listed")
            nc.vector.tensor_tensor(x[:], y_sb[i][:].indirect(idx3[:]), snap_sb[i][:], ALU.add)
            picked.append(x)

        pick(0)
        for i in range(N // P):
            if 0 < i < N // P - 1:
                pick(i + 1)
            nc.vector.tensor_tensor(slots[i % 2][:].indirect(idx4[:]), picked[i][:], wgo_sb[:], ALU.mult)
            for hf in range(2):
                cols = slice(hf * T2 // 2, (hf + 1) * T2 // 2)
                queue = nc.scalar if hf and i == N // P - 1 else nc.sync
                queue.dma_start(out=out[i * P : (i + 1) * P, cols], in_=slots[i % 2][:, cols])
            if i == 0:
                pick(1)
